import numpy as np
import ml_dtypes


def mxq(x, axis, fmt="e4m3"):
    dtype, down = {"e4m3": (ml_dtypes.float8_e4m3fn, 7), "e5m2": (ml_dtypes.float8_e5m2, 14)}[fmt]
    v = np.moveaxis(np.asarray(x, np.float32).astype(ml_dtypes.bfloat16).astype(np.float64), axis, -1)
    blocks = v.reshape(v.shape[:-1] + (-1, 32))
    amax = np.abs(blocks).max(-1, keepdims=True)
    byte = np.maximum(np.where(amax > 0, np.frexp(amax)[1] - 1 + 127, 0) - down, 1)
    scale = np.exp2(byte - 127.0)
    codes = (blocks / scale).astype(np.float32).astype(dtype).astype(np.float64)
    return np.moveaxis((codes * scale).reshape(v.shape), -1, axis)


WIDE = False


def mx_kscale(k):
    if not WIDE:
        return np.ones(k)
    levels = np.array([10, -10, 5, -5, 0])
    if k % 512:
        return np.exp2(np.random.permutation(np.resize(levels, k // 32))).repeat(32)
    a = np.empty((k // 512, 16))
    for p in range(k // 512):
        a[p, :8] = np.random.permutation(np.resize(levels, 8))
        for g in range(8):
            far = levels[np.abs(levels - a[p, g]) >= 10]
            a[p, g + 8] = far[np.random.randint(len(far))]
    return np.exp2(a.ravel()).repeat(32)


def f64(x):
    return np.asarray(x).astype(np.float64)


def striped(idx):
    return np.tile(idx.reshape(-1, 16).T, (8, 1)).astype(np.uint16)


def unstriped(offs):
    return offs[:16].T.reshape(-1).astype(np.int64)


E2M1 = np.array([0.0, 0.5, 1.0, 1.5, 2.0, 3.0, 4.0, 6.0, -0.0, -0.5, -1.0, -1.5, -2.0, -3.0, -4.0, -6.0])


def pack_weight(w, fmt):
    k, n = w.shape
    w = f64(np.asarray(w, np.float32).astype(ml_dtypes.bfloat16)).reshape(k // 32, 32, n)
    amax = np.abs(w).max(1)
    if fmt == "e4m3":
        byte = np.frexp(amax)[1] - 1 + 127 - 7
    else:
        mant, ex = np.frexp(amax / 6.0)
        byte = np.where(mant > 0.5, ex, ex - 1) + 127
    byte = np.clip(np.where(amax > 0, byte, 1), 1, 254)
    scaled = (w * np.exp2(127.0 - byte)[:, None, :]).reshape(k, n).astype(np.float32)
    by_word = np.ascontiguousarray(scaled.reshape(k // 512, 128, 4, n).transpose(0, 1, 3, 2))
    if fmt == "e4m3":
        words = by_word.astype(ml_dtypes.float8_e4m3fn).view(np.uint8)
    else:
        c = by_word.astype(ml_dtypes.float4_e2m1fn).view(np.uint8) & 0xF
        words = (c[..., 0::2] | (c[..., 1::2] << 4)).reshape(k // 512, 128, 2 * n)
    return np.ascontiguousarray(words), np.ascontiguousarray(byte.astype(np.uint8).reshape(k // 512, 16, n))


def unpack_weight(words, scales, fmt):
    g, _, n = scales.shape
    words = np.ascontiguousarray(words).reshape(g, 128, n, -1)
    if fmt == "e4m3":
        vals = words.view(ml_dtypes.float8_e4m3fn).astype(np.float64)
    else:
        nib = np.empty((g, 128, n, 4), np.uint8)
        nib[..., 0::2] = words & 0xF
        nib[..., 1::2] = words >> 4
        vals = E2M1[nib]
    vals = vals * np.repeat(np.exp2(scales.astype(np.float64) - 127.0), 8, axis=1)[..., None]
    return vals.transpose(0, 1, 3, 2).reshape(g * 512, n)


def relu(v):
    return np.maximum(v, 0.0)


def d_relu(v):
    return (v > 0).astype(np.float64)


K, T, E1, C1, E2, C2, H = 512, 512, 2, 256, 2, 256, 512
N = 512


def by_expert(wq, xq, E, C):
    return np.concatenate([wq[e].T @ xq[:, e * C:(e + 1) * C] for e in range(E)], axis=1)


def setup_inputs():
    n = np.random.standard_normal
    v = mx_kscale(N)
    u = mx_kscale(H)
    slots1, slots2 = np.random.permutation(T), np.random.permutation(T)
    dy = pack_weight(n((N, T)) * v[:, None], "e4m3")
    w2t = pack_weight(n((N, H)) / np.sqrt(N) / v[:, None] * u, "e2m1")
    wat = [pack_weight(m, "e2m1") for m in n((E1, H, K)) / np.sqrt(H) / u[None, :, None]]
    return {
        "dy_words": dy[0],
        "dy_scales": dy[1],
        "w2t_words": w2t[0],
        "w2t_scales": w2t[1],
        "wat_words": np.stack([m[0] for m in wat]),
        "wat_scales": np.stack([m[1] for m in wat]),
        "wbt": (n((E2, H, K)) / np.sqrt(H) / u[None, :, None]).astype(np.float32),
        "a": (n((H, T))).astype(np.float32),
        "c": (n((H, T))).astype(np.float32),
        "offs": striped(slots1),
        "offs2": striped(slots2),
    }


def reference(dy_words, dy_scales, w2t_words, w2t_scales, wat_words, wat_scales, wbt, a, c, offs, offs2):
    w2t = unpack_weight(w2t_words, w2t_scales, "e2m1")
    wat = np.stack([unpack_weight(wat_words[e], wat_scales[e], "e2m1") for e in range(E1)])
    wbtq = mxq(f64(wbt), 1, "e4m3")
    idx, idx2 = unstriped(offs), unstriped(offs2)
    dh = w2t.T @ unpack_weight(dy_words, dy_scales, "e4m3")
    da = dh * f64(c) * d_relu(f64(a))
    dc = dh * relu(f64(a))
    out = np.zeros((K, T))
    out[:, idx] = by_expert(wat, mxq(da[:, idx], 0, "e4m3"), E1, C1)
    out[:, idx2] += by_expert(wbtq, mxq(dc[:, idx2], 0, "e4m3"), E2, C2)
    return out

@@ -1,0 +1,260 @@
+from contextlib import ExitStack
+
+import concourse.mybir as mybir
+from concourse.masks import make_identity
+
+K, T, H, N = 512, 512, 512, 512
+E, C = 2, 256
+FLOPS = 2 * N * H * T + 2 * 2 * H * K * T
+
+F32 = mybir.dt.float32
+BF16 = mybir.dt.bfloat16
+I32 = mybir.dt.int32
+U32 = mybir.dt.uint32
+U16 = mybir.dt.uint16
+U8 = mybir.dt.uint8
+FP8X4 = mybir.dt.float8_e4m3fn_x4
+FP4X4 = mybir.dt.float4_e2m1fn_x4
+ALU = mybir.AluOpType
+COPY = mybir.ActivationFunctionType.Copy
+
+P = 128
+PACK = 4
+KB = K // P
+HALF = K // 2
+LIST_COLS = C // 16
+WIDE = 704
+
+
+def tile_moe_plb_relu_kernel(
+    tc, dy_words, dy_scales, w2t_words, w2t_scales, wat_words, wat_scales, wbt, a, c, offs, offs2, out
+):
+    nc = tc.nc
+    with ExitStack() as ctx:
+        sb = ctx.enter_context(tc.tile_pool(name="sb", bufs=1))
+        ps = ctx.enter_context(tc.psum_pool(name="ps", bufs=1))
+
+        def tile(shape, dtype, name, tag=None):
+            return sb.tile(shape, dtype, name=name, tag=tag or name, align_bytes=64)
+
+        list_a = sb.tile([P, T // 16], U16, name="list_a")
+        list_c = sb.tile([P, T // 16], U16, name="list_c")
+
+        w2_plane_raw = tile([P, H], U8, "w2_plane_raw")
+        dy_plane = tile([P, T], U8, "dy_plane")
+        wa_plane = tile([P, E, K], U8, "wa_plane")
+        nc.vector.memset(w2_plane_raw[:].bitcast(I32), 0)
+        nc.gpsimd.memset(dy_plane[:].bitcast(I32), 0)
+        nc.vector.memset(wa_plane[:].bitcast(I32), 0)
+
+        warm_in = tile([P, 2], BF16, "warm_in")
+        warm_out = tile([P, 2], BF16, "warm_out")
+        nc.gpsimd.memset(warm_in[:], 0.0)
+        nc.scalar.activation(warm_out[:], warm_in[:], COPY)
+
+        identity = tile([P, P], F32, "identity")
+        make_identity(nc, identity[:])
+
+        def load_scale_rows(plane, rows):
+            by_row = rows.bitcast(I32).rearrange("(q r) n -> r q n", r=4)
+            for r in range(4):
+                nc.sync.dma_start(out=plane[r:P:32, :].bitcast(I32), in_=by_row[r])
+
+        a_planes = a.rearrange("(p t) n -> p t n", t=PACK)
+        c_planes = c.rearrange("(p t) n -> p t n", t=PACK)
+        a_sb = [tile([P, T], F32, f"a{t}") for t in range(PACK)]
+        c_sb = [tile([P, T], F32, f"c{t}") for t in range(PACK)]
+
+        w2_raw = tile([P, 2 * H], U8, "w2_raw")
+        dy_codes = tile([P, T], U32, "dy_codes")
+        wa_codes = tile([P, E, 2 * K], U8, "wa_codes")
+        wb_raw = [[tile([P, PACK, HALF], F32, f"wb_raw{e}{h}") for h in range(2)] for e in range(E)]
+
+        nc.sync.dma_start(out=w2_raw[:].bitcast(I32), in_=w2t_words[0].bitcast(I32))
+        load_scale_rows(w2_plane_raw, w2t_scales[0])
+        nc.sync.dma_start(out=dy_codes[:].bitcast(I32), in_=dy_words[0].rearrange("p t d -> p (t d)").bitcast(I32))
+        for t in range(PACK):
+            nc.sync.dma_start(out=a_sb[t][:], in_=a_planes[:, t, :])
+            nc.sync.dma_start(out=c_sb[t][:], in_=c_planes[:, t, :])
+            if t == 0:
+                load_scale_rows(dy_plane, dy_scales[0])
+                nc.sync.dma_start(list_a[:], offs)
+        nc.sync.dma_start(out=wa_codes[:].bitcast(I32), in_=wat_words.rearrange("e s p b -> p (e s) b").bitcast(I32))
+        wa_rows = wat_scales.bitcast(I32).rearrange("e s (q r) n -> r q (e s) n", r=4)
+        for r in range(4):
+            nc.sync.dma_start(out=wa_plane[r:P:32, :, :].bitcast(I32), in_=wa_rows[r])
+        nc.sync.dma_start(list_c[:], offs2)
+        for e in range(E):
+            rows = wbt[e].rearrange("(p j) k -> p j k", j=PACK)
+            for h in range(2):
+                nc.sync.dma_start(out=wb_raw[e][h][:], in_=rows[:, :, h * HALF : (h + 1) * HALF])
+
+        w2_codes = tile([P, 2 * H], U8, "w2_codes")
+        w2_plane = tile([P, H], U8, "w2_plane")
+        nc.vector.tensor_copy(
+            out=w2_codes[:].bitcast(U16).rearrange("p (t m) -> p t m", t=PACK),
+            in_=w2_raw[:].bitcast(U16).rearrange("p (m t) -> p t m", t=PACK),
+        )
+        nc.vector.tensor_copy(
+            out=w2_plane[:].rearrange("p (t m) -> p t m", t=PACK),
+            in_=w2_plane_raw[:].rearrange("p (m t) -> p t m", t=PACK),
+        )
+
+        dh = [ps.tile([P, T], F32, name=f"dh{t}", tag=f"low{t}") for t in range(PACK)]
+        for t in range(PACK):
+            nc.tensor.matmul_mx(
+                out=dh[t][:],
+                lhsT=w2_codes[:, 2 * P * t : 2 * P * (t + 1)].bitcast(FP4X4),
+                lhsT_scale=w2_plane[:, P * t : P * (t + 1)],
+                rhs=dy_codes[:].bitcast(FP8X4),
+                rhs_scale=dy_plane[:],
+                start=True,
+                stop=True,
+            )
+
+        da = [tile([P, T], BF16, f"da{t}")[:] for t in range(PACK)]
+        gated_c = [tile([P, T], F32, f"gated_c{t}") for t in range(PACK)]
+        for t in range(PACK + 1):
+            if t < PACK:
+                nc.vector.scalar_tensor_tensor(gated_c[t][:], a_sb[t][:], 0.0, c_sb[t][:], ALU.is_gt, ALU.mult)
+            if t > 0:
+                nc.vector.tensor_tensor(da[t - 1], dh[t - 1][:], gated_c[t - 1][:], ALU.mult)
+
+        def gather(planes, offsets, e, name, tag):
+            words = tile([P, C, PACK], BF16, name, tag)
+            cut = offsets[:, e * LIST_COLS : (e + 1) * LIST_COLS]
+            for t in range(PACK):
+                nc.scalar.activation(words[:, :, t], planes[t].indirect(cut), COPY)
+            return words
+
+        def quantise(words, name):
+            width = words.shape[1]
+            codes = tile([P, width], U32, name + "_codes")
+            plane = tile([P, width], U8, name + "_plane")
+            nc.vector.quantize_mx(codes[:].bitcast(FP8X4), plane[:], words[:].rearrange("p w j -> p (w j)"))
+            return codes, plane
+
+        def round_wb(e, h, tag):
+            words = tile([P, HALF, PACK], BF16, f"wb_words{e}{h}", tag)
+            nc.scalar.copy(
+                words[:].rearrange("p (g i) j -> p g j i", i=4),
+                wb_raw[e][h][:].rearrange("p j (g i) -> p g j i", i=4),
+            )
+            return words
+
+        r_bank = [ps.tile([P, T], F32, name=f"r_bank{kb}", tag=f"high{kb}") for kb in range(KB)]
+        r_tok = [tile([P, T], F32, f"r_tok{kb}") for kb in range(KB - 1)]
+        q_tok = [tile([P, T], F32, f"q_tok{kb}") for kb in range(KB - 1)]
+
+        def r_products(e, act):
+            codes, plane = act
+            for kb in range(KB):
+                nc.tensor.matmul_mx(
+                    out=r_bank[kb][:, e * C : (e + 1) * C],
+                    lhsT=wa_codes[:, e, 2 * P * kb : 2 * P * (kb + 1)].bitcast(FP4X4),
+                    lhsT_scale=wa_plane[:, e, P * kb : P * (kb + 1)],
+                    rhs=codes[:].bitcast(FP8X4),
+                    rhs_scale=plane[:],
+                    start=True,
+                    stop=True,
+                )
+
+        def q_products(e, h, act, weights):
+            codes, plane = act
+            w_codes, w_plane = weights
+            for kb in range(2 * h, 2 * h + 2):
+                cols = slice(P * (kb % 2), P * (kb % 2 + 1))
+                nc.tensor.matmul_mx(
+                    out=q_bank[kb][:, e * C : (e + 1) * C],
+                    lhsT=w_codes[:, cols].bitcast(FP8X4),
+                    lhsT_scale=w_plane[:, cols],
+                    rhs=codes[:].bitcast(FP8X4),
+                    rhs_scale=plane[:],
+                    start=True,
+                    stop=True,
+                )
+
+        def to_tokens(bank, window, offsets, e, name, tag):
+            slots = tile([P, C], F32, name, tag)
+            nc.scalar.copy(slots[:], bank[:, e * C : (e + 1) * C])
+            cut = offsets[:, e * LIST_COLS : (e + 1) * LIST_COLS]
+            nc.vector.tensor_copy(window[:].indirect(cut), slots[:])
+
+        def r_back(e, kb, tag=None):
+            to_tokens(r_bank[kb], r_tok[kb], list_a, e, f"r_slots{e}{kb}", tag)
+
+        def q_back(e, kb, tag=None):
+            to_tokens(q_bank[kb], q_tok[kb], list_c, e, f"q_slots{e}{kb}", tag)
+
+        def dc_plane(t, plane):
+            nc.vector.scalar_tensor_tensor(plane, a_sb[t][:], 0.0, dh[t][:], ALU.max, ALU.mult)
+            return plane
+
+        def turn(bank, source, start, stop):
+            for tb in range(T // P):
+                cols = slice(tb * P, (tb + 1) * P)
+                nc.tensor.matmul(
+                    bank[:, cols], source[:, cols], identity[:], is_transpose=True,
+                    start=start and tb == 0, stop=stop and tb == T // P - 1,
+                )
+
+        da_words0 = gather(da, list_a, 0, "da_words0", None)
+        dc = [dc_plane(t, tile([P, T], BF16, f"dc{t}", f"gated_c{t + 2}")[:]) for t in range(2)]
+        da_q0 = quantise(da_words0, "da_q0")
+        dc_late = tile([P, 2, T], BF16, "dc_late", "da_words0")
+        dc = dc + [dc_plane(t + 2, dc_late[:, t, :]) for t in range(2)]
+        q_bank = [ps.tile([P, T], F32, name=f"q_bank{kb}", tag=f"low{kb}") for kb in range(KB)]
+        r_products(0, da_q0)
+        r_back(0, 0)
+        r_back(0, 1)
+        da_q1 = quantise(gather(da, list_a, 1, "da_words1", "da_q0_codes"), "da_q1")
+        r_back(0, 2, "da3")
+        r_products(1, da_q1)
+
+        wb_q00 = quantise(round_wb(0, 0, "da0"), "wb_q00")
+        for kb in range(KB - 1):
+            r_back(1, kb)
+        r_slots3 = tile([P, T], F32, "r_slots3")
+        nc.scalar.copy(r_slots3[:], r_bank[3][:])
+        dc_q0 = quantise(gather(dc, list_c, 0, "dc_words0", "wb_raw00"), "dc_q0")
+        r_tok3 = tile([P, WIDE], F32, "r_tok3", "wb_raw00")
+        nc.vector.tensor_copy(r_tok3[:].indirect(list_a[:]), r_slots3[:])
+        q_products(0, 0, dc_q0, wb_q00)
+
+        sums = [ps.tile([P, T], F32, name=f"sums{kb}", tag=f"high{kb}") for kb in range(KB - 1)]
+        for kb in range(KB - 1):
+            turn(sums[kb], r_tok[kb], True, False)
+
+        wb_q01 = quantise(round_wb(0, 1, "wb_q00_codes"), "wb_q01")
+        q_products(0, 1, dc_q0, wb_q01)
+        q_back(0, 0)
+        q_back(0, 1, "wb_raw01")
+        wb_q10 = quantise(round_wb(1, 0, "wb_q00_plane"), "wb_q10")
+        dc_q1 = quantise(gather(dc, list_c, 1, "dc_words1", "wb_raw10"), "dc_q1")
+        q_back(0, 2, "gated_c2")
+        q_products(1, 0, dc_q1, wb_q10)
+        wb_q11 = quantise(round_wb(1, 1, "gated_c3"), "wb_q11")
+        q_products(1, 1, dc_q1, wb_q11)
+
+        for kb in range(KB - 1):
+            q_back(1, kb, "wb_raw11" if kb == 1 else None)
+        q_slots3 = tile([P, T], F32, "q_slots3")
+        nc.scalar.copy(q_slots3[:], q_bank[3][:])
+        q_tok3 = tile([P, WIDE], F32, "q_tok3")
+        nc.vector.tensor_copy(q_tok3[:].indirect(list_c[:]), q_slots3[:])
+
+        for kb in range(KB - 1):
+            turn(sums[kb], q_tok[kb], False, True)
+            turned = tile([P, T], F32, f"turned{kb}")
+            nc.scalar.copy(turned[:], sums[kb][:])
+            back = ps.tile([P, T], F32, name=f"back{kb}", tag=f"low{kb}")
+            turn(back, turned, True, True)
+            total = tile([P, T], F32, f"total{kb}")
+            nc.scalar.copy(total[:], back[:])
+            nc.sync.dma_start(out=out[kb * P : (kb + 1) * P, :], in_=total[:])
+
+        for h in range(2):
+            cols = slice(h * HALF, (h + 1) * HALF)
+            last = tile([P, HALF], F32, f"last{h}")
+            nc.vector.tensor_tensor(last[:], r_tok3[:, cols], q_tok3[:, cols], ALU.add)
+            nc.sync.dma_start(out=out[3 * P : 4 * P, cols], in_=last[:])

@@ -120,8 +120,7 @@ def tile_moe_plb_relu_kernel(
             if t > 0:
                 nc.vector.tensor_tensor(da[t - 1], dh[t - 1][:], gated_c[t - 1][:], ALU.mult)
 
-        def gather(planes, offsets, e, name, tag):
-            words = tile([P, C, PACK], BF16, name, tag)
+        def gather(planes, offsets, e, words):
             cut = offsets[:, e * LIST_COLS : (e + 1) * LIST_COLS]
             for t in range(PACK):
                 nc.scalar.activation(words[:, :, t], planes[t].indirect(cut), COPY)
@@ -131,7 +130,7 @@ def tile_moe_plb_relu_kernel(
             width = words.shape[1]
             codes = tile([P, width], U32, name + "_codes")
             plane = tile([P, width], U8, name + "_plane")
-            nc.vector.quantize_mx(codes[:].bitcast(FP8X4), plane[:], words[:].rearrange("p w j -> p (w j)"))
+            nc.vector.quantize_mx(codes[:].bitcast(FP8X4), plane[:], words.rearrange("p w j -> p (w j)"))
             return codes, plane
 
         def round_wb(e, h, tag):
@@ -140,7 +139,7 @@ def tile_moe_plb_relu_kernel(
                 words[:].rearrange("p (g i) j -> p g j i", i=4),
                 wb_raw[e][h][:].rearrange("p j (g i) -> p g j i", i=4),
             )
-            return words
+            return words[:]
 
         r_bank = [ps.tile([P, T], F32, name=f"r_bank{kb}", tag=f"high{kb}") for kb in range(KB)]
         r_tok = [tile([P, T], F32, f"r_tok{kb}") for kb in range(KB - 1)]
@@ -198,16 +197,23 @@ def tile_moe_plb_relu_kernel(
                     start=start and tb == 0, stop=stop and tb == T // P - 1,
                 )
 
-        da_words0 = gather(da, list_a, 0, "da_words0", None)
+        def words_tile(name, tag):
+            return tile([P, C, PACK], BF16, name, tag)[:]
+
+        da_words0 = gather(da, list_a, 0, words_tile("da_words0", None))
         dc = [dc_plane(t, tile([P, T], BF16, f"dc{t}", f"gated_c{t + 2}")[:]) for t in range(2)]
         da_q0 = quantise(da_words0, "da_q0")
-        dc_late = tile([P, 2, T], BF16, "dc_late", "da_words0")
-        dc = dc + [dc_plane(t + 2, dc_late[:, t, :]) for t in range(2)]
-        q_bank = [ps.tile([P, T], F32, name=f"q_bank{kb}", tag=f"low{kb}") for kb in range(KB)]
+        late = tile([P, C * PACK + 2 * T], BF16, "late", "da_words0")
+        dc.append(dc_plane(2, late[:, C * PACK : C * PACK + T]))
         r_products(0, da_q0)
-        r_back(0, 0)
+        first_slots = tile([P, C], F32, "r_slots00")
+        nc.vector.tensor_copy(first_slots[:], r_bank[0][:, 0:C])
+        dc.append(dc_plane(3, late[:, C * PACK + T :]))
+        nc.vector.tensor_copy(r_tok[0][:].indirect(list_a[:, 0:LIST_COLS]), first_slots[:])
+        q_bank = [ps.tile([P, T], F32, name=f"q_bank{kb}", tag=f"low{kb}") for kb in range(KB)]
         r_back(0, 1)
-        da_q1 = quantise(gather(da, list_a, 1, "da_words1", "da_q0_codes"), "da_q1")
+        da_words1 = late[:, 0 : C * PACK].rearrange("p (w j) -> p w j", j=PACK)
+        da_q1 = quantise(gather(da, list_a, 1, da_words1), "da_q1")
         r_back(0, 2, "da3")
         r_products(1, da_q1)
 
@@ -216,13 +222,13 @@ def tile_moe_plb_relu_kernel(
             r_back(1, kb)
         r_slots3 = tile([P, T], F32, "r_slots3")
         nc.scalar.copy(r_slots3[:], r_bank[3][:])
-        dc_q0 = quantise(gather(dc, list_c, 0, "dc_words0", "wb_raw00"), "dc_q0")
+        dc_q0 = quantise(gather(dc, list_c, 0, words_tile("dc_words0", "wb_raw00")), "dc_q0")
         r_tok3 = tile([P, WIDE], F32, "r_tok3", "wb_raw00")
         nc.vector.tensor_copy(r_tok3[:].indirect(list_a[:]), r_slots3[:])
         q_products(0, 0, dc_q0, wb_q00)
 
-        sums = [ps.tile([P, T], F32, name=f"sums{kb}", tag=f"high{kb}") for kb in range(KB - 1)]
-        for kb in range(KB - 1):
+        sums = [ps.tile([P, T], F32, name=f"sums{kb}", tag=f"high{kb}") for kb in range(KB - 2)]
+        for kb in range(KB - 2):
             turn(sums[kb], r_tok[kb], True, False)
 
         wb_q01 = quantise(round_wb(0, 1, "wb_q00_codes"), "wb_q01")
@@ -230,7 +236,7 @@ def tile_moe_plb_relu_kernel(
         q_back(0, 0)
         q_back(0, 1, "wb_raw01")
         wb_q10 = quantise(round_wb(1, 0, "wb_q00_plane"), "wb_q10")
-        dc_q1 = quantise(gather(dc, list_c, 1, "dc_words1", "wb_raw10"), "dc_q1")
+        dc_q1 = quantise(gather(dc, list_c, 1, words_tile("dc_words1", "wb_raw10")), "dc_q1")
         q_back(0, 2, "gated_c2")
         q_products(1, 0, dc_q1, wb_q10)
         wb_q11 = quantise(round_wb(1, 1, "gated_c3"), "wb_q11")
@@ -244,6 +250,9 @@ def tile_moe_plb_relu_kernel(
         nc.vector.tensor_copy(q_tok3[:].indirect(list_c[:]), q_slots3[:])
 
         for kb in range(KB - 1):
+            if kb == KB - 2:
+                sums.append(ps.tile([P, T], F32, name="sums2", tag="high0"))
+                turn(sums[kb], r_tok[kb], True, False)
             turn(sums[kb], q_tok[kb], False, True)
             turned = tile([P, T], F32, f"turned{kb}")
             nc.scalar.copy(turned[:], sums[kb][:])
@@ -251,7 +260,7 @@ def tile_moe_plb_relu_kernel(
             turn(back, turned, True, True)
             total = tile([P, T], F32, f"total{kb}")
             nc.scalar.copy(total[:], back[:])
-            nc.sync.dma_start(out=out[kb * P : (kb + 1) * P, :], in_=total[:])
+            nc.scalar.dma_start(out=out[kb * P : (kb + 1) * P, :], in_=total[:])
 
         for h in range(2):
             cols = slice(h * HALF, (h + 1) * HALF)

@@ -47,11 +47,6 @@ def tile_moe_plb_relu_kernel(
         nc.gpsimd.memset(dy_plane[:].bitcast(I32), 0)
         nc.vector.memset(wa_plane[:].bitcast(I32), 0)
 
-        warm_in = tile([P, 2], BF16, "warm_in")
-        warm_out = tile([P, 2], BF16, "warm_out")
-        nc.gpsimd.memset(warm_in[:], 0.0)
-        nc.scalar.activation(warm_out[:], warm_in[:], COPY)
-
         identity = tile([P, P], F32, "identity")
         make_identity(nc, identity[:])
 
@@ -62,8 +57,11 @@ def tile_moe_plb_relu_kernel(
 
         a_planes = a.rearrange("(p t) n -> p t n", t=PACK)
         c_planes = c.rearrange("(p t) n -> p t n", t=PACK)
-        a_sb = [tile([P, T], F32, f"a{t}") for t in range(PACK)]
-        c_sb = [tile([P, T], F32, f"c{t}") for t in range(PACK)]
+        groups = [(0, 1), (1, 3), (3, 4)]
+        a_tiles = [tile([P, hi - lo, T], F32, f"a{lo}") for lo, hi in groups]
+        c_tiles = [tile([P, hi - lo, T], F32, f"c{lo}") for lo, hi in groups]
+        a_sb = [a_tiles[g][:, t - lo, :] for g, (lo, hi) in enumerate(groups) for t in range(lo, hi)]
+        c_sb = [c_tiles[g][:, t - lo, :] for g, (lo, hi) in enumerate(groups) for t in range(lo, hi)]
 
         w2_raw = tile([P, 2 * H], U8, "w2_raw")
         dy_codes = tile([P, T], U32, "dy_codes")
@@ -73,10 +71,10 @@ def tile_moe_plb_relu_kernel(
         nc.sync.dma_start(out=w2_raw[:].bitcast(I32), in_=w2t_words[0].bitcast(I32))
         load_scale_rows(w2_plane_raw, w2t_scales[0])
         nc.sync.dma_start(out=dy_codes[:].bitcast(I32), in_=dy_words[0].rearrange("p t d -> p (t d)").bitcast(I32))
-        for t in range(PACK):
-            nc.sync.dma_start(out=a_sb[t][:], in_=a_planes[:, t, :])
-            nc.sync.dma_start(out=c_sb[t][:], in_=c_planes[:, t, :])
-            if t == 0:
+        for g, (lo, hi) in enumerate(groups):
+            nc.sync.dma_start(out=a_tiles[g][:], in_=a_planes[:, lo:hi, :])
+            nc.sync.dma_start(out=c_tiles[g][:], in_=c_planes[:, lo:hi, :])
+            if g == 0:
                 load_scale_rows(dy_plane, dy_scales[0])
                 nc.sync.dma_start(list_a[:], offs)
         nc.sync.dma_start(out=wa_codes[:].bitcast(I32), in_=wat_words.rearrange("e s p b -> p (e s) b").bitcast(I32))
@@ -116,7 +114,7 @@ def tile_moe_plb_relu_kernel(
         gated_c = [tile([P, T], F32, f"gated_c{t}") for t in range(PACK)]
         for t in range(PACK + 1):
             if t < PACK:
-                nc.vector.scalar_tensor_tensor(gated_c[t][:], a_sb[t][:], 0.0, c_sb[t][:], ALU.is_gt, ALU.mult)
+                nc.vector.scalar_tensor_tensor(gated_c[t][:], a_sb[t], 0.0, c_sb[t], ALU.is_gt, ALU.mult)
             if t > 0:
                 nc.vector.tensor_tensor(da[t - 1], dh[t - 1][:], gated_c[t - 1][:], ALU.mult)
 
@@ -186,7 +184,7 @@ def tile_moe_plb_relu_kernel(
             to_tokens(q_bank[kb], q_tok[kb], list_c, e, f"q_slots{e}{kb}", tag)
 
         def dc_plane(t, plane):
-            nc.vector.scalar_tensor_tensor(plane, a_sb[t][:], 0.0, dh[t][:], ALU.max, ALU.mult)
+            nc.vector.scalar_tensor_tensor(plane, a_sb[t], 0.0, dh[t][:], ALU.max, ALU.mult)
             return plane
 
         def turn(bank, source, start, stop):
@@ -201,7 +199,7 @@ def tile_moe_plb_relu_kernel(
             return tile([P, C, PACK], BF16, name, tag)[:]
 
         da_words0 = gather(da, list_a, 0, words_tile("da_words0", None))
-        dc = [dc_plane(t, tile([P, T], BF16, f"dc{t}", f"gated_c{t + 2}")[:]) for t in range(2)]
+        dc = [dc_plane(0, tile([P, T], BF16, "dc0")[:]), dc_plane(1, tile([P, T], BF16, "dc1", "gated_c2")[:])]
         da_q0 = quantise(da_words0, "da_q0")
         late = tile([P, C * PACK + 2 * T], BF16, "late", "da_words0")
         dc.append(dc_plane(2, late[:, C * PACK : C * PACK + T]))
@@ -237,9 +235,9 @@ def tile_moe_plb_relu_kernel(
         q_back(0, 1, "wb_raw01")
         wb_q10 = quantise(round_wb(1, 0, "wb_q00_plane"), "wb_q10")
         dc_q1 = quantise(gather(dc, list_c, 1, words_tile("dc_words1", "wb_raw10")), "dc_q1")
-        q_back(0, 2, "gated_c2")
+        q_back(0, 2, "dc0")
         q_products(1, 0, dc_q1, wb_q10)
-        wb_q11 = quantise(round_wb(1, 1, "gated_c3"), "wb_q11")
+        wb_q11 = quantise(round_wb(1, 1, "gated_c2"), "wb_q11")
         q_products(1, 1, dc_q1, wb_q11)
 
         for kb in range(KB - 1):

@@ -68,6 +68,7 @@ def tile_moe_plb_relu_kernel(
         wa_codes = tile([P, E, 2 * K], U8, "wa_codes")
         wb_raw = [[tile([P, PACK, HALF], F32, f"wb_raw{e}{h}") for h in range(2)] for e in range(E)]
 
+        nc.sync.dma_start(list_a[:], offs)
         nc.sync.dma_start(out=w2_raw[:].bitcast(I32), in_=w2t_words[0].bitcast(I32))
         load_scale_rows(w2_plane_raw, w2t_scales[0])
         nc.sync.dma_start(out=dy_codes[:].bitcast(I32), in_=dy_words[0].rearrange("p t d -> p (t d)").bitcast(I32))
@@ -76,7 +77,6 @@ def tile_moe_plb_relu_kernel(
             nc.sync.dma_start(out=c_tiles[g][:], in_=c_planes[:, lo:hi, :])
             if g == 0:
                 load_scale_rows(dy_plane, dy_scales[0])
-                nc.sync.dma_start(list_a[:], offs)
         nc.sync.dma_start(out=wa_codes[:].bitcast(I32), in_=wat_words.rearrange("e s p b -> p (e s) b").bitcast(I32))
         wa_rows = wat_scales.bitcast(I32).rearrange("e s (q r) n -> r q (e s) n", r=4)
         for r in range(4):
@@ -131,13 +131,12 @@ def tile_moe_plb_relu_kernel(
             nc.vector.quantize_mx(codes[:].bitcast(FP8X4), plane[:], words.rearrange("p w j -> p (w j)"))
             return codes, plane
 
-        def round_wb(e, h, tag):
-            words = tile([P, HALF, PACK], BF16, f"wb_words{e}{h}", tag)
+        def round_wb(e, h, words):
             nc.scalar.copy(
-                words[:].rearrange("p (g i) j -> p g j i", i=4),
+                words.rearrange("p (g i) j -> p g j i", i=4),
                 wb_raw[e][h][:].rearrange("p j (g i) -> p g j i", i=4),
             )
-            return words[:]
+            return words
 
         r_bank = [ps.tile([P, T], F32, name=f"r_bank{kb}", tag=f"high{kb}") for kb in range(KB)]
         r_tok = [tile([P, T], F32, f"r_tok{kb}") for kb in range(KB - 1)]
@@ -156,11 +155,11 @@ def tile_moe_plb_relu_kernel(
                     stop=True,
                 )
 
-        def q_products(e, h, act, weights):
+        def q_products(e, blocks, act, weights):
             codes, plane = act
             w_codes, w_plane = weights
-            for kb in range(2 * h, 2 * h + 2):
-                cols = slice(P * (kb % 2), P * (kb % 2 + 1))
+            for kb in blocks:
+                cols = slice(P * (kb - blocks[0]), P * (kb - blocks[0] + 1))
                 nc.tensor.matmul_mx(
                     out=q_bank[kb][:, e * C : (e + 1) * C],
                     lhsT=w_codes[:, cols].bitcast(FP8X4),
@@ -215,30 +214,32 @@ def tile_moe_plb_relu_kernel(
         r_back(0, 2, "da3")
         r_products(1, da_q1)
 
-        wb_q00 = quantise(round_wb(0, 0, "da0"), "wb_q00")
+        wb_words0 = tile([P, K * PACK], BF16, "wb_words0", "da0")
+        halves0 = [wb_words0[:, h * HALF * PACK : (h + 1) * HALF * PACK].rearrange("p (w j) -> p w j", j=PACK) for h in range(2)]
+        round_wb(0, 0, halves0[0])
         for kb in range(KB - 1):
             r_back(1, kb)
+        round_wb(0, 1, halves0[1])
+        wb_q0 = quantise(wb_words0[:].rearrange("p (w j) -> p w j", j=PACK), "wb_q0")
         r_slots3 = tile([P, T], F32, "r_slots3")
         nc.scalar.copy(r_slots3[:], r_bank[3][:])
-        dc_q0 = quantise(gather(dc, list_c, 0, words_tile("dc_words0", "wb_raw00")), "dc_q0")
-        r_tok3 = tile([P, WIDE], F32, "r_tok3", "wb_raw00")
+        dc_q0 = quantise(gather(dc, list_c, 0, words_tile("dc_words0", "wb_raw01")), "dc_q0")
+        r_tok3 = tile([P, WIDE], F32, "r_tok3", "wb_raw01")
         nc.vector.tensor_copy(r_tok3[:].indirect(list_a[:]), r_slots3[:])
-        q_products(0, 0, dc_q0, wb_q00)
+        q_products(0, range(KB), dc_q0, wb_q0)
 
         sums = [ps.tile([P, T], F32, name=f"sums{kb}", tag=f"high{kb}") for kb in range(KB - 2)]
         for kb in range(KB - 2):
             turn(sums[kb], r_tok[kb], True, False)
 
-        wb_q01 = quantise(round_wb(0, 1, "wb_q00_codes"), "wb_q01")
-        q_products(0, 1, dc_q0, wb_q01)
         q_back(0, 0)
-        q_back(0, 1, "wb_raw01")
-        wb_q10 = quantise(round_wb(1, 0, "wb_q00_plane"), "wb_q10")
+        q_back(0, 1)
+        wb_q10 = quantise(round_wb(1, 0, words_tile("wb_words10", "wb_q0_plane")), "wb_q10")
         dc_q1 = quantise(gather(dc, list_c, 1, words_tile("dc_words1", "wb_raw10")), "dc_q1")
         q_back(0, 2, "dc0")
-        q_products(1, 0, dc_q1, wb_q10)
-        wb_q11 = quantise(round_wb(1, 1, "gated_c2"), "wb_q11")
-        q_products(1, 1, dc_q1, wb_q11)
+        q_products(1, range(0, 2), dc_q1, wb_q10)
+        wb_q11 = quantise(round_wb(1, 1, words_tile("wb_words11", "gated_c2")), "wb_q11")
+        q_products(1, range(2, 4), dc_q1, wb_q11)
 
         for kb in range(KB - 1):
             q_back(1, kb, "wb_raw11" if kb == 1 else None)

@@ -124,10 +124,10 @@ def tile_moe_plb_relu_kernel(
                 nc.scalar.activation(words[:, :, t], planes[t].indirect(cut), COPY)
             return words
 
-        def quantise(words, name):
+        def quantise(words, name, tag=None):
             width = words.shape[1]
             codes = tile([P, width], U32, name + "_codes")
-            plane = tile([P, width], U8, name + "_plane")
+            plane = tile([P, width], U8, name + "_plane", tag)
             nc.vector.quantize_mx(codes[:].bitcast(FP8X4), plane[:], words.rearrange("p w j -> p (w j)"))
             return codes, plane
 
@@ -140,7 +140,7 @@ def tile_moe_plb_relu_kernel(
 
         r_bank = [ps.tile([P, T], F32, name=f"r_bank{kb}", tag=f"high{kb}") for kb in range(KB)]
         r_tok = [tile([P, T], F32, f"r_tok{kb}") for kb in range(KB - 1)]
-        q_tok = [tile([P, T], F32, f"q_tok{kb}") for kb in range(KB - 1)]
+        q_tok = [tile([P, T if kb < 2 else WIDE], F32, f"q_tok{kb}") for kb in range(KB)]
 
         def r_products(e, act):
             codes, plane = act
@@ -197,6 +197,14 @@ def tile_moe_plb_relu_kernel(
         def words_tile(name, tag):
             return tile([P, C, PACK], BF16, name, tag)[:]
 
+        wb_words0 = [tile([P, HALF, PACK], BF16, f"wb_words0{h}") for h in range(2)]
+        for kb in range(KB):
+            nc.gpsimd.tensor_scalar(
+                wb_words0[kb // 2][:, (kb % 2) * P : (kb % 2 + 1) * P, :],
+                wb_raw[0][kb // 2][:, :, (kb % 2) * P : (kb % 2 + 1) * P].rearrange("p j k -> p k j"),
+                1.0, 0.0, ALU.mult, ALU.add,
+            )
+
         da_words0 = gather(da, list_a, 0, words_tile("da_words0", None))
         dc = [dc_plane(0, tile([P, T], BF16, "dc0")[:]), dc_plane(1, tile([P, T], BF16, "dc1", "gated_c2")[:])]
         da_q0 = quantise(da_words0, "da_q0")
@@ -214,39 +222,36 @@ def tile_moe_plb_relu_kernel(
         r_back(0, 2, "da3")
         r_products(1, da_q1)
 
-        wb_words0 = tile([P, K * PACK], BF16, "wb_words0", "da0")
-        halves0 = [wb_words0[:, h * HALF * PACK : (h + 1) * HALF * PACK].rearrange("p (w j) -> p w j", j=PACK) for h in range(2)]
-        round_wb(0, 0, halves0[0])
+        wb_q10 = quantise(round_wb(1, 0, words_tile("wb_words10", "da0")), "wb_q10")
         for kb in range(KB - 1):
             r_back(1, kb)
-        round_wb(0, 1, halves0[1])
-        wb_q0 = quantise(wb_words0[:].rearrange("p (w j) -> p w j", j=PACK), "wb_q0")
+        wb_q00 = quantise(wb_words0[0][:], "wb_q00", "da_q1_plane")
+        wb_q01 = quantise(wb_words0[1][:], "wb_q01", "da_q1_codes")
         r_slots3 = tile([P, T], F32, "r_slots3")
         nc.scalar.copy(r_slots3[:], r_bank[3][:])
-        dc_q0 = quantise(gather(dc, list_c, 0, words_tile("dc_words0", "wb_raw01")), "dc_q0")
-        r_tok3 = tile([P, WIDE], F32, "r_tok3", "wb_raw01")
+        dc_q0 = quantise(gather(dc, list_c, 0, words_tile("dc_words0", "wb_raw10")), "dc_q0")
+        r_tok3 = tile([P, WIDE], F32, "r_tok3", "wb_raw10")
         nc.vector.tensor_copy(r_tok3[:].indirect(list_a[:]), r_slots3[:])
-        q_products(0, range(KB), dc_q0, wb_q0)
+        q_products(0, range(0, 2), dc_q0, wb_q00)
+        q_products(0, range(2, 4), dc_q0, wb_q01)
 
         sums = [ps.tile([P, T], F32, name=f"sums{kb}", tag=f"high{kb}") for kb in range(KB - 2)]
         for kb in range(KB - 2):
             turn(sums[kb], r_tok[kb], True, False)
 
         q_back(0, 0)
-        q_back(0, 1)
-        wb_q10 = quantise(round_wb(1, 0, words_tile("wb_words10", "wb_q0_plane")), "wb_q10")
-        dc_q1 = quantise(gather(dc, list_c, 1, words_tile("dc_words1", "wb_raw10")), "dc_q1")
-        q_back(0, 2, "dc0")
+        dc_q1 = quantise(gather(dc, list_c, 1, words_tile("dc_words1", "da_q1_plane")), "dc_q1")
+        q_back(0, 1, "dc0")
         q_products(1, range(0, 2), dc_q1, wb_q10)
         wb_q11 = quantise(round_wb(1, 1, words_tile("wb_words11", "gated_c2")), "wb_q11")
         q_products(1, range(2, 4), dc_q1, wb_q11)
 
-        for kb in range(KB - 1):
-            q_back(1, kb, "wb_raw11" if kb == 1 else None)
-        q_slots3 = tile([P, T], F32, "q_slots3")
-        nc.scalar.copy(q_slots3[:], q_bank[3][:])
-        q_tok3 = tile([P, WIDE], F32, "q_tok3")
-        nc.vector.tensor_copy(q_tok3[:].indirect(list_c[:]), q_slots3[:])
+        q_back(1, 0)
+        q_back(1, 1, "wb_raw11")
+        for kb in range(2, KB):
+            q_slots = tile([P, T], F32, f"q_slots{kb}")
+            nc.scalar.copy(q_slots[:], q_bank[kb][:])
+            nc.vector.tensor_copy(q_tok[kb][:].indirect(list_c[:]), q_slots[:])
 
         for kb in range(KB - 1):
             if kb == KB - 2:
@@ -264,5 +269,5 @@ def tile_moe_plb_relu_kernel(
         for h in range(2):
             cols = slice(h * HALF, (h + 1) * HALF)
             last = tile([P, HALF], F32, f"last{h}")
-            nc.vector.tensor_tensor(last[:], r_tok3[:, cols], q_tok3[:, cols], ALU.add)
+            nc.vector.tensor_tensor(last[:], r_tok3[:, cols], q_tok[3][:, cols], ALU.add)
             nc.sync.dma_start(out=out[3 * P : 4 * P, cols], in_=last[:])

@@ -1,7 +1,6 @@
 from contextlib import ExitStack
 
 import concourse.mybir as mybir
-from concourse.masks import make_identity
 
 K, T, H, N = 512, 512, 512, 512
 E, C = 2, 256
@@ -43,12 +42,9 @@ def tile_moe_plb_relu_kernel(
         w2_plane_raw = tile([P, H], U8, "w2_plane_raw")
         dy_plane = tile([P, T], U8, "dy_plane")
         wa_plane = tile([P, E, K], U8, "wa_plane")
-        nc.vector.memset(w2_plane_raw[:].bitcast(I32), 0)
+        nc.gpsimd.memset(w2_plane_raw[:].bitcast(I32), 0)
         nc.gpsimd.memset(dy_plane[:].bitcast(I32), 0)
         nc.vector.memset(wa_plane[:].bitcast(I32), 0)
-
-        identity = tile([P, P], F32, "identity")
-        make_identity(nc, identity[:])
 
         def load_scale_rows(plane, rows):
             by_row = rows.bitcast(I32).rearrange("(q r) n -> r q n", r=4)
@@ -57,35 +53,35 @@ def tile_moe_plb_relu_kernel(
 
         a_planes = a.rearrange("(p t) n -> p t n", t=PACK)
         c_planes = c.rearrange("(p t) n -> p t n", t=PACK)
-        groups = [(0, 1), (1, 3), (3, 4)]
-        a_tiles = [tile([P, hi - lo, T], F32, f"a{lo}") for lo, hi in groups]
-        c_tiles = [tile([P, hi - lo, T], F32, f"c{lo}") for lo, hi in groups]
-        a_sb = [a_tiles[g][:, t - lo, :] for g, (lo, hi) in enumerate(groups) for t in range(lo, hi)]
-        c_sb = [c_tiles[g][:, t - lo, :] for g, (lo, hi) in enumerate(groups) for t in range(lo, hi)]
+        a_sb = [tile([P, T], F32, f"a{t}") for t in range(PACK)]
+        c_sb = [tile([P, T], F32, f"c{t}") for t in range(PACK)]
 
         w2_raw = tile([P, 2 * H], U8, "w2_raw")
         dy_codes = tile([P, T], U32, "dy_codes")
         wa_codes = tile([P, E, 2 * K], U8, "wa_codes")
         wb_raw = [[tile([P, PACK, HALF], F32, f"wb_raw{e}{h}") for h in range(2)] for e in range(E)]
 
-        nc.sync.dma_start(list_a[:], offs)
+        def load_wb(e, h):
+            rows = wbt[e].rearrange("(p j) k -> p j k", j=PACK)
+            nc.sync.dma_start(out=wb_raw[e][h][:], in_=rows[:, :, h * HALF : (h + 1) * HALF])
+
+        nc.sync.dma_start(list_c[:], offs2)
         nc.sync.dma_start(out=w2_raw[:].bitcast(I32), in_=w2t_words[0].bitcast(I32))
         load_scale_rows(w2_plane_raw, w2t_scales[0])
         nc.sync.dma_start(out=dy_codes[:].bitcast(I32), in_=dy_words[0].rearrange("p t d -> p (t d)").bitcast(I32))
-        for g, (lo, hi) in enumerate(groups):
-            nc.sync.dma_start(out=a_tiles[g][:], in_=a_planes[:, lo:hi, :])
-            nc.sync.dma_start(out=c_tiles[g][:], in_=c_planes[:, lo:hi, :])
-            if g == 0:
-                load_scale_rows(dy_plane, dy_scales[0])
+        load_scale_rows(dy_plane, dy_scales[0])
+        for t in range(PACK):
+            nc.sync.dma_start(out=a_sb[t][:], in_=a_planes[:, t, :])
+        for e in range(E):
+            for h in range(2):
+                load_wb(e, h)
+        for t in range(PACK):
+            nc.sync.dma_start(out=c_sb[t][:], in_=c_planes[:, t, :])
+        nc.sync.dma_start(list_a[:], offs)
         nc.sync.dma_start(out=wa_codes[:].bitcast(I32), in_=wat_words.rearrange("e s p b -> p (e s) b").bitcast(I32))
         wa_rows = wat_scales.bitcast(I32).rearrange("e s (q r) n -> r q (e s) n", r=4)
         for r in range(4):
             nc.sync.dma_start(out=wa_plane[r:P:32, :, :].bitcast(I32), in_=wa_rows[r])
-        nc.sync.dma_start(list_c[:], offs2)
-        for e in range(E):
-            rows = wbt[e].rearrange("(p j) k -> p j k", j=PACK)
-            for h in range(2):
-                nc.sync.dma_start(out=wb_raw[e][h][:], in_=rows[:, :, h * HALF : (h + 1) * HALF])
 
         w2_codes = tile([P, 2 * H], U8, "w2_codes")
         w2_plane = tile([P, H], U8, "w2_plane")
@@ -110,37 +106,46 @@ def tile_moe_plb_relu_kernel(
                 stop=True,
             )
 
-        da = [tile([P, T], BF16, f"da{t}")[:] for t in range(PACK)]
-        gated_c = [tile([P, T], F32, f"gated_c{t}") for t in range(PACK)]
-        for t in range(PACK + 1):
-            if t < PACK:
-                nc.vector.scalar_tensor_tensor(gated_c[t][:], a_sb[t], 0.0, c_sb[t], ALU.is_gt, ALU.mult)
-            if t > 0:
-                nc.vector.tensor_tensor(da[t - 1], dh[t - 1][:], gated_c[t - 1][:], ALU.mult)
-
         def gather(planes, offsets, e, words):
             cut = offsets[:, e * LIST_COLS : (e + 1) * LIST_COLS]
             for t in range(PACK):
-                nc.scalar.activation(words[:, :, t], planes[t].indirect(cut), COPY)
+                nc.scalar.activation(words[:, :, t], planes[t][:].indirect(cut), COPY)
             return words
 
-        def quantise(words, name, tag=None):
+        def quantise(words, name):
             width = words.shape[1]
             codes = tile([P, width], U32, name + "_codes")
-            plane = tile([P, width], U8, name + "_plane", tag)
-            nc.vector.quantize_mx(codes[:].bitcast(FP8X4), plane[:], words.rearrange("p w j -> p (w j)"))
+            plane = tile([P, width], U8, name + "_plane")
+            nc.vector.quantize_mx(codes[:].bitcast(FP8X4), plane[:], words[:].rearrange("p w j -> p (w j)"))
             return codes, plane
 
-        def round_wb(e, h, words):
-            nc.scalar.copy(
-                words.rearrange("p (g i) j -> p g j i", i=4),
-                wb_raw[e][h][:].rearrange("p j (g i) -> p g j i", i=4),
+        def round_wb(e, h):
+            words = tile([P, HALF, PACK], BF16, f"wb_words{e}{h}")
+            nc.gpsimd.tensor_scalar(
+                words[:],
+                wb_raw[e][h][:].rearrange("p j k -> p k j"),
+                1.0, 0.0, ALU.mult, ALU.add,
             )
             return words
 
-        r_bank = [ps.tile([P, T], F32, name=f"r_bank{kb}", tag=f"high{kb}") for kb in range(KB)]
-        r_tok = [tile([P, T], F32, f"r_tok{kb}") for kb in range(KB - 1)]
-        q_tok = [tile([P, T if kb < 2 else WIDE], F32, f"q_tok{kb}") for kb in range(KB)]
+        q_bank = [ps.tile([P, T], F32, name=f"q_bank{kb}", tag=f"high{kb}") for kb in range(KB)]
+        q_tok = [tile([P, T], F32, f"q_tok{kb}") for kb in range(KB)]
+        r_tok = [tile([P, T if kb < KB - 1 else WIDE], F32, f"r_tok{kb}") for kb in range(KB)]
+
+        def q_products(e, h, act, weights):
+            codes, plane = act
+            w_codes, w_plane = weights
+            for b in range(2):
+                cols = slice(P * b, P * (b + 1))
+                nc.tensor.matmul_mx(
+                    out=q_bank[2 * h + b][:, e * C : (e + 1) * C],
+                    lhsT=w_codes[:, cols].bitcast(FP8X4),
+                    lhsT_scale=w_plane[:, cols],
+                    rhs=codes[:].bitcast(FP8X4),
+                    rhs_scale=plane[:],
+                    start=True,
+                    stop=True,
+                )
 
         def r_products(e, act):
             codes, plane = act
@@ -149,21 +154,6 @@ def tile_moe_plb_relu_kernel(
                     out=r_bank[kb][:, e * C : (e + 1) * C],
                     lhsT=wa_codes[:, e, 2 * P * kb : 2 * P * (kb + 1)].bitcast(FP4X4),
                     lhsT_scale=wa_plane[:, e, P * kb : P * (kb + 1)],
-                    rhs=codes[:].bitcast(FP8X4),
-                    rhs_scale=plane[:],
-                    start=True,
-                    stop=True,
-                )
-
-        def q_products(e, blocks, act, weights):
-            codes, plane = act
-            w_codes, w_plane = weights
-            for kb in blocks:
-                cols = slice(P * (kb - blocks[0]), P * (kb - blocks[0] + 1))
-                nc.tensor.matmul_mx(
-                    out=q_bank[kb][:, e * C : (e + 1) * C],
-                    lhsT=w_codes[:, cols].bitcast(FP8X4),
-                    lhsT_scale=w_plane[:, cols],
                     rhs=codes[:].bitcast(FP8X4),
                     rhs_scale=plane[:],
                     start=True,
@@ -182,92 +172,58 @@ def tile_moe_plb_relu_kernel(
         def q_back(e, kb, tag=None):
             to_tokens(q_bank[kb], q_tok[kb], list_c, e, f"q_slots{e}{kb}", tag)
 
-        def dc_plane(t, plane):
-            nc.vector.scalar_tensor_tensor(plane, a_sb[t], 0.0, dh[t][:], ALU.max, ALU.mult)
-            return plane
+        def words_tile(name, tag=None):
+            return tile([P, C, PACK], BF16, name, tag)
 
-        def turn(bank, source, start, stop):
-            for tb in range(T // P):
-                cols = slice(tb * P, (tb + 1) * P)
-                nc.tensor.matmul(
-                    bank[:, cols], source[:, cols], identity[:], is_transpose=True,
-                    start=start and tb == 0, stop=stop and tb == T // P - 1,
-                )
+        dc = [tile([P, T], BF16, f"dc{t}") for t in range(PACK)]
+        for t in range(PACK):
+            nc.vector.scalar_tensor_tensor(dc[t][:], a_sb[t][:], 0.0, dh[t][:], ALU.max, ALU.mult)
+        wb_words = [[round_wb(e, h) for h in range(2)] for e in range(E)]
 
-        def words_tile(name, tag):
-            return tile([P, C, PACK], BF16, name, tag)[:]
+        wb_q00 = quantise(wb_words[0][0], "wb_q00")
+        dc_q0 = quantise(gather(dc, list_c, 0, words_tile("dc_words0")), "dc_q0")
+        q_products(0, 0, dc_q0, wb_q00)
 
-        wb_words0 = [tile([P, HALF, PACK], BF16, f"wb_words0{h}") for h in range(2)]
-        for kb in range(KB):
-            nc.gpsimd.tensor_scalar(
-                wb_words0[kb // 2][:, (kb % 2) * P : (kb % 2 + 1) * P, :],
-                wb_raw[0][kb // 2][:, :, (kb % 2) * P : (kb % 2 + 1) * P].rearrange("p j k -> p k j"),
-                1.0, 0.0, ALU.mult, ALU.add,
-            )
-
-        da_words0 = gather(da, list_a, 0, words_tile("da_words0", None))
-        dc = [dc_plane(0, tile([P, T], BF16, "dc0")[:]), dc_plane(1, tile([P, T], BF16, "dc1", "gated_c2")[:])]
-        da_q0 = quantise(da_words0, "da_q0")
-        late = tile([P, C * PACK + 2 * T], BF16, "late", "da_words0")
-        dc.append(dc_plane(2, late[:, C * PACK : C * PACK + T]))
-        r_products(0, da_q0)
-        first_slots = tile([P, C], F32, "r_slots00")
-        nc.vector.tensor_copy(first_slots[:], r_bank[0][:, 0:C])
-        dc.append(dc_plane(3, late[:, C * PACK + T :]))
-        nc.vector.tensor_copy(r_tok[0][:].indirect(list_a[:, 0:LIST_COLS]), first_slots[:])
-        q_bank = [ps.tile([P, T], F32, name=f"q_bank{kb}", tag=f"low{kb}") for kb in range(KB)]
-        r_back(0, 1)
-        da_words1 = late[:, 0 : C * PACK].rearrange("p (w j) -> p w j", j=PACK)
-        da_q1 = quantise(gather(da, list_a, 1, da_words1), "da_q1")
-        r_back(0, 2, "da3")
-        r_products(1, da_q1)
-
-        wb_q10 = quantise(round_wb(1, 0, words_tile("wb_words10", "da0")), "wb_q10")
-        for kb in range(KB - 1):
-            r_back(1, kb)
-        wb_q00 = quantise(wb_words0[0][:], "wb_q00", "da_q1_plane")
-        wb_q01 = quantise(wb_words0[1][:], "wb_q01", "da_q1_codes")
-        r_slots3 = tile([P, T], F32, "r_slots3")
-        nc.scalar.copy(r_slots3[:], r_bank[3][:])
-        dc_q0 = quantise(gather(dc, list_c, 0, words_tile("dc_words0", "wb_raw10")), "dc_q0")
-        r_tok3 = tile([P, WIDE], F32, "r_tok3", "wb_raw10")
-        nc.vector.tensor_copy(r_tok3[:].indirect(list_a[:]), r_slots3[:])
-        q_products(0, range(0, 2), dc_q0, wb_q00)
-        q_products(0, range(2, 4), dc_q0, wb_q01)
-
-        sums = [ps.tile([P, T], F32, name=f"sums{kb}", tag=f"high{kb}") for kb in range(KB - 2)]
-        for kb in range(KB - 2):
-            turn(sums[kb], r_tok[kb], True, False)
+        open_dh = [tile([P, T], F32, f"open_dh{t}") for t in range(PACK)]
+        da = [tile([P, T], BF16, f"da{t}") for t in range(PACK)]
+        for t in range(PACK):
+            nc.vector.scalar_tensor_tensor(open_dh[t][:], a_sb[t][:], 0.0, dh[t][:], ALU.is_gt, ALU.mult)
+            nc.gpsimd.tensor_tensor(da[t][:], open_dh[t][:], c_sb[t][:], ALU.mult)
+        r_bank = [ps.tile([P, T], F32, name=f"r_bank{kb}", tag=f"low{kb}") for kb in range(KB)]
 
         q_back(0, 0)
-        dc_q1 = quantise(gather(dc, list_c, 1, words_tile("dc_words1", "da_q1_plane")), "dc_q1")
-        q_back(0, 1, "dc0")
-        q_products(1, range(0, 2), dc_q1, wb_q10)
-        wb_q11 = quantise(round_wb(1, 1, words_tile("wb_words11", "gated_c2")), "wb_q11")
-        q_products(1, range(2, 4), dc_q1, wb_q11)
-
+        q_back(0, 1)
+        q_products(0, 1, dc_q0, quantise(wb_words[0][1], "wb_q01"))
+        q_back(0, 2)
+        dc_q1 = quantise(gather(dc, list_c, 1, words_tile("dc_words1", "wb_q00_codes")), "dc_q1")
+        q_products(1, 0, dc_q1, quantise(wb_words[1][0], "wb_q10"))
+        q_back(0, 3, "dc3")
         q_back(1, 0)
-        q_back(1, 1, "wb_raw11")
-        for kb in range(2, KB):
-            q_slots = tile([P, T], F32, f"q_slots{kb}")
-            nc.scalar.copy(q_slots[:], q_bank[kb][:])
-            nc.vector.tensor_copy(q_tok[kb][:].indirect(list_c[:]), q_slots[:])
+        q_products(1, 1, dc_q1, quantise(wb_words[1][1], "wb_q11"))
+        q_back(1, 1)
+        da_q0 = quantise(gather(da, list_a, 0, words_tile("da_words0")), "da_q0")
+        r_products(0, da_q0)
+        q_back(1, 2, "open_dh3")
+        q_back(1, 3)
+
+        r_back(0, 0)
+        da_q1 = quantise(gather(da, list_a, 1, words_tile("da_words1")), "da_q1")
+        r_products(1, da_q1)
+        r_back(0, 1, "da3")
+        r_back(0, 2)
+        for kb in range(KB - 1):
+            r_back(1, kb)
+        r_slots3 = tile([P, T], F32, "r_slots3")
+        nc.scalar.copy(r_slots3[:], r_bank[3][:])
+        nc.vector.tensor_copy(r_tok[3][:].indirect(list_a[:]), r_slots3[:])
 
         for kb in range(KB - 1):
-            if kb == KB - 2:
-                sums.append(ps.tile([P, T], F32, name="sums2", tag="high0"))
-                turn(sums[kb], r_tok[kb], True, False)
-            turn(sums[kb], q_tok[kb], False, True)
-            turned = tile([P, T], F32, f"turned{kb}")
-            nc.scalar.copy(turned[:], sums[kb][:])
-            back = ps.tile([P, T], F32, name=f"back{kb}", tag=f"low{kb}")
-            turn(back, turned, True, True)
             total = tile([P, T], F32, f"total{kb}")
-            nc.scalar.copy(total[:], back[:])
+            nc.gpsimd.tensor_tensor(total[:], r_tok[kb][:], q_tok[kb][:], ALU.add)
             nc.scalar.dma_start(out=out[kb * P : (kb + 1) * P, :], in_=total[:])
 
         for h in range(2):
             cols = slice(h * HALF, (h + 1) * HALF)
             last = tile([P, HALF], F32, f"last{h}")
-            nc.vector.tensor_tensor(last[:], r_tok3[:, cols], q_tok[3][:, cols], ALU.add)
+            nc.vector.tensor_tensor(last[:], r_tok[3][:, cols], q_tok[3][:, cols], ALU.add)
             nc.sync.dma_start(out=out[3 * P : 4 * P, cols], in_=last[:])

@@ -53,30 +53,29 @@ def tile_moe_plb_relu_kernel(
 
         a_planes = a.rearrange("(p t) n -> p t n", t=PACK)
         c_planes = c.rearrange("(p t) n -> p t n", t=PACK)
-        a_sb = [tile([P, T], F32, f"a{t}") for t in range(PACK)]
-        c_sb = [tile([P, T], F32, f"c{t}") for t in range(PACK)]
+        a_pairs = [tile([P, 2, T], F32, f"a_pair{u}") for u in range(2)]
+        c_pairs = [tile([P, 2, T], F32, f"c_pair{u}") for u in range(2)]
+        a_sb = [a_pairs[t // 2][:, t % 2, :] for t in range(PACK)]
+        c_sb = [c_pairs[t // 2][:, t % 2, :] for t in range(PACK)]
 
         w2_raw = tile([P, 2 * H], U8, "w2_raw")
         dy_codes = tile([P, T], U32, "dy_codes")
         wa_codes = tile([P, E, 2 * K], U8, "wa_codes")
+        wb_rows = [wbt[e].rearrange("(p j) k -> p j k", j=PACK) for e in range(E)]
         wb_raw = [[tile([P, PACK, HALF], F32, f"wb_raw{e}{h}") for h in range(2)] for e in range(E)]
-
-        def load_wb(e, h):
-            rows = wbt[e].rearrange("(p j) k -> p j k", j=PACK)
-            nc.sync.dma_start(out=wb_raw[e][h][:], in_=rows[:, :, h * HALF : (h + 1) * HALF])
 
         nc.sync.dma_start(list_c[:], offs2)
         nc.sync.dma_start(out=w2_raw[:].bitcast(I32), in_=w2t_words[0].bitcast(I32))
         load_scale_rows(w2_plane_raw, w2t_scales[0])
         nc.sync.dma_start(out=dy_codes[:].bitcast(I32), in_=dy_words[0].rearrange("p t d -> p (t d)").bitcast(I32))
+        nc.sync.dma_start(out=a_pairs[0][:], in_=a_planes[:, 0:2, :])
         load_scale_rows(dy_plane, dy_scales[0])
-        for t in range(PACK):
-            nc.sync.dma_start(out=a_sb[t][:], in_=a_planes[:, t, :])
+        nc.sync.dma_start(out=a_pairs[1][:], in_=a_planes[:, 2:4, :])
         for e in range(E):
             for h in range(2):
-                load_wb(e, h)
-        for t in range(PACK):
-            nc.sync.dma_start(out=c_sb[t][:], in_=c_planes[:, t, :])
+                nc.sync.dma_start(out=wb_raw[e][h][:], in_=wb_rows[e][:, :, h * HALF : (h + 1) * HALF])
+        for u in range(2):
+            nc.sync.dma_start(out=c_pairs[u][:], in_=c_planes[:, 2 * u : 2 * u + 2, :])
         nc.sync.dma_start(list_a[:], offs)
         nc.sync.dma_start(out=wa_codes[:].bitcast(I32), in_=wat_words.rearrange("e s p b -> p (e s) b").bitcast(I32))
         wa_rows = wat_scales.bitcast(I32).rearrange("e s (q r) n -> r q (e s) n", r=4)
@@ -109,117 +108,126 @@ def tile_moe_plb_relu_kernel(
         def gather(planes, offsets, e, words):
             cut = offsets[:, e * LIST_COLS : (e + 1) * LIST_COLS]
             for t in range(PACK):
-                nc.scalar.activation(words[:, :, t], planes[t][:].indirect(cut), COPY)
+                nc.scalar.activation(words[:, :, t], planes[t].indirect(cut), COPY)
             return words
 
-        def quantise(words, name):
+        def quantise(words, name, tag=None):
             width = words.shape[1]
-            codes = tile([P, width], U32, name + "_codes")
+            codes = tile([P, width], U32, name + "_codes", tag)
             plane = tile([P, width], U8, name + "_plane")
-            nc.vector.quantize_mx(codes[:].bitcast(FP8X4), plane[:], words[:].rearrange("p w j -> p (w j)"))
+            nc.vector.quantize_mx(codes[:].bitcast(FP8X4), plane[:], words.rearrange("p w j -> p (w j)"))
             return codes, plane
 
-        def round_wb(e, h):
-            words = tile([P, HALF, PACK], BF16, f"wb_words{e}{h}")
-            nc.gpsimd.tensor_scalar(
-                words[:],
-                wb_raw[e][h][:].rearrange("p j k -> p k j"),
-                1.0, 0.0, ALU.mult, ALU.add,
+        def round_on_gpsimd(words, raw):
+            nc.gpsimd.tensor_scalar(words, raw[:].rearrange("p j k -> p k j"), 1.0, 0.0, ALU.mult, ALU.add)
+            return words
+
+        def round_on_scalar(words, raw):
+            nc.scalar.copy(
+                words.rearrange("p (g i) j -> p g j i", i=4), raw[:].rearrange("p j (g i) -> p g j i", i=4)
             )
             return words
 
-        q_bank = [ps.tile([P, T], F32, name=f"q_bank{kb}", tag=f"high{kb}") for kb in range(KB)]
-        q_tok = [tile([P, T], F32, f"q_tok{kb}") for kb in range(KB)]
-        r_tok = [tile([P, T if kb < KB - 1 else WIDE], F32, f"r_tok{kb}") for kb in range(KB)]
-
-        def q_products(e, h, act, weights):
+        def products(bank, weights, act):
             codes, plane = act
-            w_codes, w_plane = weights
-            for b in range(2):
-                cols = slice(P * b, P * (b + 1))
+            for b, (w_codes, w_plane) in enumerate(weights):
                 nc.tensor.matmul_mx(
-                    out=q_bank[2 * h + b][:, e * C : (e + 1) * C],
-                    lhsT=w_codes[:, cols].bitcast(FP8X4),
-                    lhsT_scale=w_plane[:, cols],
-                    rhs=codes[:].bitcast(FP8X4),
-                    rhs_scale=plane[:],
-                    start=True,
-                    stop=True,
+                    out=bank[:, b, :], lhsT=w_codes, lhsT_scale=w_plane,
+                    rhs=codes[:].bitcast(FP8X4), rhs_scale=plane[:], start=True, stop=True,
                 )
 
-        def r_products(e, act):
-            codes, plane = act
-            for kb in range(KB):
-                nc.tensor.matmul_mx(
-                    out=r_bank[kb][:, e * C : (e + 1) * C],
-                    lhsT=wa_codes[:, e, 2 * P * kb : 2 * P * (kb + 1)].bitcast(FP4X4),
-                    lhsT_scale=wa_plane[:, e, P * kb : P * (kb + 1)],
-                    rhs=codes[:].bitcast(FP8X4),
-                    rhs_scale=plane[:],
-                    start=True,
-                    stop=True,
-                )
+        def wb_blocks(quantised, first):
+            codes, plane = quantised
+            cuts = [slice(P * b, P * (b + 1)) for b in range(first, first + 2)]
+            return [(codes[:, cols].bitcast(FP8X4), plane[:, cols]) for cols in cuts]
 
-        def to_tokens(bank, window, offsets, e, name, tag):
-            slots = tile([P, C], F32, name, tag)
-            nc.scalar.copy(slots[:], bank[:, e * C : (e + 1) * C])
-            cut = offsets[:, e * LIST_COLS : (e + 1) * LIST_COLS]
-            nc.vector.tensor_copy(window[:].indirect(cut), slots[:])
+        def wa_blocks(e, h):
+            return [
+                (wa_codes[:, e, 2 * P * kb : 2 * P * (kb + 1)].bitcast(FP4X4), wa_plane[:, e, P * kb : P * (kb + 1)])
+                for kb in range(2 * h, 2 * h + 2)
+            ]
 
-        def r_back(e, kb, tag=None):
-            to_tokens(r_bank[kb], r_tok[kb], list_a, e, f"r_slots{e}{kb}", tag)
+        def bank_tile(name, tag):
+            return ps.tile([P, 2, C], F32, name=name, tag=tag)
 
-        def q_back(e, kb, tag=None):
-            to_tokens(q_bank[kb], q_tok[kb], list_c, e, f"q_slots{e}{kb}", tag)
+        def slots_of(bank, name, tag=None):
+            slots = tile([P, 2, C], F32, name, tag)
+            nc.scalar.copy(slots[:], bank[:])
+            return slots
 
-        def words_tile(name, tag=None):
-            return tile([P, C, PACK], BF16, name, tag)
+        def scatter(window, offsets, e, values):
+            nc.vector.tensor_copy(window[:].indirect(offsets[:, e * LIST_COLS : (e + 1) * LIST_COLS]), values)
 
-        dc = [tile([P, T], BF16, f"dc{t}") for t in range(PACK)]
+        def words_tile(name, tag=None, width=C):
+            return tile([P, width, PACK], BF16, name, tag)[:]
+
+        q_bank = [[bank_tile(f"q_bank{e}{h}", f"high{2 * e + h}") for h in range(2)] for e in range(E)]
+
+        dc = [tile([P, T], BF16, f"dc{t}")[:] for t in range(PACK)]
         for t in range(PACK):
-            nc.vector.scalar_tensor_tensor(dc[t][:], a_sb[t][:], 0.0, dh[t][:], ALU.max, ALU.mult)
-        wb_words = [[round_wb(e, h) for h in range(2)] for e in range(E)]
+            nc.vector.scalar_tensor_tensor(dc[t], a_sb[t], 0.0, dh[t][:], ALU.max, ALU.mult)
 
-        wb_q00 = quantise(wb_words[0][0], "wb_q00")
-        dc_q0 = quantise(gather(dc, list_c, 0, words_tile("dc_words0")), "dc_q0")
-        q_products(0, 0, dc_q0, wb_q00)
-
+        wb_q00 = quantise(round_on_gpsimd(words_tile("wb_words00"), wb_raw[0][0]), "wb_q00")
         open_dh = [tile([P, T], F32, f"open_dh{t}") for t in range(PACK)]
-        da = [tile([P, T], BF16, f"da{t}") for t in range(PACK)]
         for t in range(PACK):
-            nc.vector.scalar_tensor_tensor(open_dh[t][:], a_sb[t][:], 0.0, dh[t][:], ALU.is_gt, ALU.mult)
-            nc.gpsimd.tensor_tensor(da[t][:], open_dh[t][:], c_sb[t][:], ALU.mult)
-        r_bank = [ps.tile([P, T], F32, name=f"r_bank{kb}", tag=f"low{kb}") for kb in range(KB)]
+            nc.vector.scalar_tensor_tensor(open_dh[t][:], a_sb[t], 0.0, dh[t][:], ALU.is_gt, ALU.mult)
+            if t == 1:
+                dc_q0 = quantise(gather(dc, list_c, 0, words_tile("dc_words0")), "dc_q0")
+                products(q_bank[0][0], wb_blocks(wb_q00, 0), dc_q0)
+        r_bank = [[bank_tile(f"r_bank{e}{h}", f"low{2 * e + h}") for h in range(2)] for e in range(E)]
 
-        q_back(0, 0)
-        q_back(0, 1)
-        q_products(0, 1, dc_q0, quantise(wb_words[0][1], "wb_q01"))
-        q_back(0, 2)
-        dc_q1 = quantise(gather(dc, list_c, 1, words_tile("dc_words1", "wb_q00_codes")), "dc_q1")
-        q_products(1, 0, dc_q1, quantise(wb_words[1][0], "wb_q10"))
-        q_back(0, 3, "dc3")
-        q_back(1, 0)
-        q_products(1, 1, dc_q1, quantise(wb_words[1][1], "wb_q11"))
-        q_back(1, 1)
+        wb_words01 = round_on_scalar(words_tile("wb_words01"), wb_raw[0][1])
+        wb_words1 = words_tile("wb_words1", "dc_words0", K)
+        for h in range(2):
+            round_on_gpsimd(wb_words1[:, h * HALF : (h + 1) * HALF, :], wb_raw[1][h])
+        q_slots00 = [tile([P, C], F32, f"q_slots00{b}") for b in range(2)]
+        for b in range(2):
+            nc.scalar.copy(q_slots00[b][:], q_bank[0][0][:, b, :])
+        wb_q01 = quantise(wb_words01, "wb_q01", "wb_raw11")
+        wb_q1 = quantise(wb_words1, "wb_q1")
+        products(q_bank[0][1], wb_blocks(wb_q01, 0), dc_q0)
+        q_tok = [tile([P, T], F32, f"q_tok{kb}", "wb_words01" if kb == 1 else None) for kb in range(KB)]
+        for b in range(2):
+            scatter(q_tok[b], list_c, 0, q_slots00[b][:])
+        dc_q1 = quantise(gather(dc, list_c, 1, words_tile("dc_words1", "wb_q00_codes")), "dc_q1", "q_slots001")
+        for h in range(2):
+            products(q_bank[1][h], wb_blocks(wb_q1, 2 * h), dc_q1)
+        da_all = tile([P, PACK, T], BF16, "da_all", "wb_q00_codes")
+        da = [da_all[:, t, :] for t in range(PACK)]
+        for t in range(PACK):
+            nc.gpsimd.tensor_tensor(da[t], open_dh[t][:], c_sb[t], ALU.mult)
+        q_slots01 = slots_of(q_bank[0][1], "q_slots01")
+        for b in range(2):
+            scatter(q_tok[2 + b], list_c, 0, q_slots01[:, b, :])
+        q_slots10 = slots_of(q_bank[1][0], "q_slots10")
+        for b in range(2):
+            scatter(q_tok[b], list_c, 1, q_slots10[:, b, :])
         da_q0 = quantise(gather(da, list_a, 0, words_tile("da_words0")), "da_q0")
-        r_products(0, da_q0)
-        q_back(1, 2, "open_dh3")
-        q_back(1, 3)
+        for h in range(2):
+            products(r_bank[0][h], wa_blocks(0, h), da_q0)
+        q_slots11 = slots_of(q_bank[1][1], "q_slots11", "c_pair1")
+        for b in range(2):
+            scatter(q_tok[2 + b], list_c, 1, q_slots11[:, b, :])
 
-        r_back(0, 0)
-        da_q1 = quantise(gather(da, list_a, 1, words_tile("da_words1")), "da_q1")
-        r_products(1, da_q1)
-        r_back(0, 1, "da3")
-        r_back(0, 2)
-        for kb in range(KB - 1):
-            r_back(1, kb)
-        r_slots3 = tile([P, T], F32, "r_slots3")
-        nc.scalar.copy(r_slots3[:], r_bank[3][:])
-        nc.vector.tensor_copy(r_tok[3][:].indirect(list_a[:]), r_slots3[:])
+        r_slots00 = slots_of(r_bank[0][0], "r_slots00")
+        da_q1 = quantise(gather(da, list_a, 1, words_tile("da_words1", "open_dh3")), "da_q1")
+        for h in range(2):
+            products(r_bank[1][h], wa_blocks(1, h), da_q1)
+        r_tok = [tile([P, T if kb < 2 else WIDE], F32, f"r_tok{kb}", "wb_q00_codes" if kb == 1 else None) for kb in range(KB)]
+        for b in range(2):
+            scatter(r_tok[b], list_a, 0, r_slots00[:, b, :])
+        r_slots10 = slots_of(r_bank[1][0], "r_slots10")
+        for b in range(2):
+            scatter(r_tok[b], list_a, 1, r_slots10[:, b, :])
+        r_upper = tile([P, 2, E, C], F32, "r_upper")
+        for e in range(E):
+            nc.scalar.copy(r_upper[:, :, e, :], r_bank[e][1][:])
+        for b in range(2):
+            nc.vector.tensor_copy(r_tok[2 + b][:].indirect(list_a[:]), r_upper[:, b, :, :].rearrange("p e s -> p (e s)"))
 
         for kb in range(KB - 1):
             total = tile([P, T], F32, f"total{kb}")
-            nc.gpsimd.tensor_tensor(total[:], r_tok[kb][:], q_tok[kb][:], ALU.add)
+            nc.gpsimd.tensor_tensor(total[:], r_tok[kb][:, 0:T], q_tok[kb][:], ALU.add)
             nc.scalar.dma_start(out=out[kb * P : (kb + 1) * P, :], in_=total[:])
 
         for h in range(2):

@@ -132,7 +132,7 @@ def tile_moe_plb_relu_kernel(
             codes, plane = act
             for b, (w_codes, w_plane) in enumerate(weights):
                 nc.tensor.matmul_mx(
-                    out=bank[:, b, :], lhsT=w_codes, lhsT_scale=w_plane,
+                    out=bank[b], lhsT=w_codes, lhsT_scale=w_plane,
                     rhs=codes[:].bitcast(FP8X4), rhs_scale=plane[:], start=True, stop=True,
                 )
 
@@ -161,59 +161,66 @@ def tile_moe_plb_relu_kernel(
         def words_tile(name, tag=None, width=C):
             return tile([P, width, PACK], BF16, name, tag)[:]
 
-        q_bank = [[bank_tile(f"q_bank{e}{h}", f"high{2 * e + h}") for h in range(2)] for e in range(E)]
+        def halves(bank):
+            return [bank[:, b, :] for b in range(2)]
+
+        q_first = [ps.tile([P, C], F32, name=f"q_first{b}", tag=f"high{b}") for b in range(2)]
+        q_bank01 = bank_tile("q_bank01", "high2")
+        q_bank10 = bank_tile("q_bank10", "high3")
 
         dc = [tile([P, T], BF16, f"dc{t}")[:] for t in range(PACK)]
         for t in range(PACK):
             nc.vector.scalar_tensor_tensor(dc[t], a_sb[t], 0.0, dh[t][:], ALU.max, ALU.mult)
 
-        wb_q00 = quantise(round_on_gpsimd(words_tile("wb_words00"), wb_raw[0][0]), "wb_q00")
+        wb_words00 = round_on_gpsimd(words_tile("wb_words00"), wb_raw[0][0])
         open_dh = [tile([P, T], F32, f"open_dh{t}") for t in range(PACK)]
         for t in range(PACK):
             nc.vector.scalar_tensor_tensor(open_dh[t][:], a_sb[t], 0.0, dh[t][:], ALU.is_gt, ALU.mult)
             if t == 1:
+                wb_q00 = quantise(wb_words00, "wb_q00")
                 dc_q0 = quantise(gather(dc, list_c, 0, words_tile("dc_words0")), "dc_q0")
-                products(q_bank[0][0], wb_blocks(wb_q00, 0), dc_q0)
+                products([bank[:] for bank in q_first], wb_blocks(wb_q00, 0), dc_q0)
         r_bank = [[bank_tile(f"r_bank{e}{h}", f"low{2 * e + h}") for h in range(2)] for e in range(E)]
 
         wb_words01 = round_on_scalar(words_tile("wb_words01"), wb_raw[0][1])
-        wb_words1 = words_tile("wb_words1", "dc_words0", K)
+        wb_q01 = quantise(wb_words01, "wb_q01")
+        wb_words1 = words_tile("wb_words1", "wb_words01", K)
         for h in range(2):
             round_on_gpsimd(wb_words1[:, h * HALF : (h + 1) * HALF, :], wb_raw[1][h])
         q_slots00 = [tile([P, C], F32, f"q_slots00{b}") for b in range(2)]
         for b in range(2):
-            nc.scalar.copy(q_slots00[b][:], q_bank[0][0][:, b, :])
-        wb_q01 = quantise(wb_words01, "wb_q01", "wb_raw11")
-        wb_q1 = quantise(wb_words1, "wb_q1")
-        products(q_bank[0][1], wb_blocks(wb_q01, 0), dc_q0)
-        q_tok = [tile([P, T], F32, f"q_tok{kb}", "wb_words01" if kb == 1 else None) for kb in range(KB)]
+            nc.scalar.copy(q_slots00[b][:], q_first[b][:])
+        products(halves(q_bank01), wb_blocks(wb_q01, 0), dc_q0)
+        q_tok = [tile([P, T], F32, f"q_tok{kb}") for kb in range(KB)]
         for b in range(2):
             scatter(q_tok[b], list_c, 0, q_slots00[b][:])
-        dc_q1 = quantise(gather(dc, list_c, 1, words_tile("dc_words1", "wb_q00_codes")), "dc_q1", "q_slots001")
-        for h in range(2):
-            products(q_bank[1][h], wb_blocks(wb_q1, 2 * h), dc_q1)
-        da_all = tile([P, PACK, T], BF16, "da_all", "wb_q00_codes")
+        dc_q1 = quantise(gather(dc, list_c, 1, words_tile("dc_words1", "wb_q00_codes")), "dc_q1")
+        wb_q1 = quantise(wb_words1, "wb_q1")
+        q_bank11 = bank_tile("q_bank11", "high0")
+        for h, bank in enumerate((q_bank10, q_bank11)):
+            products(halves(bank), wb_blocks(wb_q1, 2 * h), dc_q1)
+        da_all = tile([P, PACK, T], BF16, "da_all", "wb_words01")
         da = [da_all[:, t, :] for t in range(PACK)]
         for t in range(PACK):
             nc.gpsimd.tensor_tensor(da[t], open_dh[t][:], c_sb[t], ALU.mult)
-        q_slots01 = slots_of(q_bank[0][1], "q_slots01")
+        q_slots01 = slots_of(q_bank01, "q_slots01", "wb_raw11")
         for b in range(2):
             scatter(q_tok[2 + b], list_c, 0, q_slots01[:, b, :])
-        q_slots10 = slots_of(q_bank[1][0], "q_slots10")
+        q_slots10 = slots_of(q_bank10, "q_slots10")
         for b in range(2):
             scatter(q_tok[b], list_c, 1, q_slots10[:, b, :])
         da_q0 = quantise(gather(da, list_a, 0, words_tile("da_words0")), "da_q0")
         for h in range(2):
-            products(r_bank[0][h], wa_blocks(0, h), da_q0)
-        q_slots11 = slots_of(q_bank[1][1], "q_slots11", "c_pair1")
+            products(halves(r_bank[0][h]), wa_blocks(0, h), da_q0)
+        q_slots11 = slots_of(q_bank11, "q_slots11", "c_pair1")
         for b in range(2):
             scatter(q_tok[2 + b], list_c, 1, q_slots11[:, b, :])
 
         r_slots00 = slots_of(r_bank[0][0], "r_slots00")
         da_q1 = quantise(gather(da, list_a, 1, words_tile("da_words1", "open_dh3")), "da_q1")
         for h in range(2):
-            products(r_bank[1][h], wa_blocks(1, h), da_q1)
-        r_tok = [tile([P, T if kb < 2 else WIDE], F32, f"r_tok{kb}", "wb_q00_codes" if kb == 1 else None) for kb in range(KB)]
+            products(halves(r_bank[1][h]), wa_blocks(1, h), da_q1)
+        r_tok = [tile([P, T if kb < 2 else WIDE], F32, f"r_tok{kb}", "wb_words01" if kb == 1 else None) for kb in range(KB)]
         for b in range(2):
             scatter(r_tok[b], list_a, 0, r_slots00[:, b, :])
         r_slots10 = slots_of(r_bank[1][0], "r_slots10")

@@ -62,7 +62,8 @@ def tile_moe_plb_relu_kernel(
         dy_codes = tile([P, T], U32, "dy_codes")
         wa_codes = tile([P, E, 2 * K], U8, "wa_codes")
         wb_rows = [wbt[e].rearrange("(p j) k -> p j k", j=PACK) for e in range(E)]
-        wb_raw = [[tile([P, PACK, HALF], F32, f"wb_raw{e}{h}") for h in range(2)] for e in range(E)]
+        wb_first = [tile([P, PACK, P], F32, f"wb_first{b}") for b in range(2)]
+        wb_raw = {(e, h): tile([P, PACK, HALF], F32, f"wb_raw{e}{h}") for e, h in ((0, 1), (1, 0), (1, 1))}
 
         nc.sync.dma_start(list_c[:], offs2)
         nc.sync.dma_start(out=w2_raw[:].bitcast(I32), in_=w2t_words[0].bitcast(I32))
@@ -71,9 +72,10 @@ def tile_moe_plb_relu_kernel(
         nc.sync.dma_start(out=a_pairs[0][:], in_=a_planes[:, 0:2, :])
         load_scale_rows(dy_plane, dy_scales[0])
         nc.sync.dma_start(out=a_pairs[1][:], in_=a_planes[:, 2:4, :])
-        for e in range(E):
-            for h in range(2):
-                nc.sync.dma_start(out=wb_raw[e][h][:], in_=wb_rows[e][:, :, h * HALF : (h + 1) * HALF])
+        for b in range(2):
+            nc.sync.dma_start(out=wb_first[b][:], in_=wb_rows[0][:, :, b * P : (b + 1) * P])
+        for (e, h), raw in wb_raw.items():
+            nc.sync.dma_start(out=raw[:], in_=wb_rows[e][:, :, h * HALF : (h + 1) * HALF])
         for u in range(2):
             nc.sync.dma_start(out=c_pairs[u][:], in_=c_planes[:, 2 * u : 2 * u + 2, :])
         nc.sync.dma_start(list_a[:], offs)
@@ -172,7 +174,9 @@ def tile_moe_plb_relu_kernel(
         for t in range(PACK):
             nc.vector.scalar_tensor_tensor(dc[t], a_sb[t], 0.0, dh[t][:], ALU.max, ALU.mult)
 
-        wb_words00 = round_on_gpsimd(words_tile("wb_words00"), wb_raw[0][0])
+        wb_words00 = words_tile("wb_words00")
+        for b in range(2):
+            round_on_gpsimd(wb_words00[:, b * P : (b + 1) * P, :], wb_first[b])
         open_dh = [tile([P, T], F32, f"open_dh{t}") for t in range(PACK)]
         for t in range(PACK):
             nc.vector.scalar_tensor_tensor(open_dh[t][:], a_sb[t], 0.0, dh[t][:], ALU.is_gt, ALU.mult)
@@ -182,11 +186,11 @@ def tile_moe_plb_relu_kernel(
                 products([bank[:] for bank in q_first], wb_blocks(wb_q00, 0), dc_q0)
         r_bank = [[bank_tile(f"r_bank{e}{h}", f"low{2 * e + h}") for h in range(2)] for e in range(E)]
 
-        wb_words01 = round_on_scalar(words_tile("wb_words01"), wb_raw[0][1])
+        wb_words01 = round_on_scalar(words_tile("wb_words01"), wb_raw[0, 1])
         wb_q01 = quantise(wb_words01, "wb_q01")
         wb_words1 = words_tile("wb_words1", "wb_words01", K)
         for h in range(2):
-            round_on_gpsimd(wb_words1[:, h * HALF : (h + 1) * HALF, :], wb_raw[1][h])
+            round_on_gpsimd(wb_words1[:, h * HALF : (h + 1) * HALF, :], wb_raw[1, h])
         q_slots00 = [tile([P, C], F32, f"q_slots00{b}") for b in range(2)]
         for b in range(2):
             nc.scalar.copy(q_slots00[b][:], q_first[b][:])

@@ -130,45 +130,41 @@ def tile_moe_plb_relu_kernel(
             )
             return words
 
-        def products(bank, weights, act):
-            codes, plane = act
-            for b, (w_codes, w_plane) in enumerate(weights):
-                nc.tensor.matmul_mx(
-                    out=bank[b], lhsT=w_codes, lhsT_scale=w_plane,
-                    rhs=codes[:].bitcast(FP8X4), rhs_scale=plane[:], start=True, stop=True,
-                )
+        def product(target, weights, act):
+            nc.tensor.matmul_mx(
+                out=target, lhsT=weights[0], lhsT_scale=weights[1],
+                rhs=act[0][:].bitcast(FP8X4), rhs_scale=act[1][:], start=True, stop=True,
+            )
 
-        def wb_blocks(quantised, first):
-            codes, plane = quantised
-            cuts = [slice(P * b, P * (b + 1)) for b in range(first, first + 2)]
-            return [(codes[:, cols].bitcast(FP8X4), plane[:, cols]) for cols in cuts]
+        def wb_block(quantised, b):
+            cols = slice(P * b, P * (b + 1))
+            return quantised[0][:, cols].bitcast(FP8X4), quantised[1][:, cols]
 
-        def wa_blocks(e, h):
-            return [
-                (wa_codes[:, e, 2 * P * kb : 2 * P * (kb + 1)].bitcast(FP4X4), wa_plane[:, e, P * kb : P * (kb + 1)])
-                for kb in range(2 * h, 2 * h + 2)
-            ]
+        def wa_block(e, kb):
+            return wa_codes[:, e, 2 * P * kb : 2 * P * (kb + 1)].bitcast(FP4X4), wa_plane[:, e, P * kb : P * (kb + 1)]
 
-        def bank_tile(name, tag):
-            return ps.tile([P, 2, C], F32, name=name, tag=tag)
+        def bank_tile(name, tag, parts):
+            return ps.tile([P, parts * C], F32, name=name, tag=tag)
+
+        def part(bank, u):
+            return bank[:, u * C : (u + 1) * C]
 
         def slots_of(bank, name, tag=None):
-            slots = tile([P, 2, C], F32, name, tag)
+            slots = tile([P, bank.shape[1]], F32, name, tag)
             nc.scalar.copy(slots[:], bank[:])
             return slots
 
         def scatter(window, offsets, e, values):
             nc.vector.tensor_copy(window[:].indirect(offsets[:, e * LIST_COLS : (e + 1) * LIST_COLS]), values)
 
+        def scatter_all(window, offsets, values):
+            nc.vector.tensor_copy(window[:].indirect(offsets[:]), values[:])
+
         def words_tile(name, tag=None, width=C):
             return tile([P, width, PACK], BF16, name, tag)[:]
 
-        def halves(bank):
-            return [bank[:, b, :] for b in range(2)]
-
-        q_first = [ps.tile([P, C], F32, name=f"q_first{b}", tag=f"high{b}") for b in range(2)]
-        q_bank01 = bank_tile("q_bank01", "high2")
-        q_bank10 = bank_tile("q_bank10", "high3")
+        q00, q01, q02 = [bank_tile(f"q0{kb}", f"high{kb}", 1) for kb in range(3)]
+        q_last = bank_tile("q_last", "high3", E)
 
         dc = [tile([P, T], BF16, f"dc{t}")[:] for t in range(PACK)]
         for t in range(PACK):
@@ -183,60 +179,62 @@ def tile_moe_plb_relu_kernel(
             if t == 1:
                 wb_q00 = quantise(wb_words00, "wb_q00")
                 dc_q0 = quantise(gather(dc, list_c, 0, words_tile("dc_words0")), "dc_q0")
-                products([bank[:] for bank in q_first], wb_blocks(wb_q00, 0), dc_q0)
-        r_bank = [[bank_tile(f"r_bank{e}{h}", f"low{2 * e + h}") for h in range(2)] for e in range(E)]
+                product(q00[:], wb_block(wb_q00, 0), dc_q0)
+                product(q01[:], wb_block(wb_q00, 1), dc_q0)
 
         wb_words01 = round_on_scalar(words_tile("wb_words01"), wb_raw[0, 1])
         wb_q01 = quantise(wb_words01, "wb_q01")
         wb_words1 = words_tile("wb_words1", "wb_words01", K)
         for h in range(2):
             round_on_gpsimd(wb_words1[:, h * HALF : (h + 1) * HALF, :], wb_raw[1, h])
-        q_slots00 = [tile([P, C], F32, f"q_slots00{b}") for b in range(2)]
-        for b in range(2):
-            nc.scalar.copy(q_slots00[b][:], q_first[b][:])
-        products(halves(q_bank01), wb_blocks(wb_q01, 0), dc_q0)
-        q_tok = [tile([P, T], F32, f"q_tok{kb}") for kb in range(KB)]
-        for b in range(2):
-            scatter(q_tok[b], list_c, 0, q_slots00[b][:])
+        q_slots00 = slots_of(q00, "q_slots00")
+        q_slots01 = slots_of(q01, "q_slots01")
+        product(q02[:], wb_block(wb_q01, 0), dc_q0)
+        product(part(q_last, 0), wb_block(wb_q01, 1), dc_q0)
+        q_tok = [tile([P, T if kb < 3 else WIDE], F32, f"q_tok{kb}") for kb in range(KB)]
+        scatter(q_tok[0], list_c, 0, q_slots00[:])
+        scatter(q_tok[1], list_c, 0, q_slots01[:])
         dc_q1 = quantise(gather(dc, list_c, 1, words_tile("dc_words1", "wb_q00_codes")), "dc_q1")
         wb_q1 = quantise(wb_words1, "wb_q1")
-        q_bank11 = bank_tile("q_bank11", "high0")
-        for h, bank in enumerate((q_bank10, q_bank11)):
-            products(halves(bank), wb_blocks(wb_q1, 2 * h), dc_q1)
+        q10 = bank_tile("q10", "high0", 1)
+        q1_middle = bank_tile("q1_middle", "high1", 2)
+        product(q10[:], wb_block(wb_q1, 0), dc_q1)
+        for u in range(2):
+            product(part(q1_middle, u), wb_block(wb_q1, 1 + u), dc_q1)
+        product(part(q_last, 1), wb_block(wb_q1, 3), dc_q1)
         da_all = tile([P, PACK, T], BF16, "da_all", "wb_words01")
         da = [da_all[:, t, :] for t in range(PACK)]
         for t in range(PACK):
             nc.gpsimd.tensor_tensor(da[t], open_dh[t][:], c_sb[t], ALU.mult)
-        q_slots01 = slots_of(q_bank01, "q_slots01", "wb_raw11")
-        for b in range(2):
-            scatter(q_tok[2 + b], list_c, 0, q_slots01[:, b, :])
-        q_slots10 = slots_of(q_bank10, "q_slots10")
-        for b in range(2):
-            scatter(q_tok[b], list_c, 1, q_slots10[:, b, :])
+        scatter(q_tok[2], list_c, 0, slots_of(q02, "q_slots02", "wb_raw11")[:])
+        scatter(q_tok[0], list_c, 1, slots_of(q10, "q_slots10")[:])
+        q_slots_middle = slots_of(q1_middle, "q_slots_middle")
+        for u in range(2):
+            scatter(q_tok[1 + u], list_c, 1, part(q_slots_middle, u))
+
+        r00 = bank_tile("r00", "low0", 1)
+        r10 = bank_tile("r10", "high2", 1)
+        r_both = [bank_tile(f"r_both{kb}", f"low{kb}", E) for kb in range(1, KB)]
         da_q0 = quantise(gather(da, list_a, 0, words_tile("da_words0")), "da_q0")
-        for h in range(2):
-            products(halves(r_bank[0][h]), wa_blocks(0, h), da_q0)
-        q_slots11 = slots_of(q_bank11, "q_slots11", "c_pair1")
-        for b in range(2):
-            scatter(q_tok[2 + b], list_c, 1, q_slots11[:, b, :])
+        product(r00[:], wa_block(0, 0), da_q0)
+        for kb in range(1, KB):
+            product(part(r_both[kb - 1], 0), wa_block(0, kb), da_q0)
+        scatter_all(q_tok[3], list_c, slots_of(q_last, "q_slots_last", "c_pair1"))
 
-        r_slots00 = slots_of(r_bank[0][0], "r_slots00")
+        r_slots00 = slots_of(r00, "r_slots00")
         da_q1 = quantise(gather(da, list_a, 1, words_tile("da_words1", "open_dh3")), "da_q1")
-        for h in range(2):
-            products(halves(r_bank[1][h]), wa_blocks(1, h), da_q1)
-        r_tok = [tile([P, T if kb < 2 else WIDE], F32, f"r_tok{kb}", "wb_words01" if kb == 1 else None) for kb in range(KB)]
-        for b in range(2):
-            scatter(r_tok[b], list_a, 0, r_slots00[:, b, :])
-        r_slots10 = slots_of(r_bank[1][0], "r_slots10")
-        for b in range(2):
-            scatter(r_tok[b], list_a, 1, r_slots10[:, b, :])
-        r_upper = tile([P, 2, E, C], F32, "r_upper")
-        for e in range(E):
-            nc.scalar.copy(r_upper[:, :, e, :], r_bank[e][1][:])
-        for b in range(2):
-            nc.vector.tensor_copy(r_tok[2 + b][:].indirect(list_a[:]), r_upper[:, b, :, :].rearrange("p e s -> p (e s)"))
+        for kb in range(1, KB):
+            product(part(r_both[kb - 1], 1), wa_block(1, kb), da_q1)
+            if kb == 1:
+                product(r10[:], wa_block(1, 0), da_q1)
+        r_tok = [tile([P, WIDE if kb else T], F32, f"r_tok{kb}", None if kb else "wb_words01") for kb in range(KB)]
+        scatter(r_tok[0], list_a, 0, r_slots00[:])
+        for kb in range(1, KB):
+            scatter_all(r_tok[kb], list_a, slots_of(r_both[kb - 1], f"r_slots_both{kb}"))
+            if kb == 1:
+                scatter(r_tok[0], list_a, 1, slots_of(r10, "r_slots10")[:])
 
-        for kb in range(KB - 1):
+        for kb in (1, 0, 2):
             total = tile([P, T], F32, f"total{kb}")
             nc.gpsimd.tensor_tensor(total[:], r_tok[kb][:, 0:T], q_tok[kb][:], ALU.add)
             nc.scalar.dma_start(out=out[kb * P : (kb + 1) * P, :], in_=total[:])

@@ -107,38 +107,37 @@ def tile_moe_plb_relu_kernel(
                 stop=True,
             )
 
-        def gather(planes, offsets, e, words):
-            cut = offsets[:, e * LIST_COLS : (e + 1) * LIST_COLS]
+        def gather(planes, cut, words):
             for t in range(PACK):
                 nc.scalar.activation(words[:, :, t], planes[t].indirect(cut), COPY)
             return words
 
-        def quantise(words, name, tag=None):
-            width = words.shape[1]
-            codes = tile([P, width], U32, name + "_codes", tag)
+        def quantise(values, name):
+            width = values.shape[1] // PACK
+            codes = tile([P, width], U32, name + "_codes")
             plane = tile([P, width], U8, name + "_plane")
-            nc.vector.quantize_mx(codes[:].bitcast(FP8X4), plane[:], words.rearrange("p w j -> p (w j)"))
+            nc.vector.quantize_mx(codes[:].bitcast(FP8X4), plane[:], values)
             return codes, plane
 
         def round_on_gpsimd(words, raw):
-            nc.gpsimd.tensor_scalar(words, raw[:].rearrange("p j k -> p k j"), 1.0, 0.0, ALU.mult, ALU.add)
+            nc.gpsimd.tensor_scalar(words, raw.rearrange("p j k -> p k j"), 1.0, 0.0, ALU.mult, ALU.add)
             return words
 
         def round_on_scalar(words, raw):
             nc.scalar.copy(
-                words.rearrange("p (g i) j -> p g j i", i=4), raw[:].rearrange("p j (g i) -> p g j i", i=4)
+                words.rearrange("p (g i) j -> p g j i", i=4), raw.rearrange("p j (g i) -> p g j i", i=4)
             )
             return words
+
+        def columns(quantised, first, count):
+            codes, plane = quantised
+            return codes[:, first : first + count].bitcast(FP8X4), plane[:, first : first + count]
 
         def product(target, weights, act):
             nc.tensor.matmul_mx(
                 out=target, lhsT=weights[0], lhsT_scale=weights[1],
-                rhs=act[0][:].bitcast(FP8X4), rhs_scale=act[1][:], start=True, stop=True,
+                rhs=act[0], rhs_scale=act[1], start=True, stop=True,
             )
-
-        def wb_block(quantised, b):
-            cols = slice(P * b, P * (b + 1))
-            return quantised[0][:, cols].bitcast(FP8X4), quantised[1][:, cols]
 
         def wa_block(e, kb):
             return wa_codes[:, e, 2 * P * kb : 2 * P * (kb + 1)].bitcast(FP4X4), wa_plane[:, e, P * kb : P * (kb + 1)]
@@ -154,89 +153,92 @@ def tile_moe_plb_relu_kernel(
             nc.scalar.copy(slots[:], bank[:])
             return slots
 
-        def scatter(window, offsets, e, values):
-            nc.vector.tensor_copy(window[:].indirect(offsets[:, e * LIST_COLS : (e + 1) * LIST_COLS]), values)
+        def expert_list(offsets, e):
+            return offsets[:, e * LIST_COLS : (e + 1) * LIST_COLS]
 
-        def scatter_all(window, offsets, values):
-            nc.vector.tensor_copy(window[:].indirect(offsets[:]), values[:])
+        def scatter(window, cut, values):
+            nc.vector.tensor_copy(window[:].indirect(cut), values)
 
-        def words_tile(name, tag=None, width=C):
-            return tile([P, width, PACK], BF16, name, tag)[:]
+        stage = tile([P, PACK * (P + 4 * C)], BF16, "stage")
 
-        q00, q01, q02 = [bank_tile(f"q0{kb}", f"high{kb}", 1) for kb in range(3)]
-        q_last = bank_tile("q_last", "high3", E)
+        def staged(first, count):
+            return stage[:, PACK * first : PACK * (first + count)].rearrange("p (w j) -> p w j", j=PACK)
 
         dc = [tile([P, T], BF16, f"dc{t}")[:] for t in range(PACK)]
+        open_dh = [tile([P, T], F32, f"open_dh{t}") for t in range(PACK)]
+
+        def mask_dh(t):
+            nc.vector.scalar_tensor_tensor(open_dh[t][:], a_sb[t], 0.0, dh[t][:], ALU.is_gt, ALU.mult)
+
         for t in range(PACK):
             nc.vector.scalar_tensor_tensor(dc[t], a_sb[t], 0.0, dh[t][:], ALU.max, ALU.mult)
-
-        wb_words00 = words_tile("wb_words00")
-        for b in range(2):
-            round_on_gpsimd(wb_words00[:, b * P : (b + 1) * P, :], wb_first[b])
-        open_dh = [tile([P, T], F32, f"open_dh{t}") for t in range(PACK)]
-        for t in range(PACK):
-            nc.vector.scalar_tensor_tensor(open_dh[t][:], a_sb[t], 0.0, dh[t][:], ALU.is_gt, ALU.mult)
             if t == 1:
-                wb_q00 = quantise(wb_words00, "wb_q00")
-                dc_q0 = quantise(gather(dc, list_c, 0, words_tile("dc_words0")), "dc_q0")
-                product(q00[:], wb_block(wb_q00, 0), dc_q0)
-                product(q01[:], wb_block(wb_q00, 1), dc_q0)
+                mask_dh(0)
+        mask_dh(1)
 
-        wb_words01 = round_on_scalar(words_tile("wb_words01"), wb_raw[0, 1])
-        wb_q01 = quantise(wb_words01, "wb_q01")
-        wb_words1 = words_tile("wb_words1", "wb_words01", K)
-        for h in range(2):
-            round_on_gpsimd(wb_words1[:, h * HALF : (h + 1) * HALF, :], wb_raw[1, h])
-        q_slots00 = slots_of(q00, "q_slots00")
-        q_slots01 = slots_of(q01, "q_slots01")
-        product(q02[:], wb_block(wb_q01, 0), dc_q0)
-        product(part(q_last, 0), wb_block(wb_q01, 1), dc_q0)
-        q_tok = [tile([P, T if kb < 3 else WIDE], F32, f"q_tok{kb}") for kb in range(KB)]
-        scatter(q_tok[0], list_c, 0, q_slots00[:])
-        scatter(q_tok[1], list_c, 0, q_slots01[:])
-        dc_q1 = quantise(gather(dc, list_c, 1, words_tile("dc_words1", "wb_q00_codes")), "dc_q1")
-        wb_q1 = quantise(wb_words1, "wb_q1")
-        q10 = bank_tile("q10", "high0", 1)
-        q1_middle = bank_tile("q1_middle", "high1", 2)
-        product(q10[:], wb_block(wb_q1, 0), dc_q1)
-        for u in range(2):
-            product(part(q1_middle, u), wb_block(wb_q1, 1 + u), dc_q1)
-        product(part(q_last, 1), wb_block(wb_q1, 3), dc_q1)
-        da_all = tile([P, PACK, T], BF16, "da_all", "wb_words01")
-        da = [da_all[:, t, :] for t in range(PACK)]
+        for b in range(2):
+            round_on_gpsimd(staged(b * P, P), wb_first[b][:])
+        round_on_gpsimd(staged(4 * P, HALF), wb_raw[0, 1][:])
+        gather(dc, expert_list(list_c, 0), staged(HALF, C))
+        early = quantise(stage[:, 0 : PACK * (HALF + C)], "early")
+        dc_q0 = columns(early, HALF, C)
+        q00, q01 = [bank_tile(f"q0{kb}", f"high{kb}", 1) for kb in range(2)]
+        product(q00[:], columns(early, 0, P), dc_q0)
+        product(q01[:], columns(early, P, P), dc_q0)
+
+        gather(dc, expert_list(list_c, 1), staged(7 * P, C))
+        round_on_gpsimd(staged(P, HALF), wb_raw[1, 0][:])
+        round_on_gpsimd(staged(3 * P, P), wb_raw[1, 1][:, :, 0:P])
+        round_on_scalar(staged(6 * P, P), wb_raw[1, 1][:, :, P:HALF])
+
+        mask_dh(2)
+        q_slots00 = tile([P, C], F32, "q_slots00")
+        nc.vector.tensor_copy(q_slots00[:], q00[:])
+        mask_dh(3)
+        q_tok = [tile([P, T if kb < 2 else WIDE], F32, f"q_tok{kb}") for kb in range(KB)]
+        scatter(q_tok[0], expert_list(list_c, 0), q_slots00[:])
+
+        late = quantise(stage[:, PACK * P :], "late")
+        dc_q1 = columns(late, 6 * P, C)
+        q10, q11 = bank_tile("q10", "high0", 1), bank_tile("q11", "low0", 1)
+        q_both = [bank_tile(f"q_both{kb}", f"high{kb}", E) for kb in range(2, KB)]
+        product(q10[:], columns(late, 0, P), dc_q1)
+        for u, (first0, first1) in enumerate(((3 * P, 2 * P), (4 * P, 5 * P))):
+            product(part(q_both[u], 0), columns(late, first0, P), dc_q0)
+            product(part(q_both[u], 1), columns(late, first1, P), dc_q1)
+        product(q11[:], columns(late, P, P), dc_q1)
+
+        da_windows = [stage[:, PACK * P + t * WIDE : PACK * P + (t + 1) * WIDE] for t in range(PACK)]
         for t in range(PACK):
-            nc.gpsimd.tensor_tensor(da[t], open_dh[t][:], c_sb[t], ALU.mult)
-        scatter(q_tok[2], list_c, 0, slots_of(q02, "q_slots02", "wb_raw11")[:])
-        scatter(q_tok[0], list_c, 1, slots_of(q10, "q_slots10")[:])
-        q_slots_middle = slots_of(q1_middle, "q_slots_middle")
+            nc.gpsimd.tensor_tensor(da_windows[t][:, 0:T], open_dh[t][:], c_sb[t], ALU.mult)
+
+        scatter(q_tok[1], expert_list(list_c, 0), slots_of(q01, "q_slots01", "wb_raw11")[:])
+        scatter(q_tok[0], expert_list(list_c, 1), slots_of(q10, "q_slots10")[:])
         for u in range(2):
-            scatter(q_tok[1 + u], list_c, 1, part(q_slots_middle, u))
+            scatter(q_tok[2 + u], list_c[:], slots_of(q_both[u], f"q_slots_both{u}")[:])
 
-        r00 = bank_tile("r00", "low0", 1)
-        r10 = bank_tile("r10", "high2", 1)
+        da_words = tile([P, T, PACK], BF16, "da_words")
+        gather(da_windows, list_a[:], da_words[:])
+        da_q = quantise(da_words[:].rearrange("p w j -> p (w j)"), "da_q")
+        r_first = [bank_tile(f"r_first{e}", f"high{e}", 1) for e in range(E)]
         r_both = [bank_tile(f"r_both{kb}", f"low{kb}", E) for kb in range(1, KB)]
-        da_q0 = quantise(gather(da, list_a, 0, words_tile("da_words0")), "da_q0")
-        product(r00[:], wa_block(0, 0), da_q0)
-        for kb in range(1, KB):
-            product(part(r_both[kb - 1], 0), wa_block(0, kb), da_q0)
-        scatter_all(q_tok[3], list_c, slots_of(q_last, "q_slots_last", "c_pair1"))
+        for kb in range(KB):
+            for e in range(E):
+                target = part(r_both[kb - 1], e) if kb else r_first[e][:]
+                product(target, wa_block(e, kb), columns(da_q, e * C, C))
+        scatter(q_tok[1], expert_list(list_c, 1), slots_of(q11, "q_slots11", "open_dh3")[:])
 
-        r_slots00 = slots_of(r00, "r_slots00")
-        da_q1 = quantise(gather(da, list_a, 1, words_tile("da_words1", "open_dh3")), "da_q1")
+        r_tok = [tile([P, WIDE], F32, f"r_tok{kb}") for kb in range(KB)]
+        r_slots0 = tile([P, T], F32, "r_slots0")
+        for e in range(E):
+            nc.scalar.copy(part(r_slots0, e), r_first[e][:])
+        scatter(r_tok[0], list_a[:], r_slots0[:])
         for kb in range(1, KB):
-            product(part(r_both[kb - 1], 1), wa_block(1, kb), da_q1)
-            if kb == 1:
-                product(r10[:], wa_block(1, 0), da_q1)
-        r_tok = [tile([P, WIDE if kb else T], F32, f"r_tok{kb}", None if kb else "wb_words01") for kb in range(KB)]
-        scatter(r_tok[0], list_a, 0, r_slots00[:])
-        for kb in range(1, KB):
-            scatter_all(r_tok[kb], list_a, slots_of(r_both[kb - 1], f"r_slots_both{kb}"))
-            if kb == 1:
-                scatter(r_tok[0], list_a, 1, slots_of(r10, "r_slots10")[:])
+            scatter(r_tok[kb], list_a[:], slots_of(r_both[kb - 1], f"r_slots{kb}")[:])
 
-        for kb in (1, 0, 2):
+        for kb in range(KB - 1):
             total = tile([P, T], F32, f"total{kb}")
-            nc.gpsimd.tensor_tensor(total[:], r_tok[kb][:, 0:T], q_tok[kb][:], ALU.add)
+            nc.gpsimd.tensor_tensor(total[:], r_tok[kb][:, 0:T], q_tok[kb][:, 0:T], ALU.add)
             nc.scalar.dma_start(out=out[kb * P : (kb + 1) * P, :], in_=total[:])
 
         for h in range(2):

@@ -31,6 +31,7 @@ def tile_moe_plb_relu_kernel(
     nc = tc.nc
     with ExitStack() as ctx:
         sb = ctx.enter_context(tc.tile_pool(name="sb", bufs=1))
+        reused = ctx.enter_context(tc.tile_pool(name="reused", bufs=1))
         ps = ctx.enter_context(tc.psum_pool(name="ps", bufs=1))
 
         def tile(shape, dtype, name, tag=None):
@@ -53,29 +54,33 @@ def tile_moe_plb_relu_kernel(
 
         a_planes = a.rearrange("(p t) n -> p t n", t=PACK)
         c_planes = c.rearrange("(p t) n -> p t n", t=PACK)
-        a_pairs = [tile([P, 2, T], F32, f"a_pair{u}") for u in range(2)]
+        a_low = [tile([P, T], F32, f"a_low{t}") for t in range(2)]
+        a_high = tile([P, 3, T], F32, "a_high")
+        a_sb = [a_low[0][:], a_low[1][:], a_high[:, 0, :], a_high[:, 1, :]]
         c_pairs = [tile([P, 2, T], F32, f"c_pair{u}") for u in range(2)]
-        a_sb = [a_pairs[t // 2][:, t % 2, :] for t in range(PACK)]
-        c_sb = [c_pairs[t // 2][:, t % 2, :] for t in range(PACK)]
 
         w2_raw = tile([P, 2 * H], U8, "w2_raw")
         dy_codes = tile([P, T], U32, "dy_codes")
         wa_codes = tile([P, E, 2 * K], U8, "wa_codes")
         wb_rows = [wbt[e].rearrange("(p j) k -> p j k", j=PACK) for e in range(E)]
-        wb_first = [tile([P, PACK, P], F32, f"wb_first{b}") for b in range(2)]
-        wb_raw = {(e, h): tile([P, PACK, HALF], F32, f"wb_raw{e}{h}") for e, h in ((0, 1), (1, 0), (1, 1))}
+        wb_raw = {(e, h): tile([P, PACK, HALF], F32, f"wb_raw{e}{h}") for e, h in ((0, 0), (1, 0), (0, 1))}
+        wb_raw[1, 1] = reused.tile([P, PACK, HALF], F32, name="wb_raw11", align_bytes=64, offset=0)
+
+        def load_wb(e, h):
+            nc.sync.dma_start(out=wb_raw[e, h][:], in_=wb_rows[e][:, :, h * HALF : (h + 1) * HALF])
 
         nc.sync.dma_start(list_c[:], offs2)
         nc.sync.dma_start(out=w2_raw[:].bitcast(I32), in_=w2t_words[0].bitcast(I32))
         load_scale_rows(w2_plane_raw, w2t_scales[0])
         nc.sync.dma_start(out=dy_codes[:].bitcast(I32), in_=dy_words[0].rearrange("p t d -> p (t d)").bitcast(I32))
-        nc.sync.dma_start(out=a_pairs[0][:], in_=a_planes[:, 0:2, :])
+        load_wb(0, 0)
         load_scale_rows(dy_plane, dy_scales[0])
-        nc.sync.dma_start(out=a_pairs[1][:], in_=a_planes[:, 2:4, :])
-        for b in range(2):
-            nc.sync.dma_start(out=wb_first[b][:], in_=wb_rows[0][:, :, b * P : (b + 1) * P])
-        for (e, h), raw in wb_raw.items():
-            nc.sync.dma_start(out=raw[:], in_=wb_rows[e][:, :, h * HALF : (h + 1) * HALF])
+        for t in range(2):
+            nc.sync.dma_start(out=a_sb[t], in_=a_planes[:, t, :])
+        nc.sync.dma_start(out=a_high[:, 0:2, :], in_=a_planes[:, 2:4, :])
+        load_wb(1, 0)
+        load_wb(0, 1)
+        load_wb(1, 1)
         for u in range(2):
             nc.sync.dma_start(out=c_pairs[u][:], in_=c_planes[:, 2 * u : 2 * u + 2, :])
         nc.sync.dma_start(list_a[:], offs)
@@ -112,9 +117,10 @@ def tile_moe_plb_relu_kernel(
                 nc.scalar.activation(words[:, :, t], planes[t].indirect(cut), COPY)
             return words
 
-        def quantise(values, name):
+        def quantise(values, name, codes=None):
             width = values.shape[1] // PACK
-            codes = tile([P, width], U32, name + "_codes")
+            if codes is None:
+                codes = tile([P, width], U32, name + "_codes")
             plane = tile([P, width], U8, name + "_plane")
             nc.vector.quantize_mx(codes[:].bitcast(FP8X4), plane[:], values)
             return codes, plane
@@ -125,6 +131,12 @@ def tile_moe_plb_relu_kernel(
 
         def round_on_scalar(words, raw):
             nc.scalar.copy(
+                words.rearrange("p (g i) j -> p g j i", i=4), raw.rearrange("p j (g i) -> p g j i", i=4)
+            )
+            return words
+
+        def round_on_vector(words, raw):
+            nc.vector.tensor_copy(
                 words.rearrange("p (g i) j -> p g j i", i=4), raw.rearrange("p j (g i) -> p g j i", i=4)
             )
             return words
@@ -159,60 +171,74 @@ def tile_moe_plb_relu_kernel(
         def scatter(window, cut, values):
             nc.vector.tensor_copy(window[:].indirect(cut), values)
 
-        stage = tile([P, PACK * (P + 4 * C)], BF16, "stage")
+        dc_and_stage = tile([P, PACK * (T + 4 * C)], BF16, "dc_and_stage")
+        stage = dc_and_stage[:, PACK * T :]
+        stage_first = stage[:, PACK * 3 * C :]
 
-        def staged(first, count):
-            return stage[:, PACK * first : PACK * (first + count)].rearrange("p (w j) -> p w j", j=PACK)
+        def staged(first, count, base=stage):
+            return base[:, PACK * first : PACK * (first + count)].rearrange("p (w j) -> p w j", j=PACK)
 
-        dc = [tile([P, T], BF16, f"dc{t}")[:] for t in range(PACK)]
-        open_dh = [tile([P, T], F32, f"open_dh{t}") for t in range(PACK)]
+        round_on_scalar(staged(P, P, stage_first), wb_raw[0, 0][:, :, P:HALF])
+        round_on_gpsimd(staged(0, P, stage_first), wb_raw[0, 0][:, :, 0:P])
+        wb00 = quantise(stage_first, "wb00")
+
+        dc = [dc_and_stage[:, t * T : (t + 1) * T] for t in range(PACK)]
+        dc_long = [dc_and_stage[:, t * T : PACK * T] for t in range(PACK)]
+        open_high = tile([P, 2, T], F32, "open_high")
+        open_pairs = [a_high[:, 1:3, :], open_high[:]]
 
         def mask_dh(t):
-            nc.vector.scalar_tensor_tensor(open_dh[t][:], a_sb[t], 0.0, dh[t][:], ALU.is_gt, ALU.mult)
+            nc.vector.scalar_tensor_tensor(open_pairs[t // 2][:, t % 2, :], a_sb[t], 0.0, dh[t][:], ALU.is_gt, ALU.mult)
 
         for t in range(PACK):
             nc.vector.scalar_tensor_tensor(dc[t], a_sb[t], 0.0, dh[t][:], ALU.max, ALU.mult)
             if t == 1:
-                mask_dh(0)
-        mask_dh(1)
-
-        for b in range(2):
-            round_on_gpsimd(staged(b * P, P), wb_first[b][:])
-        round_on_gpsimd(staged(4 * P, HALF), wb_raw[0, 1][:])
-        gather(dc, expert_list(list_c, 0), staged(HALF, C))
-        early = quantise(stage[:, 0 : PACK * (HALF + C)], "early")
-        dc_q0 = columns(early, HALF, C)
-        q00, q01 = [bank_tile(f"q0{kb}", f"high{kb}", 1) for kb in range(2)]
-        product(q00[:], columns(early, 0, P), dc_q0)
-        product(q01[:], columns(early, P, P), dc_q0)
-
-        gather(dc, expert_list(list_c, 1), staged(7 * P, C))
-        round_on_gpsimd(staged(P, HALF), wb_raw[1, 0][:])
-        round_on_gpsimd(staged(3 * P, P), wb_raw[1, 1][:, :, 0:P])
-        round_on_scalar(staged(6 * P, P), wb_raw[1, 1][:, :, P:HALF])
-
+                mask_dh(1)
+        mask_dh(3)
         mask_dh(2)
+
+        round_on_gpsimd(staged(HALF, HALF), wb_raw[1, 0][:])
+        gather(dc, expert_list(list_c, 0), staged(0, C))
+        wb10 = quantise(stage[:, PACK * HALF : PACK * K], "wb10")
+        dc_codes0 = tile([P, C], U32, "dc_codes0", "wb_raw10")
+        dc_q0 = columns(quantise(stage[:, 0 : PACK * C], "dc_q0", dc_codes0), 0, C)
+        q00, q01 = [bank_tile(f"q0{kb}", f"high{kb}", 1) for kb in range(2)]
+        product(q00[:], columns(wb00, 0, P), dc_q0)
+        product(q01[:], columns(wb00, P, P), dc_q0)
+
+        gather(dc_long, expert_list(list_c, 1), staged(2 * C, C))
+        outer_blocks = stage[:, 0 : PACK * 6 * P].rearrange("p (b w j) -> p b w j", b=2, j=PACK)[:, :, 0:P, :]
+        nc.gpsimd.tensor_scalar(
+            outer_blocks, wb_raw[0, 1][:].rearrange("p j (b k) -> p b k j", b=2), 1.0, 0.0, ALU.mult, ALU.add
+        )
+        round_on_gpsimd(staged(P, HALF), wb_raw[1, 1][:])
+
+        mask_dh(0)
         q_slots00 = tile([P, C], F32, "q_slots00")
         nc.vector.tensor_copy(q_slots00[:], q00[:])
-        mask_dh(3)
         q_tok = [tile([P, T if kb < 2 else WIDE], F32, f"q_tok{kb}") for kb in range(KB)]
         scatter(q_tok[0], expert_list(list_c, 0), q_slots00[:])
 
-        late = quantise(stage[:, PACK * P :], "late")
-        dc_q1 = columns(late, 6 * P, C)
+        upper = quantise(stage[:, 0 : PACK * K], "upper")
+        q_slots01 = reused.tile([P, C], F32, name="q_slots01", align_bytes=64, offset=0)
+        nc.scalar.copy(q_slots01[:], q01[:])
+        dc_codes1 = reused.tile([P, C], U32, name="dc_codes1", align_bytes=64, offset=4 * C)
+        dc_q1 = columns(quantise(stage[:, PACK * 2 * C : PACK * 3 * C], "dc_q1", dc_codes1), 0, C)
         q10, q11 = bank_tile("q10", "high0", 1), bank_tile("q11", "low0", 1)
         q_both = [bank_tile(f"q_both{kb}", f"high{kb}", E) for kb in range(2, KB)]
-        product(q10[:], columns(late, 0, P), dc_q1)
-        for u, (first0, first1) in enumerate(((3 * P, 2 * P), (4 * P, 5 * P))):
-            product(part(q_both[u], 0), columns(late, first0, P), dc_q0)
-            product(part(q_both[u], 1), columns(late, first1, P), dc_q1)
-        product(q11[:], columns(late, P, P), dc_q1)
+        product(q10[:], columns(wb10, 0, P), dc_q1)
+        for u in range(2):
+            product(part(q_both[u], 0), columns(upper, 3 * u * P, P), dc_q0)
+            product(part(q_both[u], 1), columns(upper, (1 + u) * P, P), dc_q1)
+        product(q11[:], columns(wb10, P, P), dc_q1)
 
-        da_windows = [stage[:, PACK * P + t * WIDE : PACK * P + (t + 1) * WIDE] for t in range(PACK)]
-        for t in range(PACK):
-            nc.gpsimd.tensor_tensor(da_windows[t][:, 0:T], open_dh[t][:], c_sb[t], ALU.mult)
+        da_first = PACK * C
+        da_windows = [stage[:, da_first + t * WIDE : da_first + (t + 1) * WIDE] for t in range(PACK)]
+        for u in range(2):
+            pair = stage[:, da_first + 2 * u * WIDE : da_first + 2 * (u + 1) * WIDE].rearrange("p (t w) -> p t w", t=2)
+            nc.gpsimd.tensor_tensor(pair[:, :, 0:T], open_pairs[u], c_pairs[u][:], ALU.mult)
 
-        scatter(q_tok[1], expert_list(list_c, 0), slots_of(q01, "q_slots01", "wb_raw11")[:])
+        scatter(q_tok[1], expert_list(list_c, 0), q_slots01[:])
         scatter(q_tok[0], expert_list(list_c, 1), slots_of(q10, "q_slots10")[:])
         for u in range(2):
             scatter(q_tok[2 + u], list_c[:], slots_of(q_both[u], f"q_slots_both{u}")[:])
@@ -226,7 +252,7 @@ def tile_moe_plb_relu_kernel(
             for e in range(E):
                 target = part(r_both[kb - 1], e) if kb else r_first[e][:]
                 product(target, wa_block(e, kb), columns(da_q, e * C, C))
-        scatter(q_tok[1], expert_list(list_c, 1), slots_of(q11, "q_slots11", "open_dh3")[:])
+        scatter(q_tok[1], expert_list(list_c, 1), slots_of(q11, "q_slots11", "open_high")[:])
 
         r_tok = [tile([P, WIDE], F32, f"r_tok{kb}") for kb in range(KB)]
         r_slots0 = tile([P, T], F32, "r_slots0")

@@ -171,15 +171,15 @@ def tile_moe_plb_relu_kernel(
         def scatter(window, cut, values):
             nc.vector.tensor_copy(window[:].indirect(cut), values)
 
-        dc_and_stage = tile([P, PACK * (T + 4 * C)], BF16, "dc_and_stage")
+        dc_and_stage = tile([P, PACK * (T + 9 * P)], BF16, "dc_and_stage")
         stage = dc_and_stage[:, PACK * T :]
-        stage_first = stage[:, PACK * 3 * C :]
+        stage_first = stage[:, PACK * 5 * P : PACK * 7 * P]
 
         def staged(first, count, base=stage):
             return base[:, PACK * first : PACK * (first + count)].rearrange("p (w j) -> p w j", j=PACK)
 
         round_on_scalar(staged(P, P, stage_first), wb_raw[0, 0][:, :, P:HALF])
-        round_on_gpsimd(staged(0, P, stage_first), wb_raw[0, 0][:, :, 0:P])
+        round_on_vector(staged(0, P, stage_first), wb_raw[0, 0][:, :, 0:P])
         wb00 = quantise(stage_first, "wb00")
 
         dc = [dc_and_stage[:, t * T : (t + 1) * T] for t in range(PACK)]
@@ -199,19 +199,17 @@ def tile_moe_plb_relu_kernel(
 
         round_on_gpsimd(staged(HALF, HALF), wb_raw[1, 0][:])
         gather(dc, expert_list(list_c, 0), staged(0, C))
-        wb10 = quantise(stage[:, PACK * HALF : PACK * K], "wb10")
-        dc_codes0 = tile([P, C], U32, "dc_codes0", "wb_raw10")
-        dc_q0 = columns(quantise(stage[:, 0 : PACK * C], "dc_q0", dc_codes0), 0, C)
+        dc_q0 = columns(quantise(stage[:, 0 : PACK * C], "dc_q0"), 0, C)
         q00, q01 = [bank_tile(f"q0{kb}", f"high{kb}", 1) for kb in range(2)]
         product(q00[:], columns(wb00, 0, P), dc_q0)
         product(q01[:], columns(wb00, P, P), dc_q0)
 
-        gather(dc_long, expert_list(list_c, 1), staged(2 * C, C))
-        outer_blocks = stage[:, 0 : PACK * 6 * P].rearrange("p (b w j) -> p b w j", b=2, j=PACK)[:, :, 0:P, :]
+        gather(dc_long, expert_list(list_c, 1), staged(7 * P, C))
+        round_on_gpsimd(staged(0, P), wb_raw[0, 1][:, :, 0:P])
+        apart = stage[:, PACK * P : PACK * 7 * P].rearrange("p (b w j) -> p b w j", b=2, j=PACK)[:, :, 0:P, :]
         nc.gpsimd.tensor_scalar(
-            outer_blocks, wb_raw[0, 1][:].rearrange("p j (b k) -> p b k j", b=2), 1.0, 0.0, ALU.mult, ALU.add
+            apart, wb_raw[1, 1][:].rearrange("p j (b k) -> p b k j", b=2), 1.0, 0.0, ALU.mult, ALU.add
         )
-        round_on_gpsimd(staged(P, HALF), wb_raw[1, 1][:])
 
         mask_dh(0)
         q_slots00 = tile([P, C], F32, "q_slots00")
@@ -219,26 +217,31 @@ def tile_moe_plb_relu_kernel(
         q_tok = [tile([P, T if kb < 2 else WIDE], F32, f"q_tok{kb}") for kb in range(KB)]
         scatter(q_tok[0], expert_list(list_c, 0), q_slots00[:])
 
-        upper = quantise(stage[:, 0 : PACK * K], "upper")
+        middle = quantise(stage[:, 0 : PACK * K], "middle")
         q_slots01 = reused.tile([P, C], F32, name="q_slots01", align_bytes=64, offset=0)
         nc.scalar.copy(q_slots01[:], q01[:])
         dc_codes1 = reused.tile([P, C], U32, name="dc_codes1", align_bytes=64, offset=4 * C)
-        dc_q1 = columns(quantise(stage[:, PACK * 2 * C : PACK * 3 * C], "dc_q1", dc_codes1), 0, C)
+        dc_q1 = columns(quantise(stage[:, PACK * 7 * P :], "dc_q1", dc_codes1), 0, C)
+        round_on_scalar(staged(3 * P, P), wb_raw[0, 1][:, :, P:HALF])
         q10, q11 = bank_tile("q10", "high0", 1), bank_tile("q11", "low0", 1)
         q_both = [bank_tile(f"q_both{kb}", f"high{kb}", E) for kb in range(2, KB)]
-        product(q10[:], columns(wb10, 0, P), dc_q1)
-        for u in range(2):
-            product(part(q_both[u], 0), columns(upper, 3 * u * P, P), dc_q0)
-            product(part(q_both[u], 1), columns(upper, (1 + u) * P, P), dc_q1)
-        product(q11[:], columns(wb10, P, P), dc_q1)
-
-        da_first = PACK * C
-        da_windows = [stage[:, da_first + t * WIDE : da_first + (t + 1) * WIDE] for t in range(PACK)]
-        for u in range(2):
-            pair = stage[:, da_first + 2 * u * WIDE : da_first + 2 * (u + 1) * WIDE].rearrange("p (t w) -> p t w", t=2)
-            nc.gpsimd.tensor_tensor(pair[:, :, 0:T], open_pairs[u], c_pairs[u][:], ALU.mult)
+        product(q10[:], columns(middle, HALF, P), dc_q1)
+        product(part(q_both[0], 0), columns(middle, 0, P), dc_q0)
+        product(part(q_both[0], 1), columns(middle, P, P), dc_q1)
+        product(q11[:], columns(middle, HALF + P, P), dc_q1)
 
         scatter(q_tok[1], expert_list(list_c, 0), q_slots01[:])
+        late = quantise(stage[:, PACK * 3 * P : PACK * 5 * P], "late")
+        product(part(q_both[1], 0), columns(late, 0, P), dc_q0)
+        product(part(q_both[1], 1), columns(late, P, P), dc_q1)
+
+        da_starts = [PACK * 7 * P] + [1216 + t * WIDE for t in range(3)]
+        da_windows = [stage[:, first : first + WIDE] for first in da_starts]
+        for t in range(2):
+            nc.gpsimd.tensor_tensor(da_windows[t][:, 0:T], open_pairs[0][:, t, :], c_pairs[0][:, t, :], ALU.mult)
+        pair = stage[:, da_starts[2] : da_starts[2] + 2 * WIDE].rearrange("p (t w) -> p t w", t=2)
+        nc.gpsimd.tensor_tensor(pair[:, :, 0:T], open_pairs[1], c_pairs[1][:], ALU.mult)
+
         scatter(q_tok[0], expert_list(list_c, 1), slots_of(q10, "q_slots10")[:])
         for u in range(2):
             scatter(q_tok[2 + u], list_c[:], slots_of(q_both[u], f"q_slots_both{u}")[:])

@@ -55,7 +55,7 @@ def tile_moe_plb_relu_kernel(
         a_planes = a.rearrange("(p t) n -> p t n", t=PACK)
         c_planes = c.rearrange("(p t) n -> p t n", t=PACK)
         a_low = [tile([P, T], F32, f"a_low{t}") for t in range(2)]
-        a_high = tile([P, 3, T], F32, "a_high")
+        a_high = tile([P, 2, T], F32, "a_high")
         a_sb = [a_low[0][:], a_low[1][:], a_high[:, 0, :], a_high[:, 1, :]]
         c_pairs = [tile([P, 2, T], F32, f"c_pair{u}") for u in range(2)]
 
@@ -63,7 +63,8 @@ def tile_moe_plb_relu_kernel(
         dy_codes = tile([P, T], U32, "dy_codes")
         wa_codes = tile([P, E, 2 * K], U8, "wa_codes")
         wb_rows = [wbt[e].rearrange("(p j) k -> p j k", j=PACK) for e in range(E)]
-        wb_raw = {(e, h): tile([P, PACK, HALF], F32, f"wb_raw{e}{h}") for e, h in ((0, 0), (1, 0), (0, 1))}
+        wb_raw = {(e, h): tile([P, PACK, HALF], F32, f"wb_raw{e}{h}") for e, h in ((0, 0), (0, 1))}
+        wb_raw[1, 0] = reused.tile([P, PACK, HALF], F32, name="wb_raw10", align_bytes=64, offset=16 * C)
         wb_raw[1, 1] = reused.tile([P, PACK, HALF], F32, name="wb_raw11", align_bytes=64, offset=0)
 
         def load_wb(e, h):
@@ -77,7 +78,7 @@ def tile_moe_plb_relu_kernel(
         load_scale_rows(dy_plane, dy_scales[0])
         for t in range(2):
             nc.sync.dma_start(out=a_sb[t], in_=a_planes[:, t, :])
-        nc.sync.dma_start(out=a_high[:, 0:2, :], in_=a_planes[:, 2:4, :])
+        nc.sync.dma_start(out=a_high[:], in_=a_planes[:, 2:4, :])
         load_wb(1, 0)
         load_wb(0, 1)
         load_wb(1, 1)
@@ -126,7 +127,11 @@ def tile_moe_plb_relu_kernel(
             return codes, plane
 
         def round_on_gpsimd(words, raw):
-            nc.gpsimd.tensor_scalar(words, raw.rearrange("p j k -> p k j"), 1.0, 0.0, ALU.mult, ALU.add)
+            nc.gpsimd.tensor_scalar(
+                words.rearrange("p (g i) j -> p g j i", i=4),
+                raw.rearrange("p j (g i) -> p g j i", i=4),
+                1.0, 0.0, ALU.mult, ALU.add,
+            )
             return words
 
         def round_on_scalar(words, raw):
@@ -171,83 +176,87 @@ def tile_moe_plb_relu_kernel(
         def scatter(window, cut, values):
             nc.vector.tensor_copy(window[:].indirect(cut), values)
 
-        dc_and_stage = tile([P, PACK * (T + 9 * P)], BF16, "dc_and_stage")
+        dc_and_stage = tile([P, PACK * (T + 10 * P)], BF16, "dc_and_stage")
         stage = dc_and_stage[:, PACK * T :]
-        stage_first = stage[:, PACK * 5 * P : PACK * 7 * P]
 
-        def staged(first, count, base=stage):
-            return base[:, PACK * first : PACK * (first + count)].rearrange("p (w j) -> p w j", j=PACK)
+        def staged(first, count):
+            return stage[:, PACK * first : PACK * (first + count)]
 
-        round_on_scalar(staged(P, P, stage_first), wb_raw[0, 0][:, :, P:HALF])
-        round_on_vector(staged(0, P, stage_first), wb_raw[0, 0][:, :, 0:P])
-        wb00 = quantise(stage_first, "wb00")
+        def as_words(values):
+            return values.rearrange("p (w j) -> p w j", j=PACK)
+
+        round_on_scalar(as_words(staged(8 * P, P)), wb_raw[0, 0][:, :, P:HALF])
+        round_on_vector(as_words(staged(7 * P, P)), wb_raw[0, 0][:, :, 0:P])
+        wb00 = quantise(staged(7 * P, HALF), "wb00")
+
+        mask0 = stage[:, PACK * 9 * P - 192 : PACK * 9 * P - 192 + T]
+        nc.gpsimd.tensor_scalar(mask0, a_sb[0], 0.0, None, ALU.is_gt)
 
         dc = [dc_and_stage[:, t * T : (t + 1) * T] for t in range(PACK)]
         dc_long = [dc_and_stage[:, t * T : PACK * T] for t in range(PACK)]
-        open_high = tile([P, 2, T], F32, "open_high")
-        open_pairs = [a_high[:, 1:3, :], open_high[:]]
+        open3 = tile([P, T], F32, "open3")
+        open1 = tile([P, T], F32, "open1")
 
-        def mask_dh(t):
-            nc.vector.scalar_tensor_tensor(open_pairs[t // 2][:, t % 2, :], a_sb[t], 0.0, dh[t][:], ALU.is_gt, ALU.mult)
+        def mask_dh(target, t):
+            nc.vector.scalar_tensor_tensor(target, a_sb[t], 0.0, dh[t][:], ALU.is_gt, ALU.mult)
 
         for t in range(PACK):
             nc.vector.scalar_tensor_tensor(dc[t], a_sb[t], 0.0, dh[t][:], ALU.max, ALU.mult)
             if t == 1:
-                mask_dh(1)
-        mask_dh(3)
-        mask_dh(2)
+                mask_dh(open1[:], 1)
+        mask_dh(open3[:], 3)
 
-        round_on_gpsimd(staged(HALF, HALF), wb_raw[1, 0][:])
-        gather(dc, expert_list(list_c, 0), staged(0, C))
-        dc_q0 = columns(quantise(stage[:, 0 : PACK * C], "dc_q0"), 0, C)
+        round_on_gpsimd(as_words(staged(3 * P, HALF)), wb_raw[1, 0][:])
+        gather(dc, expert_list(list_c, 0), as_words(staged(P, C)))
+        wb10 = quantise(staged(3 * P, HALF), "wb10")
+        dc_q0 = columns(quantise(staged(P, C), "dc_q0", reused.tile([P, C], U32, name="dc_codes0", align_bytes=64, offset=16 * C)), 0, C)
         q00, q01 = [bank_tile(f"q0{kb}", f"high{kb}", 1) for kb in range(2)]
         product(q00[:], columns(wb00, 0, P), dc_q0)
         product(q01[:], columns(wb00, P, P), dc_q0)
 
-        gather(dc_long, expert_list(list_c, 1), staged(7 * P, C))
-        round_on_gpsimd(staged(0, P), wb_raw[0, 1][:, :, 0:P])
-        apart = stage[:, PACK * P : PACK * 7 * P].rearrange("p (b w j) -> p b w j", b=2, j=PACK)[:, :, 0:P, :]
-        nc.gpsimd.tensor_scalar(
-            apart, wb_raw[1, 1][:].rearrange("p j (b k) -> p b k j", b=2), 1.0, 0.0, ALU.mult, ALU.add
-        )
+        gather(dc_long, expert_list(list_c, 1), as_words(staged(5 * P, C)))
+        round_on_gpsimd(as_words(staged(0, HALF)), wb_raw[0, 1][:])
+        round_on_gpsimd(as_words(staged(HALF, HALF)), wb_raw[1, 1][:])
 
-        mask_dh(0)
+        open2 = reused.tile([P, T], F32, name="open2", align_bytes=64, offset=20 * C)
+        mask_dh(open2[:], 2)
         q_slots00 = tile([P, C], F32, "q_slots00")
         nc.vector.tensor_copy(q_slots00[:], q00[:])
         q_tok = [tile([P, T if kb < 2 else WIDE], F32, f"q_tok{kb}") for kb in range(KB)]
         scatter(q_tok[0], expert_list(list_c, 0), q_slots00[:])
 
-        middle = quantise(stage[:, 0 : PACK * K], "middle")
+        upper = quantise(staged(0, K), "upper")
         q_slots01 = reused.tile([P, C], F32, name="q_slots01", align_bytes=64, offset=0)
         nc.scalar.copy(q_slots01[:], q01[:])
         dc_codes1 = reused.tile([P, C], U32, name="dc_codes1", align_bytes=64, offset=4 * C)
-        dc_q1 = columns(quantise(stage[:, PACK * 7 * P :], "dc_q1", dc_codes1), 0, C)
-        round_on_scalar(staged(3 * P, P), wb_raw[0, 1][:, :, P:HALF])
+        dc_q1 = columns(quantise(staged(5 * P, C), "dc_q1", dc_codes1), 0, C)
+        dh0_sb = reused.tile([P, T], F32, name="dh0_sb", align_bytes=64, offset=8 * C)
+        nc.scalar.copy(dh0_sb[:], dh[0][:])
         q10, q11 = bank_tile("q10", "high0", 1), bank_tile("q11", "low0", 1)
         q_both = [bank_tile(f"q_both{kb}", f"high{kb}", E) for kb in range(2, KB)]
-        product(q10[:], columns(middle, HALF, P), dc_q1)
-        product(part(q_both[0], 0), columns(middle, 0, P), dc_q0)
-        product(part(q_both[0], 1), columns(middle, P, P), dc_q1)
-        product(q11[:], columns(middle, HALF + P, P), dc_q1)
+        product(q10[:], columns(wb10, 0, P), dc_q1)
+        for u in range(2):
+            product(part(q_both[u], 0), columns(upper, u * P, P), dc_q0)
+            product(part(q_both[u], 1), columns(upper, HALF + u * P, P), dc_q1)
+        product(q11[:], columns(wb10, P, P), dc_q1)
 
         scatter(q_tok[1], expert_list(list_c, 0), q_slots01[:])
-        late = quantise(stage[:, PACK * 3 * P : PACK * 5 * P], "late")
-        product(part(q_both[1], 0), columns(late, 0, P), dc_q0)
-        product(part(q_both[1], 1), columns(late, P, P), dc_q1)
 
-        da_starts = [PACK * 7 * P] + [1216 + t * WIDE for t in range(3)]
+        da_starts = [0, 2688, 2 * WIDE, 3 * WIDE]
         da_windows = [stage[:, first : first + WIDE] for first in da_starts]
-        for t in range(2):
-            nc.gpsimd.tensor_tensor(da_windows[t][:, 0:T], open_pairs[0][:, t, :], c_pairs[0][:, t, :], ALU.mult)
-        pair = stage[:, da_starts[2] : da_starts[2] + 2 * WIDE].rearrange("p (t w) -> p t w", t=2)
-        nc.gpsimd.tensor_tensor(pair[:, :, 0:T], open_pairs[1], c_pairs[1][:], ALU.mult)
-
+        nc.gpsimd.tensor_tensor(da_windows[1][:, 0:T], open1[:], c_pairs[0][:, 1, :], ALU.mult)
+        for t, opened in ((3, open3), (2, open2)):
+            nc.gpsimd.tensor_tensor(da_windows[t][:, 0:T], opened[:], c_pairs[1][:, t - 2, :], ALU.mult)
+        open0 = stage[:, da_starts[1] + WIDE : da_starts[1] + WIDE + 2 * T].bitcast(F32)
+        nc.gpsimd.tensor_tensor(open0, dh0_sb[:], mask0, ALU.mult)
+        nc.gpsimd.tensor_tensor(da_windows[0][:, 0:T], open0, c_pairs[0][:, 0, :], ALU.mult)
         scatter(q_tok[0], expert_list(list_c, 1), slots_of(q10, "q_slots10")[:])
         for u in range(2):
             scatter(q_tok[2 + u], list_c[:], slots_of(q_both[u], f"q_slots_both{u}")[:])
 
         da_words = tile([P, T, PACK], BF16, "da_words")
-        gather(da_windows, list_a[:], da_words[:])
+        for t in (1, 3, 2, 0):
+            nc.scalar.activation(da_words[:, :, t], da_windows[t].indirect(list_a[:]), COPY)
         da_q = quantise(da_words[:].rearrange("p w j -> p (w j)"), "da_q")
         r_first = [bank_tile(f"r_first{e}", f"high{e}", 1) for e in range(E)]
         r_both = [bank_tile(f"r_both{kb}", f"low{kb}", E) for kb in range(1, KB)]
@@ -255,7 +264,7 @@ def tile_moe_plb_relu_kernel(
             for e in range(E):
                 target = part(r_both[kb - 1], e) if kb else r_first[e][:]
                 product(target, wa_block(e, kb), columns(da_q, e * C, C))
-        scatter(q_tok[1], expert_list(list_c, 1), slots_of(q11, "q_slots11", "open_high")[:])
+        scatter(q_tok[1], expert_list(list_c, 1), slots_of(q11, "q_slots11", "c_pair0")[:])
 
         r_tok = [tile([P, WIDE], F32, f"r_tok{kb}") for kb in range(KB)]
         r_slots0 = tile([P, T], F32, "r_slots0")

@@ -15,14 +15,15 @@ U8 = mybir.dt.uint8
 FP8X4 = mybir.dt.float8_e4m3fn_x4
 FP4X4 = mybir.dt.float4_e2m1fn_x4
 ALU = mybir.AluOpType
-COPY = mybir.ActivationFunctionType.Copy
+ACT = mybir.ActivationFunctionType
 
 P = 128
 PACK = 4
 KB = K // P
 HALF = K // 2
-LIST_COLS = C // 16
+PER_COL = 16
 WIDE = 704
+SHARE = 384
 
 
 def tile_moe_plb_relu_kernel(
@@ -31,14 +32,13 @@ def tile_moe_plb_relu_kernel(
     nc = tc.nc
     with ExitStack() as ctx:
         sb = ctx.enter_context(tc.tile_pool(name="sb", bufs=1))
-        reused = ctx.enter_context(tc.tile_pool(name="reused", bufs=1))
         ps = ctx.enter_context(tc.psum_pool(name="ps", bufs=1))
 
         def tile(shape, dtype, name, tag=None):
             return sb.tile(shape, dtype, name=name, tag=tag or name, align_bytes=64)
 
-        list_a = sb.tile([P, T // 16], U16, name="list_a")
-        list_c = sb.tile([P, T // 16], U16, name="list_c")
+        list_a = sb.tile([P, T // PER_COL], U16, name="list_a")
+        list_c = sb.tile([P, T // PER_COL], U16, name="list_c")
 
         w2_plane_raw = tile([P, H], U8, "w2_plane_raw")
         dy_plane = tile([P, T], U8, "dy_plane")
@@ -54,36 +54,33 @@ def tile_moe_plb_relu_kernel(
 
         a_planes = a.rearrange("(p t) n -> p t n", t=PACK)
         c_planes = c.rearrange("(p t) n -> p t n", t=PACK)
-        a_low = [tile([P, T], F32, f"a_low{t}") for t in range(2)]
-        a_high = tile([P, 2, T], F32, "a_high")
-        a_sb = [a_low[0][:], a_low[1][:], a_high[:, 0, :], a_high[:, 1, :]]
+        a_pairs = [tile([P, 2, T], F32, f"a_pair{u}") for u in range(2)]
         c_pairs = [tile([P, 2, T], F32, f"c_pair{u}") for u in range(2)]
-
         w2_raw = tile([P, 2 * H], U8, "w2_raw")
         dy_codes = tile([P, T], U32, "dy_codes")
         wa_codes = tile([P, E, 2 * K], U8, "wa_codes")
         wb_rows = [wbt[e].rearrange("(p j) k -> p j k", j=PACK) for e in range(E)]
-        wb_raw = {(e, h): tile([P, PACK, HALF], F32, f"wb_raw{e}{h}") for e, h in ((0, 0), (0, 1))}
-        wb_raw[1, 0] = reused.tile([P, PACK, HALF], F32, name="wb_raw10", align_bytes=64, offset=16 * C)
-        wb_raw[1, 1] = reused.tile([P, PACK, HALF], F32, name="wb_raw11", align_bytes=64, offset=0)
+        wb_raw = {(e, h): tile([P, PACK, HALF], F32, f"wb_raw{e}{h}") for e in range(E) for h in range(2)}
 
         def load_wb(e, h):
             nc.sync.dma_start(out=wb_raw[e, h][:], in_=wb_rows[e][:, :, h * HALF : (h + 1) * HALF])
 
-        nc.sync.dma_start(list_c[:], offs2)
+        def load_pair(pairs, planes, u):
+            nc.sync.dma_start(out=pairs[u][:], in_=planes[:, 2 * u : 2 * u + 2, :])
+
         nc.sync.dma_start(out=w2_raw[:].bitcast(I32), in_=w2t_words[0].bitcast(I32))
         load_scale_rows(w2_plane_raw, w2t_scales[0])
         nc.sync.dma_start(out=dy_codes[:].bitcast(I32), in_=dy_words[0].rearrange("p t d -> p (t d)").bitcast(I32))
-        load_wb(0, 0)
+        load_pair(a_pairs, a_planes, 0)
+        load_pair(a_pairs, a_planes, 1)
         load_scale_rows(dy_plane, dy_scales[0])
-        for t in range(2):
-            nc.sync.dma_start(out=a_sb[t], in_=a_planes[:, t, :])
-        nc.sync.dma_start(out=a_high[:], in_=a_planes[:, 2:4, :])
+        nc.sync.dma_start(list_c[:], offs2)
+        load_wb(0, 0)
+        load_pair(c_pairs, c_planes, 0)
         load_wb(1, 0)
+        load_pair(c_pairs, c_planes, 1)
         load_wb(0, 1)
         load_wb(1, 1)
-        for u in range(2):
-            nc.sync.dma_start(out=c_pairs[u][:], in_=c_planes[:, 2 * u : 2 * u + 2, :])
         nc.sync.dma_start(list_a[:], offs)
         nc.sync.dma_start(out=wa_codes[:].bitcast(I32), in_=wat_words.rearrange("e s p b -> p (e s) b").bitcast(I32))
         wa_rows = wat_scales.bitcast(I32).rearrange("e s (q r) n -> r q (e s) n", r=4)
@@ -101,48 +98,42 @@ def tile_moe_plb_relu_kernel(
             in_=w2_plane_raw[:].rearrange("p (m t) -> p t m", t=PACK),
         )
 
-        dh = [ps.tile([P, T], F32, name=f"dh{t}", tag=f"low{t}") for t in range(PACK)]
-        for t in range(PACK):
-            nc.tensor.matmul_mx(
-                out=dh[t][:],
-                lhsT=w2_codes[:, 2 * P * t : 2 * P * (t + 1)].bitcast(FP4X4),
-                lhsT_scale=w2_plane[:, P * t : P * (t + 1)],
-                rhs=dy_codes[:].bitcast(FP8X4),
-                rhs_scale=dy_plane[:],
-                start=True,
-                stop=True,
-            )
+        relu_low = tile([P, 2, T], F32, "relu_low")
+        nc.scalar.activation(relu_low[:], a_pairs[0][:], ACT.Relu)
+        positive = [tile([P, 2, T], BF16, f"mask{u}") for u in range(2)]
+        for u in range(2):
+            nc.vector.tensor_scalar(positive[u][:], a_pairs[u][:], 0.0, None, ALU.is_gt)
 
-        def gather(planes, cut, words):
-            for t in range(PACK):
-                nc.scalar.activation(words[:, :, t], planes[t].indirect(cut), COPY)
-            return words
+        dh = {}
+        for u in (1, 0):
+            for h in range(2):
+                dh[u, h] = ps.tile([P, 2, HALF], F32, name=f"dh{u}{h}", tag=f"low{u}{h}")
+                for j in range(2):
+                    t = 2 * u + j
+                    nc.tensor.matmul_mx(
+                        out=dh[u, h][:, j, :],
+                        lhsT=w2_codes[:, 2 * P * t : 2 * P * (t + 1)].bitcast(FP4X4),
+                        lhsT_scale=w2_plane[:, P * t : P * (t + 1)],
+                        rhs=dy_codes[:, h * HALF : (h + 1) * HALF].bitcast(FP8X4),
+                        rhs_scale=dy_plane[:, h * HALF : (h + 1) * HALF],
+                        start=True,
+                        stop=True,
+                    )
 
-        def quantise(values, name, codes=None):
+        def quantise(values, name):
             width = values.shape[1] // PACK
-            if codes is None:
-                codes = tile([P, width], U32, name + "_codes")
+            codes = tile([P, width], U32, name + "_codes")
             plane = tile([P, width], U8, name + "_plane")
             nc.vector.quantize_mx(codes[:].bitcast(FP8X4), plane[:], values)
             return codes, plane
 
-        def round_on_gpsimd(words, raw):
+        def flat(words):
+            return words[:].rearrange("p w j -> p (w j)")
+
+        def rounded(e, h):
+            words = tile([P, HALF, PACK], BF16, f"wb_words{e}{h}")
             nc.gpsimd.tensor_scalar(
-                words.rearrange("p (g i) j -> p g j i", i=4),
-                raw.rearrange("p j (g i) -> p g j i", i=4),
-                1.0, 0.0, ALU.mult, ALU.add,
-            )
-            return words
-
-        def round_on_scalar(words, raw):
-            nc.scalar.copy(
-                words.rearrange("p (g i) j -> p g j i", i=4), raw.rearrange("p j (g i) -> p g j i", i=4)
-            )
-            return words
-
-        def round_on_vector(words, raw):
-            nc.vector.tensor_copy(
-                words.rearrange("p (g i) j -> p g j i", i=4), raw.rearrange("p j (g i) -> p g j i", i=4)
+                words[:], wb_raw[e, h][:].rearrange("p j k -> p k j"), 1.0, 0.0, ALU.mult, ALU.add
             )
             return words
 
@@ -159,125 +150,112 @@ def tile_moe_plb_relu_kernel(
         def wa_block(e, kb):
             return wa_codes[:, e, 2 * P * kb : 2 * P * (kb + 1)].bitcast(FP4X4), wa_plane[:, e, P * kb : P * (kb + 1)]
 
-        def bank_tile(name, tag, parts):
-            return ps.tile([P, parts * C], F32, name=name, tag=tag)
+        def entries(offsets, first, count):
+            return offsets[:, first // PER_COL : (first + count) // PER_COL]
 
-        def part(bank, u):
-            return bank[:, u * C : (u + 1) * C]
+        def pair_product(words, u, factor):
+            for h in range(2):
+                cols = slice(h * HALF, (h + 1) * HALF)
+                nc.vector.tensor_tensor(
+                    words[:, cols].bitcast(BF16).rearrange("p (g i j) -> p g j i", i=4, j=2),
+                    dh[u, h][:].rearrange("p j (g i) -> p g j i", i=4),
+                    factor[:, :, cols].rearrange("p j (g i) -> p g j i", i=4),
+                    ALU.mult,
+                )
 
-        def slots_of(bank, name, tag=None):
-            slots = tile([P, bank.shape[1]], F32, name, tag)
+        def word_half(words, u):
+            return flat(words).bitcast(U32).rearrange("p (w u) -> p w u", u=2)[:, :, u]
+
+        pairs = tile([P, 3 * T], U32, "pairs")
+        dc_pair = pairs[:, 2 * T :]
+        da_pair = [pairs[:, T : 2 * T], pairs[:, 0:T]]
+        da_window = [pairs[:, T : T + WIDE], pairs[:, 0:WIDE]]
+        dc_high = tile([P, 2 * T], BF16, "dc_high")
+        for h in range(2):
+            cols = slice(h * HALF, (h + 1) * HALF)
+            nc.vector.scalar_tensor_tensor(
+                dc_high[:].rearrange("p (j n) -> p j n", j=2)[:, :, cols],
+                a_pairs[1][:, :, cols], 0.0, dh[1, h][:], ALU.max, ALU.mult,
+            )
+        pair_product(dc_pair, 0, relu_low[:])
+
+        def gather_dc(e):
+            words = tile([P, C, PACK], BF16, f"dc_words{e}")
+            cut = entries(list_c, e * C, C)
+            for j in range(2):
+                nc.scalar.activation(words[:, :, 2 + j], dc_high[:, j * T : (j + 1) * T].indirect(cut), ACT.Copy)
+            nc.vector.tensor_copy(word_half(words, 0), dc_pair.indirect(cut))
+            return words
+
+        def gated(u):
+            factor = tile([P, 2, T], F32, f"gated{u}")
+            for j in range(2):
+                nc.gpsimd.tensor_tensor(factor[:, j, :], c_pairs[u][:, j, :], positive[u][:, j, :], ALU.mult)
+            return factor
+
+        q_tok = [tile([P, T], F32, f"q_tok{kb}") for kb in range(KB)]
+
+        def q_products(e, h, weights, act):
+            bank = ps.tile([P, 2, C], F32, name=f"q{e}{h}", tag=f"high{e}{h}")
+            for u in range(2):
+                product(bank[:, u, :], columns(weights, u * P, P), act)
+            slots = tile([P, 2, C], F32, f"q_slots{e}{h}")
             nc.scalar.copy(slots[:], bank[:])
             return slots
 
-        def expert_list(offsets, e):
-            return offsets[:, e * LIST_COLS : (e + 1) * LIST_COLS]
+        def scatter_q(slots, e, kb):
+            nc.scalar.activation(q_tok[kb][:].indirect(entries(list_c, e * C, C)), slots[:, kb % 2, :], ACT.Copy)
 
-        def scatter(window, cut, values):
-            nc.vector.tensor_copy(window[:].indirect(cut), values)
-
-        dc_and_stage = tile([P, PACK * (T + 10 * P)], BF16, "dc_and_stage")
-        stage = dc_and_stage[:, PACK * T :]
-
-        def staged(first, count):
-            return stage[:, PACK * first : PACK * (first + count)]
-
-        def as_words(values):
-            return values.rearrange("p (w j) -> p w j", j=PACK)
-
-        round_on_scalar(as_words(staged(8 * P, P)), wb_raw[0, 0][:, :, P:HALF])
-        round_on_vector(as_words(staged(7 * P, P)), wb_raw[0, 0][:, :, 0:P])
-        wb00 = quantise(staged(7 * P, HALF), "wb00")
-
-        mask0 = stage[:, PACK * 9 * P - 192 : PACK * 9 * P - 192 + T]
-        nc.gpsimd.tensor_scalar(mask0, a_sb[0], 0.0, None, ALU.is_gt)
-
-        dc = [dc_and_stage[:, t * T : (t + 1) * T] for t in range(PACK)]
-        dc_long = [dc_and_stage[:, t * T : PACK * T] for t in range(PACK)]
-        open3 = tile([P, T], F32, "open3")
-        open1 = tile([P, T], F32, "open1")
-
-        def mask_dh(target, t):
-            nc.vector.scalar_tensor_tensor(target, a_sb[t], 0.0, dh[t][:], ALU.is_gt, ALU.mult)
-
-        for t in range(PACK):
-            nc.vector.scalar_tensor_tensor(dc[t], a_sb[t], 0.0, dh[t][:], ALU.max, ALU.mult)
-            if t == 1:
-                mask_dh(open1[:], 1)
-        mask_dh(open3[:], 3)
-
-        round_on_gpsimd(as_words(staged(3 * P, HALF)), wb_raw[1, 0][:])
-        gather(dc, expert_list(list_c, 0), as_words(staged(P, C)))
-        wb10 = quantise(staged(3 * P, HALF), "wb10")
-        dc_q0 = columns(quantise(staged(P, C), "dc_q0", reused.tile([P, C], U32, name="dc_codes0", align_bytes=64, offset=16 * C)), 0, C)
-        q00, q01 = [bank_tile(f"q0{kb}", f"high{kb}", 1) for kb in range(2)]
-        product(q00[:], columns(wb00, 0, P), dc_q0)
-        product(q01[:], columns(wb00, P, P), dc_q0)
-
-        gather(dc_long, expert_list(list_c, 1), as_words(staged(5 * P, C)))
-        round_on_gpsimd(as_words(staged(0, HALF)), wb_raw[0, 1][:])
-        round_on_gpsimd(as_words(staged(HALF, HALF)), wb_raw[1, 1][:])
-
-        open2 = reused.tile([P, T], F32, name="open2", align_bytes=64, offset=20 * C)
-        mask_dh(open2[:], 2)
-        q_slots00 = tile([P, C], F32, "q_slots00")
-        nc.vector.tensor_copy(q_slots00[:], q00[:])
-        q_tok = [tile([P, T if kb < 2 else WIDE], F32, f"q_tok{kb}") for kb in range(KB)]
-        scatter(q_tok[0], expert_list(list_c, 0), q_slots00[:])
-
-        upper = quantise(staged(0, K), "upper")
-        q_slots01 = reused.tile([P, C], F32, name="q_slots01", align_bytes=64, offset=0)
-        nc.scalar.copy(q_slots01[:], q01[:])
-        dc_codes1 = reused.tile([P, C], U32, name="dc_codes1", align_bytes=64, offset=4 * C)
-        dc_q1 = columns(quantise(staged(5 * P, C), "dc_q1", dc_codes1), 0, C)
-        dh0_sb = reused.tile([P, T], F32, name="dh0_sb", align_bytes=64, offset=8 * C)
-        nc.scalar.copy(dh0_sb[:], dh[0][:])
-        q10, q11 = bank_tile("q10", "high0", 1), bank_tile("q11", "low0", 1)
-        q_both = [bank_tile(f"q_both{kb}", f"high{kb}", E) for kb in range(2, KB)]
-        product(q10[:], columns(wb10, 0, P), dc_q1)
-        for u in range(2):
-            product(part(q_both[u], 0), columns(upper, u * P, P), dc_q0)
-            product(part(q_both[u], 1), columns(upper, HALF + u * P, P), dc_q1)
-        product(q11[:], columns(wb10, P, P), dc_q1)
-
-        scatter(q_tok[1], expert_list(list_c, 0), q_slots01[:])
-
-        da_starts = [0, 2688, 2 * WIDE, 3 * WIDE]
-        da_windows = [stage[:, first : first + WIDE] for first in da_starts]
-        nc.gpsimd.tensor_tensor(da_windows[1][:, 0:T], open1[:], c_pairs[0][:, 1, :], ALU.mult)
-        for t, opened in ((3, open3), (2, open2)):
-            nc.gpsimd.tensor_tensor(da_windows[t][:, 0:T], opened[:], c_pairs[1][:, t - 2, :], ALU.mult)
-        open0 = stage[:, da_starts[1] + WIDE : da_starts[1] + WIDE + 2 * T].bitcast(F32)
-        nc.gpsimd.tensor_tensor(open0, dh0_sb[:], mask0, ALU.mult)
-        nc.gpsimd.tensor_tensor(da_windows[0][:, 0:T], open0, c_pairs[0][:, 0, :], ALU.mult)
-        scatter(q_tok[0], expert_list(list_c, 1), slots_of(q10, "q_slots10")[:])
-        for u in range(2):
-            scatter(q_tok[2 + u], list_c[:], slots_of(q_both[u], f"q_slots_both{u}")[:])
+        wb00 = quantise(flat(rounded(0, 0)), "wb00")
+        dc_words0 = gather_dc(0)
+        dc_q0 = columns(quantise(flat(dc_words0), "dc_q0"), 0, C)
+        dc_words1 = gather_dc(1)
+        slots00 = q_products(0, 0, wb00, dc_q0)
+        for kb in range(2):
+            scatter_q(slots00, 0, kb)
 
         da_words = tile([P, T, PACK], BF16, "da_words")
-        for t in (1, 3, 2, 0):
-            nc.scalar.activation(da_words[:, :, t], da_windows[t].indirect(list_a[:]), COPY)
-        da_q = quantise(da_words[:].rearrange("p w j -> p (w j)"), "da_q")
-        r_first = [bank_tile(f"r_first{e}", f"high{e}", 1) for e in range(E)]
-        r_both = [bank_tile(f"r_both{kb}", f"low{kb}", E) for kb in range(1, KB)]
-        for kb in range(KB):
-            for e in range(E):
-                target = part(r_both[kb - 1], e) if kb else r_first[e][:]
-                product(target, wa_block(e, kb), columns(da_q, e * C, C))
-        scatter(q_tok[1], expert_list(list_c, 1), slots_of(q11, "q_slots11", "c_pair0")[:])
+        pair_product(da_pair[0], 0, gated(0)[:])
+        dc_q1 = columns(quantise(flat(dc_words1), "dc_q1"), 0, C)
+        wb10_words = rounded(1, 0)
+        nc.vector.tensor_copy(word_half(da_words, 0), da_window[0].indirect(list_a[:]))
+        wb10 = quantise(flat(wb10_words), "wb10")
+        slots10 = q_products(1, 0, wb10, dc_q1)
+        for kb in range(2):
+            scatter_q(slots10, 1, kb)
 
-        r_tok = [tile([P, WIDE], F32, f"r_tok{kb}") for kb in range(KB)]
-        r_slots0 = tile([P, T], F32, "r_slots0")
-        for e in range(E):
-            nc.scalar.copy(part(r_slots0, e), r_first[e][:])
-        scatter(r_tok[0], list_a[:], r_slots0[:])
-        for kb in range(1, KB):
-            scatter(r_tok[kb], list_a[:], slots_of(r_both[kb - 1], f"r_slots{kb}")[:])
+        pair_product(da_pair[1], 1, gated(1)[:])
+        wb01 = quantise(flat(rounded(0, 1)), "wb01")
+        nc.vector.tensor_copy(word_half(da_words, 1), da_window[1].indirect(list_a[:]))
+        slots01 = q_products(0, 1, wb01, dc_q0)
+        da_q = quantise(flat(da_words), "da_q")
+        wb11 = quantise(flat(rounded(1, 1)), "wb11")
+        slots11 = q_products(1, 1, wb11, dc_q1)
+        scatter_q(slots01, 0, 2)
+        scatter_q(slots01, 0, 3)
+        scatter_q(slots11, 1, 2)
+
+        r_tok = [tile([P, T if kb == 1 else WIDE], F32, f"r_tok{kb}") for kb in range(KB)]
+        r_slots = []
+        for kb in range(KB):
+            bank = ps.tile([P, E, C], F32, name=f"r{kb}", tag=f"low{1 - kb // 2}{kb % 2}")
+            for e in range(E):
+                product(bank[:, e, :], wa_block(e, kb), columns(da_q, e * C, C))
+            slots = tile([P, T], F32, f"r_slots{kb}")
+            nc.vector.tensor_copy(slots[:], bank[:].rearrange("p e s -> p (e s)"))
+            r_slots.append(slots)
+
+        nc.vector.tensor_copy(r_tok[0][:].indirect(list_a[:]), r_slots[0][:])
+        nc.vector.tensor_copy(r_tok[1][:].indirect(entries(list_a, SHARE, T - SHARE)), r_slots[1][:, SHARE:])
+        nc.scalar.activation(r_tok[1][:].indirect(entries(list_a, 0, SHARE)), r_slots[1][:, 0:SHARE], ACT.Copy)
+        scatter_q(slots11, 1, 3)
+        for kb in range(2, KB):
+            nc.vector.tensor_copy(r_tok[kb][:].indirect(list_a[:]), r_slots[kb][:])
 
         for kb in range(KB - 1):
             total = tile([P, T], F32, f"total{kb}")
-            nc.gpsimd.tensor_tensor(total[:], r_tok[kb][:, 0:T], q_tok[kb][:, 0:T], ALU.add)
-            nc.scalar.dma_start(out=out[kb * P : (kb + 1) * P, :], in_=total[:])
+            nc.gpsimd.tensor_tensor(total[:], r_tok[kb][:, 0:T], q_tok[kb][:], ALU.add)
+            nc.sync.dma_start(out=out[kb * P : (kb + 1) * P, :], in_=total[:])
 
         for h in range(2):
             cols = slice(h * HALF, (h + 1) * HALF)

@@ -1,3 +1,4 @@
+import math
 from contextlib import ExitStack
 
 import concourse.mybir as mybir
@@ -23,7 +24,7 @@ KB = K // P
 HALF = K // 2
 PER_COL = 16
 WIDE = 704
-SHARE = 384
+SHARE = 192
 
 
 def tile_moe_plb_relu_kernel(
@@ -71,13 +72,13 @@ def tile_moe_plb_relu_kernel(
         nc.sync.dma_start(out=w2_raw[:].bitcast(I32), in_=w2t_words[0].bitcast(I32))
         load_scale_rows(w2_plane_raw, w2t_scales[0])
         nc.sync.dma_start(out=dy_codes[:].bitcast(I32), in_=dy_words[0].rearrange("p t d -> p (t d)").bitcast(I32))
-        load_pair(a_pairs, a_planes, 0)
         load_pair(a_pairs, a_planes, 1)
-        load_scale_rows(dy_plane, dy_scales[0])
         nc.sync.dma_start(list_c[:], offs2)
+        load_scale_rows(dy_plane, dy_scales[0])
+        load_pair(a_pairs, a_planes, 0)
         load_wb(0, 0)
-        load_pair(c_pairs, c_planes, 0)
         load_wb(1, 0)
+        load_pair(c_pairs, c_planes, 0)
         load_pair(c_pairs, c_planes, 1)
         load_wb(0, 1)
         load_wb(1, 1)
@@ -99,10 +100,9 @@ def tile_moe_plb_relu_kernel(
         )
 
         relu_low = tile([P, 2, T], F32, "relu_low")
-        nc.scalar.activation(relu_low[:], a_pairs[0][:], ACT.Relu)
-        positive = [tile([P, 2, T], BF16, f"mask{u}") for u in range(2)]
-        for u in range(2):
-            nc.vector.tensor_scalar(positive[u][:], a_pairs[u][:], 0.0, None, ALU.is_gt)
+        for h in range(2):
+            cols = slice(h * HALF, (h + 1) * HALF)
+            nc.gpsimd.tensor_scalar(relu_low[:, :, cols], a_pairs[0][:, :, cols], math.inf, 0.0, ALU.min, ALU.max)
 
         dh = {}
         for u in (1, 0):
@@ -128,14 +128,12 @@ def tile_moe_plb_relu_kernel(
             return codes, plane
 
         def flat(words):
-            return words[:].rearrange("p w j -> p (w j)")
+            return words.rearrange("p w j -> p (w j)")
 
-        def rounded(e, h):
-            words = tile([P, HALF, PACK], BF16, f"wb_words{e}{h}")
-            nc.gpsimd.tensor_scalar(
-                words[:], wb_raw[e, h][:].rearrange("p j k -> p k j"), 1.0, 0.0, ALU.mult, ALU.add
+        def round_wb(words, e, h):
+            nc.vector.tensor_copy(
+                words.rearrange("p (g i) j -> p g j i", i=4), wb_raw[e, h][:].rearrange("p j (g i) -> p g j i", i=4)
             )
-            return words
 
         def columns(quantised, first, count):
             codes, plane = quantised
@@ -171,91 +169,101 @@ def tile_moe_plb_relu_kernel(
         da_pair = [pairs[:, T : 2 * T], pairs[:, 0:T]]
         da_window = [pairs[:, T : T + WIDE], pairs[:, 0:WIDE]]
         dc_high = tile([P, 2 * T], BF16, "dc_high")
-        for h in range(2):
-            cols = slice(h * HALF, (h + 1) * HALF)
-            nc.vector.scalar_tensor_tensor(
-                dc_high[:].rearrange("p (j n) -> p j n", j=2)[:, :, cols],
-                a_pairs[1][:, :, cols], 0.0, dh[1, h][:], ALU.max, ALU.mult,
-            )
+        for j in range(2):
+            for h in range(2):
+                first = j * T + h * HALF
+                nc.vector.scalar_tensor_tensor(
+                    dc_high[:, first : first + HALF], a_pairs[1][:, j, h * HALF : (h + 1) * HALF], 0.0,
+                    dh[1, h][:, j, :], ALU.max, ALU.mult,
+                )
         pair_product(dc_pair, 0, relu_low[:])
 
-        def gather_dc(e):
-            words = tile([P, C, PACK], BF16, f"dc_words{e}")
+        def gather_dc(words, e):
             cut = entries(list_c, e * C, C)
             for j in range(2):
                 nc.scalar.activation(words[:, :, 2 + j], dc_high[:, j * T : (j + 1) * T].indirect(cut), ACT.Copy)
             nc.vector.tensor_copy(word_half(words, 0), dc_pair.indirect(cut))
-            return words
 
         def gated(u):
             factor = tile([P, 2, T], F32, f"gated{u}")
-            for j in range(2):
-                nc.gpsimd.tensor_tensor(factor[:, j, :], c_pairs[u][:, j, :], positive[u][:, j, :], ALU.mult)
+            nc.vector.scalar_tensor_tensor(factor[:], a_pairs[u][:], 0.0, c_pairs[u][:], ALU.is_gt, ALU.mult)
             return factor
 
         q_tok = [tile([P, T], F32, f"q_tok{kb}") for kb in range(KB)]
 
-        def q_products(e, h, weights, act):
-            bank = ps.tile([P, 2, C], F32, name=f"q{e}{h}", tag=f"high{e}{h}")
-            for u in range(2):
-                product(bank[:, u, :], columns(weights, u * P, P), act)
-            slots = tile([P, 2, C], F32, f"q_slots{e}{h}")
+        def q_bank(name, tag, weights, act):
+            bank = ps.tile([P, len(weights) * C], F32, name=name, tag=tag)
+            for u, block in enumerate(weights):
+                product(bank[:, u * C : (u + 1) * C], block, act)
+            slots = tile([P, len(weights) * C], F32, name + "_slots")
             nc.scalar.copy(slots[:], bank[:])
             return slots
 
-        def scatter_q(slots, e, kb):
-            nc.scalar.activation(q_tok[kb][:].indirect(entries(list_c, e * C, C)), slots[:, kb % 2, :], ACT.Copy)
+        def scatter_on_scalar(window, offsets, first, values):
+            nc.scalar.activation(window[:].indirect(entries(offsets, first, values.shape[1])), values, ACT.Copy)
 
-        wb00 = quantise(flat(rounded(0, 0)), "wb00")
-        dc_words0 = gather_dc(0)
-        dc_q0 = columns(quantise(flat(dc_words0), "dc_q0"), 0, C)
-        dc_words1 = gather_dc(1)
-        slots00 = q_products(0, 0, wb00, dc_q0)
-        for kb in range(2):
-            scatter_q(slots00, 0, kb)
+        def scatter_on_vector(window, offsets, first, values):
+            nc.vector.tensor_copy(window[:].indirect(entries(offsets, first, values.shape[1])), values)
 
+        dc_q = []
+        for e in range(E):
+            staged = tile([P, C + HALF, PACK], BF16, f"staged{e}")
+            round_wb(staged[:, C:, :], e, 0)
+            gather_dc(staged[:, 0:C, :], e)
+            both = quantise(flat(staged[:]), f"lower{e}")
+            dc_q.append(columns(both, 0, C))
+            slots = q_bank(f"q_lower{e}", f"high{e}", [columns(both, C + u * P, P) for u in range(2)], dc_q[e])
+            for kb in range(2):
+                scatter_on_scalar(q_tok[kb], list_c, e * C, slots[:, kb * C : (kb + 1) * C])
+
+        factors = [gated(u) for u in range(2)]
+        wb01_words = tile([P, HALF, PACK], BF16, "wb01_words")
+        round_wb(wb01_words[:], 0, 1)
+        pair_product(da_pair[0], 0, factors[0][:])
+        wb01 = quantise(flat(wb01_words[:]), "wb01")
+        slots01 = q_bank("q01", "high2", [columns(wb01, u * P, P) for u in range(2)], dc_q[0])
+        pair_product(da_pair[1], 1, factors[1][:])
         da_words = tile([P, T, PACK], BF16, "da_words")
-        pair_product(da_pair[0], 0, gated(0)[:])
-        dc_q1 = columns(quantise(flat(dc_words1), "dc_q1"), 0, C)
-        wb10_words = rounded(1, 0)
-        nc.vector.tensor_copy(word_half(da_words, 0), da_window[0].indirect(list_a[:]))
-        wb10 = quantise(flat(wb10_words), "wb10")
-        slots10 = q_products(1, 0, wb10, dc_q1)
-        for kb in range(2):
-            scatter_q(slots10, 1, kb)
+        for u in range(2):
+            nc.vector.tensor_copy(word_half(da_words[:], u), da_window[u].indirect(list_a[:]))
+        wb11_words = tile([P, HALF, PACK], BF16, "wb11_words")
+        round_wb(wb11_words[:], 1, 1)
+        da_q = quantise(flat(da_words[:]), "da_q")
+        wb11 = quantise(flat(wb11_words[:]), "wb11")
+        slots12 = q_bank("q12", "high3", [columns(wb11, 0, P)], dc_q[1])
+        for u in range(2):
+            scatter_on_scalar(q_tok[2 + u], list_c, 0, slots01[:, u * C : (u + 1) * C])
+        scatter_on_scalar(q_tok[2], list_c, C, slots12[:])
 
-        pair_product(da_pair[1], 1, gated(1)[:])
-        wb01 = quantise(flat(rounded(0, 1)), "wb01")
-        nc.vector.tensor_copy(word_half(da_words, 1), da_window[1].indirect(list_a[:]))
-        slots01 = q_products(0, 1, wb01, dc_q0)
-        da_q = quantise(flat(da_words), "da_q")
-        wb11 = quantise(flat(rounded(1, 1)), "wb11")
-        slots11 = q_products(1, 1, wb11, dc_q1)
-        scatter_q(slots01, 0, 2)
-        scatter_q(slots01, 0, 3)
-        scatter_q(slots11, 1, 2)
+        r_tok = [tile([P, WIDE if kb in (0, 3) else T], F32, f"r_tok{kb}") for kb in range(KB)]
 
-        r_tok = [tile([P, T if kb == 1 else WIDE], F32, f"r_tok{kb}") for kb in range(KB)]
-        r_slots = []
-        for kb in range(KB):
-            bank = ps.tile([P, E, C], F32, name=f"r{kb}", tag=f"low{1 - kb // 2}{kb % 2}")
+        def r_bank(kb, engine_copy):
+            bank = ps.tile([P, T], F32, name=f"r{kb}", tag=f"low{kb // 2}{kb % 2}")
             for e in range(E):
-                product(bank[:, e, :], wa_block(e, kb), columns(da_q, e * C, C))
+                product(bank[:, e * C : (e + 1) * C], wa_block(e, kb), columns(da_q, e * C, C))
             slots = tile([P, T], F32, f"r_slots{kb}")
-            nc.vector.tensor_copy(slots[:], bank[:].rearrange("p e s -> p (e s)"))
-            r_slots.append(slots)
+            engine_copy(slots[:], bank[:])
+            return slots
 
-        nc.vector.tensor_copy(r_tok[0][:].indirect(list_a[:]), r_slots[0][:])
-        nc.vector.tensor_copy(r_tok[1][:].indirect(entries(list_a, SHARE, T - SHARE)), r_slots[1][:, SHARE:])
-        nc.scalar.activation(r_tok[1][:].indirect(entries(list_a, 0, SHARE)), r_slots[1][:, 0:SHARE], ACT.Copy)
-        scatter_q(slots11, 1, 3)
-        for kb in range(2, KB):
-            nc.vector.tensor_copy(r_tok[kb][:].indirect(list_a[:]), r_slots[kb][:])
+        r_slots0 = r_bank(0, nc.vector.tensor_copy)
+        r_slots1 = r_bank(1, nc.vector.tensor_copy)
+        scatter_on_scalar(r_tok[1], list_a, 0, r_slots1[:, 0:SHARE])
+        r_slots2 = r_bank(2, nc.scalar.copy)
+        r_slots3 = r_bank(3, nc.vector.tensor_copy)
+        scatter_on_vector(r_tok[0], list_a, 0, r_slots0[:])
+        scatter_on_vector(r_tok[1], list_a, SHARE, r_slots1[:, SHARE:])
+        scatter_on_vector(r_tok[3], list_a, 0, r_slots3[:])
+        for e in range(E):
+            scatter_on_scalar(r_tok[2], list_a, e * C, r_slots2[:, e * C : (e + 1) * C])
+        slots13 = q_bank("q13", "low10", [columns(wb11, P, P)], dc_q[1])
+        scatter_on_scalar(q_tok[3], list_c, C, slots13[:])
 
+        before = None
         for kb in range(KB - 1):
-            total = tile([P, T], F32, f"total{kb}")
+            total = tile([P, T], F32, f"total{kb}", before)
             nc.gpsimd.tensor_tensor(total[:], r_tok[kb][:, 0:T], q_tok[kb][:], ALU.add)
             nc.sync.dma_start(out=out[kb * P : (kb + 1) * P, :], in_=total[:])
+            before = f"r_tok{kb}"
 
         for h in range(2):
             cols = slice(h * HALF, (h + 1) * HALF)

@@ -24,7 +24,6 @@ KB = K // P
 HALF = K // 2
 PER_COL = 16
 WIDE = 704
-SHARE = 192
 
 
 def tile_moe_plb_relu_kernel(
@@ -56,7 +55,11 @@ def tile_moe_plb_relu_kernel(
         a_planes = a.rearrange("(p t) n -> p t n", t=PACK)
         c_planes = c.rearrange("(p t) n -> p t n", t=PACK)
         a_pairs = [tile([P, 2, T], F32, f"a_pair{u}") for u in range(2)]
-        c_pairs = [tile([P, 2, T], F32, f"c_pair{u}") for u in range(2)]
+        a_views = [pair[:] for pair in a_pairs]
+        c_low = tile([P, 2, T], F32, "c_low")
+        c_high_zone = tile([P, 4 * T], BF16, "c_high_zone")
+        c_high = c_high_zone[:].bitcast(F32).rearrange("p (j n) -> p j n", j=2)
+        c_pairs = [c_low[:], c_high]
         w2_raw = tile([P, 2 * H], U8, "w2_raw")
         dy_codes = tile([P, T], U32, "dy_codes")
         wa_codes = tile([P, E, 2 * K], U8, "wa_codes")
@@ -67,15 +70,15 @@ def tile_moe_plb_relu_kernel(
             nc.sync.dma_start(out=wb_raw[e, h][:], in_=wb_rows[e][:, :, h * HALF : (h + 1) * HALF])
 
         def load_pair(pairs, planes, u):
-            nc.sync.dma_start(out=pairs[u][:], in_=planes[:, 2 * u : 2 * u + 2, :])
+            nc.sync.dma_start(out=pairs[u], in_=planes[:, 2 * u : 2 * u + 2, :])
 
         nc.sync.dma_start(out=w2_raw[:].bitcast(I32), in_=w2t_words[0].bitcast(I32))
         load_scale_rows(w2_plane_raw, w2t_scales[0])
         nc.sync.dma_start(out=dy_codes[:].bitcast(I32), in_=dy_words[0].rearrange("p t d -> p (t d)").bitcast(I32))
-        load_pair(a_pairs, a_planes, 1)
+        load_pair(a_views, a_planes, 1)
         nc.sync.dma_start(list_c[:], offs2)
         load_scale_rows(dy_plane, dy_scales[0])
-        load_pair(a_pairs, a_planes, 0)
+        load_pair(a_views, a_planes, 0)
         load_wb(0, 0)
         load_wb(1, 0)
         load_pair(c_pairs, c_planes, 0)
@@ -104,21 +107,24 @@ def tile_moe_plb_relu_kernel(
             cols = slice(h * HALF, (h + 1) * HALF)
             nc.gpsimd.tensor_scalar(relu_low[:, :, cols], a_pairs[0][:, :, cols], math.inf, 0.0, ALU.min, ALU.max)
 
+        def dh_product(target, t, cols):
+            nc.tensor.matmul_mx(
+                out=target,
+                lhsT=w2_codes[:, 2 * P * t : 2 * P * (t + 1)].bitcast(FP4X4),
+                lhsT_scale=w2_plane[:, P * t : P * (t + 1)],
+                rhs=dy_codes[:, cols].bitcast(FP8X4),
+                rhs_scale=dy_plane[:, cols],
+                start=True,
+                stop=True,
+            )
+
+        halves = [slice(h * HALF, (h + 1) * HALF) for h in range(2)]
         dh = {}
         for u in (1, 0):
             for h in range(2):
-                dh[u, h] = ps.tile([P, 2, HALF], F32, name=f"dh{u}{h}", tag=f"low{u}{h}")
+                dh[u, h] = ps.tile([P, 2, HALF], F32, name=f"dh{u}{h}", tag=f"low{2 * u + h}")
                 for j in range(2):
-                    t = 2 * u + j
-                    nc.tensor.matmul_mx(
-                        out=dh[u, h][:, j, :],
-                        lhsT=w2_codes[:, 2 * P * t : 2 * P * (t + 1)].bitcast(FP4X4),
-                        lhsT_scale=w2_plane[:, P * t : P * (t + 1)],
-                        rhs=dy_codes[:, h * HALF : (h + 1) * HALF].bitcast(FP8X4),
-                        rhs_scale=dy_plane[:, h * HALF : (h + 1) * HALF],
-                        start=True,
-                        stop=True,
-                    )
+                    dh_product(dh[u, h][:, j, :], 2 * u + j, halves[h])
 
         def quantise(values, name):
             width = values.shape[1] // PACK
@@ -130,9 +136,15 @@ def tile_moe_plb_relu_kernel(
         def flat(words):
             return words.rearrange("p w j -> p (w j)")
 
-        def round_wb(words, e, h):
-            nc.vector.tensor_copy(
-                words.rearrange("p (g i) j -> p g j i", i=4), wb_raw[e, h][:].rearrange("p j (g i) -> p g j i", i=4)
+        def round_wb(engine_copy, words, raw):
+            engine_copy(
+                words.rearrange("p (g i j) -> p g j i", i=4, j=PACK), raw.rearrange("p j (g i) -> p g j i", i=4)
+            )
+
+        def round_on_gpsimd(words, raw):
+            nc.gpsimd.tensor_scalar(
+                words.rearrange("p (k j) -> p k j", j=PACK), raw.rearrange("p j k -> p k j"),
+                1.0, 0.0, ALU.mult, ALU.add,
             )
 
         def columns(quantised, first, count):
@@ -151,52 +163,49 @@ def tile_moe_plb_relu_kernel(
         def entries(offsets, first, count):
             return offsets[:, first // PER_COL : (first + count) // PER_COL]
 
-        def pair_product(words, u, factor):
-            for h in range(2):
-                cols = slice(h * HALF, (h + 1) * HALF)
-                nc.vector.tensor_tensor(
-                    words[:, cols].bitcast(BF16).rearrange("p (g i j) -> p g j i", i=4, j=2),
-                    dh[u, h][:].rearrange("p j (g i) -> p g j i", i=4),
-                    factor[:, :, cols].rearrange("p j (g i) -> p g j i", i=4),
-                    ALU.mult,
-                )
-
         def word_half(words, u):
             return flat(words).bitcast(U32).rearrange("p (w u) -> p w u", u=2)[:, :, u]
 
-        pairs = tile([P, 3 * T], U32, "pairs")
-        dc_pair = pairs[:, 2 * T :]
-        da_pair = [pairs[:, T : 2 * T], pairs[:, 0:T]]
-        da_window = [pairs[:, T : T + WIDE], pairs[:, 0:WIDE]]
+        def as_words(values):
+            return values.rearrange("p (w j) -> p w j", j=PACK)
+
+        def pair_product(words, u, factor):
+            for h in range(2):
+                nc.vector.tensor_tensor(
+                    words[:, halves[h]].bitcast(BF16).rearrange("p (g i j) -> p g j i", i=4, j=2),
+                    dh[u, h][:].rearrange("p j (g i) -> p g j i", i=4),
+                    factor[:, :, halves[h]].rearrange("p j (g i) -> p g j i", i=4),
+                    ALU.mult,
+                )
+
         dc_high = tile([P, 2 * T], BF16, "dc_high")
         for j in range(2):
             for h in range(2):
                 first = j * T + h * HALF
                 nc.vector.scalar_tensor_tensor(
-                    dc_high[:, first : first + HALF], a_pairs[1][:, j, h * HALF : (h + 1) * HALF], 0.0,
+                    dc_high[:, first : first + HALF], a_pairs[1][:, j, halves[h]], 0.0,
                     dh[1, h][:, j, :], ALU.max, ALU.mult,
                 )
+        pairs = tile([P, 4 * T], U32, "pairs")
+        dc_pair = pairs[:, 2 * T : 3 * T]
+        wb00_words = pairs[:, 3 * T :].bitcast(BF16)
         pair_product(dc_pair, 0, relu_low[:])
 
-        def gather_dc(words, e):
+        def gather_dc(words, e, window):
             cut = entries(list_c, e * C, C)
             for j in range(2):
                 nc.scalar.activation(words[:, :, 2 + j], dc_high[:, j * T : (j + 1) * T].indirect(cut), ACT.Copy)
-            nc.vector.tensor_copy(word_half(words, 0), dc_pair.indirect(cut))
-
-        def gated(u):
-            factor = tile([P, 2, T], F32, f"gated{u}")
-            nc.vector.scalar_tensor_tensor(factor[:], a_pairs[u][:], 0.0, c_pairs[u][:], ALU.is_gt, ALU.mult)
-            return factor
+            nc.vector.tensor_copy(word_half(words, 0), window.indirect(cut))
 
         q_tok = [tile([P, T], F32, f"q_tok{kb}") for kb in range(KB)]
 
-        def q_bank(name, tag, weights, act):
-            bank = ps.tile([P, len(weights) * C], F32, name=name, tag=tag)
+        def q_bank(name, tag, weights, act, engine_copy=nc.scalar.copy, slots_tag=None):
+            count = act[1].shape[1]
+            bank = ps.tile([P, len(weights) * count], F32, name=name, tag=tag)
             for u, block in enumerate(weights):
-                product(bank[:, u * C : (u + 1) * C], block, act)
-            slots = tile([P, len(weights) * C], F32, name + "_slots")
-            nc.scalar.copy(slots[:], bank[:])
+                product(bank[:, u * count : (u + 1) * count], block, act)
+            slots = tile([P, len(weights) * count], F32, name + "_slots", slots_tag)
+            engine_copy(slots[:], bank[:])
             return slots
 
         def scatter_on_scalar(window, offsets, first, values):
@@ -205,61 +214,77 @@ def tile_moe_plb_relu_kernel(
         def scatter_on_vector(window, offsets, first, values):
             nc.vector.tensor_copy(window[:].indirect(entries(offsets, first, values.shape[1])), values)
 
-        dc_q = []
-        for e in range(E):
-            staged = tile([P, C + HALF, PACK], BF16, f"staged{e}")
-            round_wb(staged[:, C:, :], e, 0)
-            gather_dc(staged[:, 0:C, :], e)
-            both = quantise(flat(staged[:]), f"lower{e}")
-            dc_q.append(columns(both, 0, C))
-            slots = q_bank(f"q_lower{e}", f"high{e}", [columns(both, C + u * P, P) for u in range(2)], dc_q[e])
-            for kb in range(2):
-                scatter_on_scalar(q_tok[kb], list_c, e * C, slots[:, kb * C : (kb + 1) * C])
+        dc_words0 = tile([P, C, PACK], BF16, "dc_words0")
+        round_wb(nc.vector.tensor_copy, wb00_words, wb_raw[0, 0][:])
+        gather_dc(dc_words0[:], 0, dc_pair)
+        wb00 = quantise(wb00_words, "wb00")
+        dc_q0 = columns(quantise(flat(dc_words0[:]), "dc_q0"), 0, C)
+        slots00 = q_bank("q00", "high0", [columns(wb00, u * P, P) for u in range(2)], dc_q0)
+        lower1_words = tile([P, (C + HALF) * PACK], BF16, "lower1_words")
+        gather_dc(as_words(lower1_words[:, 0 : C * PACK]), 1, pairs[:, 2 * T :])
+        round_wb(nc.scalar.copy, lower1_words[:, C * PACK :], wb_raw[1, 0][:])
+        for kb in range(2):
+            scatter_on_scalar(q_tok[kb], list_c, 0, slots00[:, kb * C : (kb + 1) * C])
 
-        factors = [gated(u) for u in range(2)]
-        wb01_words = tile([P, HALF, PACK], BF16, "wb01_words")
-        round_wb(wb01_words[:], 0, 1)
-        pair_product(da_pair[0], 0, factors[0][:])
-        wb01 = quantise(flat(wb01_words[:]), "wb01")
-        slots01 = q_bank("q01", "high2", [columns(wb01, u * P, P) for u in range(2)], dc_q[0])
-        pair_product(da_pair[1], 1, factors[1][:])
-        da_words = tile([P, T, PACK], BF16, "da_words")
-        for u in range(2):
-            nc.vector.tensor_copy(word_half(da_words[:], u), da_window[u].indirect(list_a[:]))
-        wb11_words = tile([P, HALF, PACK], BF16, "wb11_words")
-        round_wb(wb11_words[:], 1, 1)
-        da_q = quantise(flat(da_words[:]), "da_q")
-        wb11 = quantise(flat(wb11_words[:]), "wb11")
-        slots12 = q_bank("q12", "high3", [columns(wb11, 0, P)], dc_q[1])
+        gated = [tile([P, 2, T], F32, f"gated{u}") for u in range(2)]
+        nc.vector.scalar_tensor_tensor(gated[0][:], a_pairs[0][:], 0.0, c_pairs[0], ALU.is_gt, ALU.mult)
+        lower1 = quantise(lower1_words[:], "lower1")
+        dc_q1 = columns(lower1, 0, C)
+        slots10 = q_bank("q10", "high1", [columns(lower1, C + u * P, P) for u in range(2)], dc_q1)
+        for kb in range(2):
+            scatter_on_scalar(q_tok[kb], list_c, C, slots10[:, kb * C : (kb + 1) * C])
+
+        upper_words = c_high_zone[:, 0 : 3 * P * PACK]
+        nc.vector.scalar_tensor_tensor(gated[1][:], a_pairs[1][:], 0.0, c_pairs[1], ALU.is_gt, ALU.mult)
+        round_on_gpsimd(upper_words[:, 0 : HALF * PACK], wb_raw[0, 1][:])
+        round_on_gpsimd(upper_words[:, HALF * PACK :], wb_raw[1, 1][:, :, 0:P])
+        pair_product(pairs[:, T : 2 * T], 0, gated[0][:])
+        pair_product(pairs[:, 0:T], 1, gated[1][:])
+        upper = quantise(upper_words, "upper")
+        slots01 = q_bank("q01", "high2", [columns(upper, u * P, P) for u in range(2)], dc_q0)
         for u in range(2):
             scatter_on_scalar(q_tok[2 + u], list_c, 0, slots01[:, u * C : (u + 1) * C])
-        scatter_on_scalar(q_tok[2], list_c, C, slots12[:])
+
+        picked = tile([P, 2 * T], U32, "picked")
+        for u in range(2):
+            first = (1 - u) * T
+            nc.vector.tensor_copy(picked[:, u * T : (u + 1) * T], pairs[:, first : first + WIDE].indirect(list_a[:]))
+        last_words = pairs[:, T + HALF : 2 * T].bitcast(BF16)
+        round_wb(nc.vector.tensor_copy, last_words, wb_raw[1, 1][:, :, P:HALF])
+        da_words = tile([P, 2 * T], U32, "da_words")
+        nc.vector.tensor_copy(
+            da_words[:].bitcast(I32).rearrange("p (g i u) -> p g u i", i=4, u=2),
+            picked[:].bitcast(I32).rearrange("p (u g i) -> p g u i", i=4, u=2),
+        )
+        wb13 = quantise(last_words, "wb13")
+        da_q = quantise(da_words[:].bitcast(BF16), "da_q")
+        slots12 = q_bank("q12", "high3", [columns(upper, C, P)], dc_q1, nc.vector.tensor_copy, "da_words")
+        scatter_on_vector(q_tok[2], list_c, C, slots12[:])
 
         r_tok = [tile([P, WIDE if kb in (0, 3) else T], F32, f"r_tok{kb}") for kb in range(KB)]
 
         def r_bank(kb, engine_copy):
-            bank = ps.tile([P, T], F32, name=f"r{kb}", tag=f"low{kb // 2}{kb % 2}")
+            bank = ps.tile([P, T], F32, name=f"r{kb}", tag=f"low{kb}")
             for e in range(E):
                 product(bank[:, e * C : (e + 1) * C], wa_block(e, kb), columns(da_q, e * C, C))
             slots = tile([P, T], F32, f"r_slots{kb}")
             engine_copy(slots[:], bank[:])
             return slots
 
+        r_slots1 = r_bank(1, nc.scalar.copy)
         r_slots0 = r_bank(0, nc.vector.tensor_copy)
-        r_slots1 = r_bank(1, nc.vector.tensor_copy)
-        scatter_on_scalar(r_tok[1], list_a, 0, r_slots1[:, 0:SHARE])
-        r_slots2 = r_bank(2, nc.scalar.copy)
+        r_slots2 = r_bank(2, nc.vector.tensor_copy)
         r_slots3 = r_bank(3, nc.vector.tensor_copy)
         scatter_on_vector(r_tok[0], list_a, 0, r_slots0[:])
-        scatter_on_vector(r_tok[1], list_a, SHARE, r_slots1[:, SHARE:])
         scatter_on_vector(r_tok[3], list_a, 0, r_slots3[:])
         for e in range(E):
-            scatter_on_scalar(r_tok[2], list_a, e * C, r_slots2[:, e * C : (e + 1) * C])
-        slots13 = q_bank("q13", "low10", [columns(wb11, P, P)], dc_q[1])
+            for kb, slots in ((1, r_slots1), (2, r_slots2)):
+                scatter_on_scalar(r_tok[kb], list_a, e * C, slots[:, e * C : (e + 1) * C])
+        slots13 = q_bank("q13", "low3", [columns(wb13, 0, P)], dc_q1)
         scatter_on_scalar(q_tok[3], list_c, C, slots13[:])
 
         before = None
-        for kb in range(KB - 1):
+        for kb in (1, 0, 2):
             total = tile([P, T], F32, f"total{kb}", before)
             nc.gpsimd.tensor_tensor(total[:], r_tok[kb][:, 0:T], q_tok[kb][:], ALU.add)
             nc.sync.dma_start(out=out[kb * P : (kb + 1) * P, :], in_=total[:])
@@ -269,4 +294,4 @@ def tile_moe_plb_relu_kernel(
             cols = slice(h * HALF, (h + 1) * HALF)
             last = tile([P, HALF], F32, f"last{h}")
             nc.vector.tensor_tensor(last[:], r_tok[3][:, cols], q_tok[3][:, cols], ALU.add)
-            nc.sync.dma_start(out=out[3 * P : 4 * P, cols], in_=last[:])
+            nc.scalar.dma_start(out=out[3 * P : 4 * P, cols], in_=last[:])

@@ -178,7 +178,8 @@ def tile_moe_plb_relu_kernel(
                     ALU.mult,
                 )
 
-        dc_high = tile([P, 2 * T], BF16, "dc_high")
+        dc_high = tile([P, 2 * T + (HALF + C) * PACK], BF16, "dc_high")
+        lower0_words = dc_high[:, 2 * T :]
         for j in range(2):
             for h in range(2):
                 first = j * T + h * HALF
@@ -186,26 +187,26 @@ def tile_moe_plb_relu_kernel(
                     dc_high[:, first : first + HALF], a_pairs[1][:, j, halves[h]], 0.0,
                     dh[1, h][:, j, :], ALU.max, ALU.mult,
                 )
-        pairs = tile([P, 4 * T], U32, "pairs")
-        dc_pair = pairs[:, 2 * T : 3 * T]
-        wb00_words = pairs[:, 3 * T :].bitcast(BF16)
+        pairs = tile([P, 3 * T], U32, "pairs")
+        dc_pair = pairs[:, 2 * T :]
         pair_product(dc_pair, 0, relu_low[:])
 
-        def gather_dc(words, e, window):
+        def gather_dc(words, e, windows):
             cut = entries(list_c, e * C, C)
             for j in range(2):
-                nc.scalar.activation(words[:, :, 2 + j], dc_high[:, j * T : (j + 1) * T].indirect(cut), ACT.Copy)
-            nc.vector.tensor_copy(word_half(words, 0), window.indirect(cut))
+                nc.scalar.activation(words[:, :, 2 + j], windows[j].indirect(cut), ACT.Copy)
+            nc.vector.tensor_copy(word_half(words, 0), dc_pair.indirect(cut))
 
         q_tok = [tile([P, T], F32, f"q_tok{kb}") for kb in range(KB)]
 
-        def q_bank(name, tag, weights, act, engine_copy=nc.scalar.copy, slots_tag=None):
+        def q_bank(name, tag, weights, act, engine_copy=nc.scalar.copy, slots=None):
             count = act[1].shape[1]
             bank = ps.tile([P, len(weights) * count], F32, name=name, tag=tag)
             for u, block in enumerate(weights):
                 product(bank[:, u * count : (u + 1) * count], block, act)
-            slots = tile([P, len(weights) * count], F32, name + "_slots", slots_tag)
-            engine_copy(slots[:], bank[:])
+            if slots is None:
+                slots = tile([P, len(weights) * count], F32, name + "_slots")[:]
+            engine_copy(slots, bank[:])
             return slots
 
         def scatter_on_scalar(window, offsets, first, values):
@@ -214,25 +215,24 @@ def tile_moe_plb_relu_kernel(
         def scatter_on_vector(window, offsets, first, values):
             nc.vector.tensor_copy(window[:].indirect(entries(offsets, first, values.shape[1])), values)
 
-        dc_words0 = tile([P, C, PACK], BF16, "dc_words0")
-        round_wb(nc.vector.tensor_copy, wb00_words, wb_raw[0, 0][:])
-        gather_dc(dc_words0[:], 0, dc_pair)
-        wb00 = quantise(wb00_words, "wb00")
-        dc_q0 = columns(quantise(flat(dc_words0[:]), "dc_q0"), 0, C)
-        slots00 = q_bank("q00", "high0", [columns(wb00, u * P, P) for u in range(2)], dc_q0)
+        gather_dc(as_words(lower0_words[:, HALF * PACK :]), 0, [dc_high[:, j * T : (j + 1) * T] for j in range(2)])
+        round_wb(nc.scalar.copy, lower0_words[:, 0 : P * PACK], wb_raw[0, 0][:, :, 0:P])
+        round_on_gpsimd(lower0_words[:, P * PACK : HALF * PACK], wb_raw[0, 0][:, :, P:HALF])
         lower1_words = tile([P, (C + HALF) * PACK], BF16, "lower1_words")
-        gather_dc(as_words(lower1_words[:, 0 : C * PACK]), 1, pairs[:, 2 * T :])
-        round_wb(nc.scalar.copy, lower1_words[:, C * PACK :], wb_raw[1, 0][:])
+        gather_dc(as_words(lower1_words[:, 0 : C * PACK]), 1, [dc_high[:, j * T : 2 * T + P] for j in range(2)])
+        lower0 = quantise(lower0_words, "lower0")
+        dc_q0 = columns(lower0, HALF, C)
+        slots00 = q_bank("q00", "high0", [columns(lower0, u * P, P) for u in range(2)], dc_q0)
         for kb in range(2):
             scatter_on_scalar(q_tok[kb], list_c, 0, slots00[:, kb * C : (kb + 1) * C])
 
+        round_wb(nc.vector.tensor_copy, lower1_words[:, C * PACK :], wb_raw[1, 0][:])
         gated = [tile([P, 2, T], F32, f"gated{u}") for u in range(2)]
         nc.vector.scalar_tensor_tensor(gated[0][:], a_pairs[0][:], 0.0, c_pairs[0], ALU.is_gt, ALU.mult)
         lower1 = quantise(lower1_words[:], "lower1")
         dc_q1 = columns(lower1, 0, C)
-        slots10 = q_bank("q10", "high1", [columns(lower1, C + u * P, P) for u in range(2)], dc_q1)
-        for kb in range(2):
-            scatter_on_scalar(q_tok[kb], list_c, C, slots10[:, kb * C : (kb + 1) * C])
+        slots10 = q_bank("q10", "high1", [columns(lower1, C, P)], dc_q1, nc.vector.tensor_copy)
+        scatter_on_scalar(q_tok[0], list_c, C, slots10[:])
 
         upper_words = c_high_zone[:, 0 : 3 * P * PACK]
         nc.vector.scalar_tensor_tensor(gated[1][:], a_pairs[1][:], 0.0, c_pairs[1], ALU.is_gt, ALU.mult)
@@ -244,22 +244,26 @@ def tile_moe_plb_relu_kernel(
         slots01 = q_bank("q01", "high2", [columns(upper, u * P, P) for u in range(2)], dc_q0)
         for u in range(2):
             scatter_on_scalar(q_tok[2 + u], list_c, 0, slots01[:, u * C : (u + 1) * C])
+        slots12 = q_bank("q12", "high0", [columns(upper, C, P)], dc_q1, nc.vector.tensor_copy)
+        scatter_on_scalar(q_tok[2], list_c, C, slots12[:])
 
         picked = tile([P, 2 * T], U32, "picked")
         for u in range(2):
             first = (1 - u) * T
             nc.vector.tensor_copy(picked[:, u * T : (u + 1) * T], pairs[:, first : first + WIDE].indirect(list_a[:]))
-        last_words = pairs[:, T + HALF : 2 * T].bitcast(BF16)
-        round_wb(nc.vector.tensor_copy, last_words, wb_raw[1, 1][:, :, P:HALF])
         da_words = tile([P, 2 * T], U32, "da_words")
-        nc.vector.tensor_copy(
-            da_words[:].bitcast(I32).rearrange("p (g i u) -> p g u i", i=4, u=2),
-            picked[:].bitcast(I32).rearrange("p (u g i) -> p g u i", i=4, u=2),
+        nc.gpsimd.tensor_copy(
+            da_words[:].rearrange("p (s u) -> p s u", u=2), picked[:].rearrange("p (u s) -> p s u", u=2)
         )
-        wb13 = quantise(last_words, "wb13")
+        slots11 = q_bank(
+            "q11", "high3", [columns(lower1, C + P, P)], dc_q1, nc.vector.tensor_copy,
+            pairs[:, T + HALF : 2 * T].bitcast(F32),
+        )
+        scatter_on_vector(q_tok[1], list_c, C, slots11)
         da_q = quantise(da_words[:].bitcast(BF16), "da_q")
-        slots12 = q_bank("q12", "high3", [columns(upper, C, P)], dc_q1, nc.vector.tensor_copy, "da_words")
-        scatter_on_vector(q_tok[2], list_c, C, slots12[:])
+        last_words = picked[:, 0:HALF].bitcast(BF16)
+        round_wb(nc.vector.tensor_copy, last_words, wb_raw[1, 1][:, :, P:HALF])
+        wb13 = quantise(last_words, "wb13")
 
         r_tok = [tile([P, WIDE if kb in (0, 3) else T], F32, f"r_tok{kb}") for kb in range(KB)]
 
@@ -271,16 +275,16 @@ def tile_moe_plb_relu_kernel(
             engine_copy(slots[:], bank[:])
             return slots
 
-        r_slots1 = r_bank(1, nc.scalar.copy)
+        r_slots1 = r_bank(1, nc.vector.tensor_copy)
         r_slots0 = r_bank(0, nc.vector.tensor_copy)
         r_slots2 = r_bank(2, nc.vector.tensor_copy)
         r_slots3 = r_bank(3, nc.vector.tensor_copy)
+        slots13 = q_bank("q13", "high1", [columns(wb13, 0, P)], dc_q1, nc.vector.tensor_copy)
         scatter_on_vector(r_tok[0], list_a, 0, r_slots0[:])
         scatter_on_vector(r_tok[3], list_a, 0, r_slots3[:])
         for e in range(E):
             for kb, slots in ((1, r_slots1), (2, r_slots2)):
                 scatter_on_scalar(r_tok[kb], list_a, e * C, slots[:, e * C : (e + 1) * C])
-        slots13 = q_bank("q13", "low3", [columns(wb13, 0, P)], dc_q1)
         scatter_on_scalar(q_tok[3], list_c, C, slots13[:])
 
         before = None

@@ -24,6 +24,7 @@ KB = K // P
 HALF = K // 2
 PER_COL = 16
 WIDE = 704
+FILL = 160
 
 
 def tile_moe_plb_relu_kernel(
@@ -197,16 +198,15 @@ def tile_moe_plb_relu_kernel(
                 nc.scalar.activation(words[:, :, 2 + j], windows[j].indirect(cut), ACT.Copy)
             nc.vector.tensor_copy(word_half(words, 0), dc_pair.indirect(cut))
 
-        q_tok = [tile([P, T], F32, f"q_tok{kb}") for kb in range(KB)]
+        q_tok = [tile([P, T], F32, f"q_tok{kb}") for kb in range(KB - 1)]
 
-        def q_bank(name, tag, weights, act, engine_copy=nc.scalar.copy, slots=None):
+        def q_bank(name, tag, weights, act, engine_copy=nc.scalar.copy):
             count = act[1].shape[1]
             bank = ps.tile([P, len(weights) * count], F32, name=name, tag=tag)
             for u, block in enumerate(weights):
                 product(bank[:, u * count : (u + 1) * count], block, act)
-            if slots is None:
-                slots = tile([P, len(weights) * count], F32, name + "_slots")[:]
-            engine_copy(slots, bank[:])
+            slots = tile([P, len(weights) * count], F32, name + "_slots")
+            engine_copy(slots[:], bank[:])
             return slots
 
         def scatter_on_scalar(window, offsets, first, values):
@@ -231,8 +231,11 @@ def tile_moe_plb_relu_kernel(
         nc.vector.scalar_tensor_tensor(gated[0][:], a_pairs[0][:], 0.0, c_pairs[0], ALU.is_gt, ALU.mult)
         lower1 = quantise(lower1_words[:], "lower1")
         dc_q1 = columns(lower1, 0, C)
-        slots10 = q_bank("q10", "high1", [columns(lower1, C, P)], dc_q1, nc.vector.tensor_copy)
-        scatter_on_scalar(q_tok[0], list_c, C, slots10[:])
+        slots10 = q_bank(
+            "q10", "high1", [columns(lower1, C + u * P, P) for u in range(2)], dc_q1, nc.vector.tensor_copy
+        )
+        for kb in range(2):
+            scatter_on_scalar(q_tok[kb], list_c, C, slots10[:, kb * C : (kb + 1) * C])
 
         upper_words = c_high_zone[:, 0 : 3 * P * PACK]
         nc.vector.scalar_tensor_tensor(gated[1][:], a_pairs[1][:], 0.0, c_pairs[1], ALU.is_gt, ALU.mult)
@@ -242,24 +245,25 @@ def tile_moe_plb_relu_kernel(
         pair_product(pairs[:, 0:T], 1, gated[1][:])
         upper = quantise(upper_words, "upper")
         slots01 = q_bank("q01", "high2", [columns(upper, u * P, P) for u in range(2)], dc_q0)
-        for u in range(2):
-            scatter_on_scalar(q_tok[2 + u], list_c, 0, slots01[:, u * C : (u + 1) * C])
-        slots12 = q_bank("q12", "high0", [columns(upper, C, P)], dc_q1, nc.vector.tensor_copy)
-        scatter_on_scalar(q_tok[2], list_c, C, slots12[:])
+        scatter_on_scalar(q_tok[2], list_c, 0, slots01[:, 0:C])
 
         picked = tile([P, 2 * T], U32, "picked")
-        for u in range(2):
+
+        def gather_da(u):
             first = (1 - u) * T
             nc.vector.tensor_copy(picked[:, u * T : (u + 1) * T], pairs[:, first : first + WIDE].indirect(list_a[:]))
+
+        gather_da(0)
+        slots12 = q_bank("q12", "high0", [columns(upper, C, P)], dc_q1, nc.vector.tensor_copy)
+        scatter_on_scalar(q_tok[2], list_c, C, slots12[:])
+        gather_da(1)
         da_words = tile([P, 2 * T], U32, "da_words")
         nc.gpsimd.tensor_copy(
             da_words[:].rearrange("p (s u) -> p s u", u=2), picked[:].rearrange("p (u s) -> p s u", u=2)
         )
-        slots11 = q_bank(
-            "q11", "high3", [columns(lower1, C + P, P)], dc_q1, nc.vector.tensor_copy,
-            pairs[:, T + HALF : 2 * T].bitcast(F32),
-        )
-        scatter_on_vector(q_tok[1], list_c, C, slots11)
+        q_tok.append(tile([P, T], F32, "q_tok3", "pairs"))
+        scatter_on_vector(q_tok[3], list_c, 0, slots01[:, C : C + FILL])
+        scatter_on_scalar(q_tok[3], list_c, FILL, slots01[:, C + FILL :])
         da_q = quantise(da_words[:].bitcast(BF16), "da_q")
         last_words = picked[:, 0:HALF].bitcast(BF16)
         round_wb(nc.vector.tensor_copy, last_words, wb_raw[1, 1][:, :, P:HALF])

@@ -24,7 +24,6 @@ KB = K // P
 HALF = K // 2
 PER_COL = 16
 WIDE = 704
-FILL = 160
 
 
 def tile_moe_plb_relu_kernel(
@@ -200,12 +199,15 @@ def tile_moe_plb_relu_kernel(
 
         q_tok = [tile([P, T], F32, f"q_tok{kb}") for kb in range(KB - 1)]
 
-        def q_bank(name, tag, weights, act, engine_copy=nc.scalar.copy):
-            count = act[1].shape[1]
-            bank = ps.tile([P, len(weights) * count], F32, name=name, tag=tag)
-            for u, block in enumerate(weights):
-                product(bank[:, u * count : (u + 1) * count], block, act)
-            slots = tile([P, len(weights) * count], F32, name + "_slots")
+        def q_bank(name, tag, operands, engine_copy=nc.scalar.copy):
+            width = sum(act[1].shape[1] for block, act in operands)
+            bank = ps.tile([P, width], F32, name=name, tag=tag)
+            first = 0
+            for block, act in operands:
+                count = act[1].shape[1]
+                product(bank[:, first : first + count], block, act)
+                first += count
+            slots = tile([P, width], F32, name + "_slots")
             engine_copy(slots[:], bank[:])
             return slots
 
@@ -221,8 +223,8 @@ def tile_moe_plb_relu_kernel(
         lower1_words = tile([P, (C + HALF) * PACK], BF16, "lower1_words")
         gather_dc(as_words(lower1_words[:, 0 : C * PACK]), 1, [dc_high[:, j * T : 2 * T + P] for j in range(2)])
         lower0 = quantise(lower0_words, "lower0")
-        dc_q0 = columns(lower0, HALF, C)
-        slots00 = q_bank("q00", "high0", [columns(lower0, u * P, P) for u in range(2)], dc_q0)
+        dc_q = [columns(lower0, HALF, C)]
+        slots00 = q_bank("q00", "high0", [(columns(lower0, u * P, P), dc_q[0]) for u in range(2)])
         for kb in range(2):
             scatter_on_scalar(q_tok[kb], list_c, 0, slots00[:, kb * C : (kb + 1) * C])
 
@@ -230,9 +232,9 @@ def tile_moe_plb_relu_kernel(
         gated = [tile([P, 2, T], F32, f"gated{u}") for u in range(2)]
         nc.vector.scalar_tensor_tensor(gated[0][:], a_pairs[0][:], 0.0, c_pairs[0], ALU.is_gt, ALU.mult)
         lower1 = quantise(lower1_words[:], "lower1")
-        dc_q1 = columns(lower1, 0, C)
+        dc_q.append(columns(lower1, 0, C))
         slots10 = q_bank(
-            "q10", "high1", [columns(lower1, C + u * P, P) for u in range(2)], dc_q1, nc.vector.tensor_copy
+            "q10", "high1", [(columns(lower1, C + u * P, P), dc_q[1]) for u in range(2)], nc.vector.tensor_copy
         )
         for kb in range(2):
             scatter_on_scalar(q_tok[kb], list_c, C, slots10[:, kb * C : (kb + 1) * C])
@@ -244,8 +246,9 @@ def tile_moe_plb_relu_kernel(
         pair_product(pairs[:, T : 2 * T], 0, gated[0][:])
         pair_product(pairs[:, 0:T], 1, gated[1][:])
         upper = quantise(upper_words, "upper")
-        slots01 = q_bank("q01", "high2", [columns(upper, u * P, P) for u in range(2)], dc_q0)
-        scatter_on_scalar(q_tok[2], list_c, 0, slots01[:, 0:C])
+        slots2 = q_bank("q2", "high2", [(columns(upper, e * C, P), dc_q[e]) for e in range(E)])
+        for e in range(E):
+            scatter_on_scalar(q_tok[2], list_c, e * C, slots2[:, e * C : (e + 1) * C])
 
         picked = tile([P, 2 * T], U32, "picked")
 
@@ -254,20 +257,19 @@ def tile_moe_plb_relu_kernel(
             nc.vector.tensor_copy(picked[:, u * T : (u + 1) * T], pairs[:, first : first + WIDE].indirect(list_a[:]))
 
         gather_da(0)
-        slots12 = q_bank("q12", "high0", [columns(upper, C, P)], dc_q1, nc.vector.tensor_copy)
-        scatter_on_scalar(q_tok[2], list_c, C, slots12[:])
+        slots03 = q_bank("q03", "high0", [(columns(upper, P, P), columns(lower0, HALF, P))], nc.vector.tensor_copy)
         gather_da(1)
-        da_words = tile([P, 2 * T], U32, "da_words")
-        nc.gpsimd.tensor_copy(
-            da_words[:].rearrange("p (s u) -> p s u", u=2), picked[:].rearrange("p (u s) -> p s u", u=2)
-        )
-        q_tok.append(tile([P, T], F32, "q_tok3", "pairs"))
-        scatter_on_vector(q_tok[3], list_c, 0, slots01[:, C : C + FILL])
-        scatter_on_scalar(q_tok[3], list_c, FILL, slots01[:, C + FILL :])
-        da_q = quantise(da_words[:].bitcast(BF16), "da_q")
-        last_words = picked[:, 0:HALF].bitcast(BF16)
+        last_words = pairs[:, T + HALF : 2 * T].bitcast(BF16)
         round_wb(nc.vector.tensor_copy, last_words, wb_raw[1, 1][:, :, P:HALF])
+        da_words = tile([P, 2 * T], U32, "da_words")
+        nc.vector.tensor_copy(
+            da_words[:].bitcast(I32).rearrange("p (g i u) -> p g u i", i=4, u=2),
+            picked[:].bitcast(I32).rearrange("p (u g i) -> p g u i", i=4, u=2),
+        )
         wb13 = quantise(last_words, "wb13")
+        da_q = quantise(da_words[:].bitcast(BF16), "da_q")
+        q_tok.append(tile([P, T], F32, "q_tok3", "da_words"))
+        scatter_on_vector(q_tok[3], list_c, 0, slots03[:])
 
         r_tok = [tile([P, WIDE if kb in (0, 3) else T], F32, f"r_tok{kb}") for kb in range(KB)]
 
@@ -283,13 +285,15 @@ def tile_moe_plb_relu_kernel(
         r_slots0 = r_bank(0, nc.vector.tensor_copy)
         r_slots2 = r_bank(2, nc.vector.tensor_copy)
         r_slots3 = r_bank(3, nc.vector.tensor_copy)
-        slots13 = q_bank("q13", "high1", [columns(wb13, 0, P)], dc_q1, nc.vector.tensor_copy)
+        rest3 = [(columns(upper, P, P), columns(lower0, HALF + P, P)), (columns(wb13, 0, P), dc_q[1])]
+        slots3 = q_bank("q3", "low1", rest3, nc.vector.tensor_copy)
+        scatter_on_vector(q_tok[3], list_c, P, slots3[:, 0:P])
         scatter_on_vector(r_tok[0], list_a, 0, r_slots0[:])
         scatter_on_vector(r_tok[3], list_a, 0, r_slots3[:])
         for e in range(E):
             for kb, slots in ((1, r_slots1), (2, r_slots2)):
                 scatter_on_scalar(r_tok[kb], list_a, e * C, slots[:, e * C : (e + 1) * C])
-        scatter_on_scalar(q_tok[3], list_c, C, slots13[:])
+        scatter_on_scalar(q_tok[3], list_c, C, slots3[:, P:])
 
         before = None
         for kb in (1, 0, 2):

@@ -126,9 +126,9 @@ def tile_moe_plb_relu_kernel(
                 for j in range(2):
                     dh_product(dh[u, h][:, j, :], 2 * u + j, halves[h])
 
-        def quantise(values, name):
+        def quantise(values, name, codes_tag=None):
             width = values.shape[1] // PACK
-            codes = tile([P, width], U32, name + "_codes")
+            codes = tile([P, width], U32, name + "_codes", codes_tag)
             plane = tile([P, width], U8, name + "_plane")
             nc.vector.quantize_mx(codes[:].bitcast(FP8X4), plane[:], values)
             return codes, plane
@@ -218,20 +218,20 @@ def tile_moe_plb_relu_kernel(
             nc.vector.tensor_copy(window[:].indirect(entries(offsets, first, values.shape[1])), values)
 
         gather_dc(as_words(lower0_words[:, HALF * PACK :]), 0, [dc_high[:, j * T : (j + 1) * T] for j in range(2)])
-        round_wb(nc.scalar.copy, lower0_words[:, 0 : P * PACK], wb_raw[0, 0][:, :, 0:P])
-        round_on_gpsimd(lower0_words[:, P * PACK : HALF * PACK], wb_raw[0, 0][:, :, P:HALF])
+        round_on_gpsimd(lower0_words[:, 0 : HALF * PACK], wb_raw[0, 0][:])
         lower1_words = tile([P, (C + HALF) * PACK], BF16, "lower1_words")
-        gather_dc(as_words(lower1_words[:, 0 : C * PACK]), 1, [dc_high[:, j * T : 2 * T + P] for j in range(2)])
+        gather_dc(as_words(lower1_words[:, 0 : C * PACK]), 1, [dc_high[:, j * T : (j + 1) * T] for j in range(2)])
+        round_on_gpsimd(lower1_words[:, C * PACK : (C + P) * PACK], wb_raw[1, 0][:, :, 0:P])
+        round_wb(nc.scalar.copy, lower1_words[:, (C + P) * PACK :], wb_raw[1, 0][:, :, P:HALF])
         lower0 = quantise(lower0_words, "lower0")
         dc_q = [columns(lower0, HALF, C)]
         slots00 = q_bank("q00", "high0", [(columns(lower0, u * P, P), dc_q[0]) for u in range(2)])
         for kb in range(2):
             scatter_on_scalar(q_tok[kb], list_c, 0, slots00[:, kb * C : (kb + 1) * C])
 
-        round_wb(nc.vector.tensor_copy, lower1_words[:, C * PACK :], wb_raw[1, 0][:])
         gated = [tile([P, 2, T], F32, f"gated{u}") for u in range(2)]
         nc.vector.scalar_tensor_tensor(gated[0][:], a_pairs[0][:], 0.0, c_pairs[0], ALU.is_gt, ALU.mult)
-        lower1 = quantise(lower1_words[:], "lower1")
+        lower1 = quantise(lower1_words[:], "lower1", "c_low")
         dc_q.append(columns(lower1, 0, C))
         slots10 = q_bank(
             "q10", "high1", [(columns(lower1, C + u * P, P), dc_q[1]) for u in range(2)], nc.vector.tensor_copy

@@ -24,6 +24,7 @@ KB = K // P
 HALF = K // 2
 PER_COL = 16
 WIDE = 704
+SHARE = 96
 
 
 def tile_moe_plb_relu_kernel(
@@ -72,11 +73,11 @@ def tile_moe_plb_relu_kernel(
         def load_pair(pairs, planes, u):
             nc.sync.dma_start(out=pairs[u], in_=planes[:, 2 * u : 2 * u + 2, :])
 
+        nc.sync.dma_start(list_c[:], offs2)
         nc.sync.dma_start(out=w2_raw[:].bitcast(I32), in_=w2t_words[0].bitcast(I32))
         load_scale_rows(w2_plane_raw, w2t_scales[0])
         nc.sync.dma_start(out=dy_codes[:].bitcast(I32), in_=dy_words[0].rearrange("p t d -> p (t d)").bitcast(I32))
         load_pair(a_views, a_planes, 1)
-        nc.sync.dma_start(list_c[:], offs2)
         load_scale_rows(dy_plane, dy_scales[0])
         load_pair(a_views, a_planes, 0)
         load_wb(0, 0)
@@ -273,30 +274,28 @@ def tile_moe_plb_relu_kernel(
 
         r_tok = [tile([P, WIDE if kb in (0, 3) else T], F32, f"r_tok{kb}") for kb in range(KB)]
 
-        def r_bank(kb, engine_copy):
-            bank = ps.tile([P, T], F32, name=f"r{kb}", tag=f"low{kb}")
-            for e in range(E):
-                product(bank[:, e * C : (e + 1) * C], wa_block(e, kb), columns(da_q, e * C, C))
-            slots = tile([P, T], F32, f"r_slots{kb}")
-            engine_copy(slots[:], bank[:])
-            return slots
+        def r_operands(e, kb):
+            return wa_block(e, kb), columns(da_q, e * C, C)
 
-        r_slots1 = r_bank(1, nc.vector.tensor_copy)
-        r_slots0 = r_bank(0, nc.vector.tensor_copy)
-        r_slots2 = r_bank(2, nc.vector.tensor_copy)
-        r_slots3 = r_bank(3, nc.vector.tensor_copy)
-        rest3 = [(columns(upper, P, P), columns(lower0, HALF + P, P)), (columns(wb13, 0, P), dc_q[1])]
-        slots3 = q_bank("q3", "low1", rest3, nc.vector.tensor_copy)
-        scatter_on_vector(q_tok[3], list_c, P, slots3[:, 0:P])
+        def r_bank(name, tag, operands):
+            return q_bank(name, tag, operands, nc.vector.tensor_copy)
+
+        middle = [r_bank("r_middle0", "low1", [r_operands(0, kb) for kb in (1, 2)])]
+        r_slots0 = r_bank("r0", "low0", [r_operands(e, 0) for e in range(E)])
+        middle.append(r_bank("r_middle1", "low2", [r_operands(1, kb) for kb in (1, 2)]))
         scatter_on_vector(r_tok[0], list_a, 0, r_slots0[:])
+        rest3 = [(columns(upper, P, P), columns(lower0, HALF + P, P)), (columns(wb13, 0, P), dc_q[1])]
+        slots3 = r_bank("q3", "low1", rest3)
+        r_slots3 = r_bank("r3", "low3", [r_operands(e, 3) for e in range(E)])
+        scatter_on_vector(q_tok[3], list_c, P, slots3[:, 0:SHARE])
         scatter_on_vector(r_tok[3], list_a, 0, r_slots3[:])
         for e in range(E):
-            for kb, slots in ((1, r_slots1), (2, r_slots2)):
-                scatter_on_scalar(r_tok[kb], list_a, e * C, slots[:, e * C : (e + 1) * C])
-        scatter_on_scalar(q_tok[3], list_c, C, slots3[:, P:])
+            for u in range(2):
+                scatter_on_scalar(r_tok[1 + u], list_a, e * C, middle[e][:, u * C : (u + 1) * C])
+        scatter_on_scalar(q_tok[3], list_c, P + SHARE, slots3[:, SHARE:])
 
         before = None
-        for kb in (1, 0, 2):
+        for kb in range(KB - 1):
             total = tile([P, T], F32, f"total{kb}", before)
             nc.gpsimd.tensor_tensor(total[:], r_tok[kb][:, 0:T], q_tok[kb][:], ALU.add)
             nc.sync.dma_start(out=out[kb * P : (kb + 1) * P, :], in_=total[:])

@@ -24,7 +24,7 @@ KB = K // P
 HALF = K // 2
 PER_COL = 16
 WIDE = 704
-SHARE = 96
+SHARE = 64
 
 
 def tile_moe_plb_relu_kernel(
@@ -120,12 +120,10 @@ def tile_moe_plb_relu_kernel(
             )
 
         halves = [slice(h * HALF, (h + 1) * HALF) for h in range(2)]
-        dh = {}
-        for u in (1, 0):
-            for h in range(2):
-                dh[u, h] = ps.tile([P, 2, HALF], F32, name=f"dh{u}{h}", tag=f"low{2 * u + h}")
-                for j in range(2):
-                    dh_product(dh[u, h][:, j, :], 2 * u + j, halves[h])
+        dh = {
+            (u, h): ps.tile([P, 2, HALF], F32, name=f"dh{u}{h}", tag=f"low{2 * u + h}")
+            for u in range(2) for h in range(2)
+        }
 
         def quantise(values, name, codes_tag=None):
             width = values.shape[1] // PACK
@@ -181,13 +179,23 @@ def tile_moe_plb_relu_kernel(
 
         dc_high = tile([P, 2 * T + (HALF + C) * PACK], BF16, "dc_high")
         lower0_words = dc_high[:, 2 * T :]
+        early = [ps.tile([P, HALF], F32, name=f"early{h}", tag=f"high{2 + h}") for h in range(2)]
+        sources = [[bank[:] for bank in early], [dh[1, h][:, 1, :] for h in range(2)]]
+        for j in range(2):
+            for h in range(2):
+                dh_product(sources[j][h], 2 + j, halves[h])
+        for h in range(2):
+            for j in range(2):
+                dh_product(dh[0, h][:, j, :], j, halves[h])
         for j in range(2):
             for h in range(2):
                 first = j * T + h * HALF
                 nc.vector.scalar_tensor_tensor(
                     dc_high[:, first : first + HALF], a_pairs[1][:, j, halves[h]], 0.0,
-                    dh[1, h][:, j, :], ALU.max, ALU.mult,
+                    sources[j][h], ALU.max, ALU.mult,
                 )
+        for h in range(2):
+            dh_product(dh[1, h][:, 0, :], 2, halves[h])
         pairs = tile([P, 3 * T], U32, "pairs")
         dc_pair = pairs[:, 2 * T :]
         pair_product(dc_pair, 0, relu_low[:])
@@ -226,9 +234,9 @@ def tile_moe_plb_relu_kernel(
         round_wb(nc.scalar.copy, lower1_words[:, (C + P) * PACK :], wb_raw[1, 0][:, :, P:HALF])
         lower0 = quantise(lower0_words, "lower0")
         dc_q = [columns(lower0, HALF, C)]
-        slots00 = q_bank("q00", "high0", [(columns(lower0, u * P, P), dc_q[0]) for u in range(2)])
+        slots0 = [q_bank(f"q0{kb}", f"high{3 * kb}", [(columns(lower0, kb * P, P), dc_q[0])]) for kb in range(2)]
         for kb in range(2):
-            scatter_on_scalar(q_tok[kb], list_c, 0, slots00[:, kb * C : (kb + 1) * C])
+            scatter_on_scalar(q_tok[kb], list_c, 0, slots0[kb][:])
 
         gated = [tile([P, 2, T], F32, f"gated{u}") for u in range(2)]
         nc.vector.scalar_tensor_tensor(gated[0][:], a_pairs[0][:], 0.0, c_pairs[0], ALU.is_gt, ALU.mult)
@@ -247,9 +255,9 @@ def tile_moe_plb_relu_kernel(
         pair_product(pairs[:, T : 2 * T], 0, gated[0][:])
         pair_product(pairs[:, 0:T], 1, gated[1][:])
         upper = quantise(upper_words, "upper")
-        slots2 = q_bank("q2", "high2", [(columns(upper, e * C, P), dc_q[e]) for e in range(E)])
+        slots2 = [q_bank(f"q{e}2", f"high{2 + e}", [(columns(upper, e * C, P), dc_q[e])]) for e in range(E)]
         for e in range(E):
-            scatter_on_scalar(q_tok[2], list_c, e * C, slots2[:, e * C : (e + 1) * C])
+            scatter_on_scalar(q_tok[2], list_c, e * C, slots2[e][:])
 
         picked = tile([P, 2 * T], U32, "picked")
 

@@ -57,6 +57,7 @@ def tile_moe_plb_relu_kernel(
         c_planes = c.rearrange("(p t) n -> p t n", t=PACK)
         a_pairs = [tile([P, 2, T], F32, f"a_pair{u}") for u in range(2)]
         a_views = [pair[:] for pair in a_pairs]
+        halves = [slice(h * HALF, (h + 1) * HALF) for h in range(2)]
         c_low = tile([P, 2, T], F32, "c_low")
         c_high_zone = tile([P, 4 * T], BF16, "c_high_zone")
         c_high = c_high_zone[:].bitcast(F32).rearrange("p (j n) -> p j n", j=2)
@@ -79,7 +80,8 @@ def tile_moe_plb_relu_kernel(
         nc.sync.dma_start(out=dy_codes[:].bitcast(I32), in_=dy_words[0].rearrange("p t d -> p (t d)").bitcast(I32))
         load_pair(a_views, a_planes, 1)
         load_scale_rows(dy_plane, dy_scales[0])
-        load_pair(a_views, a_planes, 0)
+        for cols in halves:
+            nc.sync.dma_start(out=a_pairs[0][:, :, cols], in_=a_planes[:, 0:2, cols])
         load_wb(0, 0)
         load_wb(1, 0)
         load_pair(c_pairs, c_planes, 0)
@@ -119,7 +121,6 @@ def tile_moe_plb_relu_kernel(
                 stop=True,
             )
 
-        halves = [slice(h * HALF, (h + 1) * HALF) for h in range(2)]
         dh = {
             (u, h): ps.tile([P, 2, HALF], F32, name=f"dh{u}{h}", tag=f"low{2 * u + h}")
             for u in range(2) for h in range(2)
@@ -277,7 +278,7 @@ def tile_moe_plb_relu_kernel(
         )
         wb13 = quantise(last_words, "wb13")
         da_q = quantise(da_words[:].bitcast(BF16), "da_q")
-        q_tok.append(tile([P, T], F32, "q_tok3", "da_words"))
+        q_tok.append(tile([P, T], F32, "q_tok3", "picked"))
         scatter_on_vector(q_tok[3], list_c, 0, slots03[:])
 
         r_tok = [tile([P, WIDE if kb in (0, 3) else T], F32, f"r_tok{kb}") for kb in range(KB)]

@@ -172,9 +172,9 @@ def tile_moe_plb_relu_kernel(
         def pair_product(words, u, factor):
             for h in range(2):
                 nc.vector.tensor_tensor(
-                    words[:, halves[h]].bitcast(BF16).rearrange("p (g i j) -> p g j i", i=4, j=2),
-                    dh[u, h][:].rearrange("p j (g i) -> p g j i", i=4),
-                    factor[:, :, halves[h]].rearrange("p j (g i) -> p g j i", i=4),
+                    words[:, halves[h]].bitcast(BF16).rearrange("p (g i j) -> p g j i", i=2, j=2),
+                    dh[u, h][:].rearrange("p j (g i) -> p g j i", i=2),
+                    factor[:, :, halves[h]].rearrange("p j (g i) -> p g j i", i=2),
                     ALU.mult,
                 )
 

import math
from contextlib import ExitStack

import concourse.mybir as mybir

K, T, H, N = 512, 512, 512, 512
E, C = 2, 256
FLOPS = 2 * N * H * T + 2 * 2 * H * K * T

F32 = mybir.dt.float32
BF16 = mybir.dt.bfloat16
I32 = mybir.dt.int32
U32 = mybir.dt.uint32
U16 = mybir.dt.uint16
U8 = mybir.dt.uint8
FP8X4 = mybir.dt.float8_e4m3fn_x4
FP4X4 = mybir.dt.float4_e2m1fn_x4
ALU = mybir.AluOpType
ACT = mybir.ActivationFunctionType

P = 128
PACK = 4
KB = K // P
HALF = K // 2
PER_COL = 16
WIDE = 704
SHARE = 64


def tile_moe_plb_relu_kernel(
    tc, dy_words, dy_scales, w2t_words, w2t_scales, wat_words, wat_scales, wbt, a, c, offs, offs2, out
):
    nc = tc.nc
    with ExitStack() as ctx:
        sb = ctx.enter_context(tc.tile_pool(name="sb", bufs=1))
        ps = ctx.enter_context(tc.psum_pool(name="ps", bufs=1))

        def tile(shape, dtype, name, tag=None):
            return sb.tile(shape, dtype, name=name, tag=tag or name, align_bytes=64)

        list_a = sb.tile([P, T // PER_COL], U16, name="list_a")
        list_c = sb.tile([P, T // PER_COL], U16, name="list_c")

        w2_plane_raw = tile([P, H], U8, "w2_plane_raw")
        dy_plane = tile([P, T], U8, "dy_plane")
        wa_plane = tile([P, E, K], U8, "wa_plane")
        nc.gpsimd.memset(w2_plane_raw[:].bitcast(I32), 0)
        nc.gpsimd.memset(dy_plane[:].bitcast(I32), 0)
        nc.vector.memset(wa_plane[:].bitcast(I32), 0)

        def load_scale_rows(plane, rows):
            by_row = rows.bitcast(I32).rearrange("(q r) n -> r q n", r=4)
            for r in range(4):
                nc.sync.dma_start(out=plane[r:P:32, :].bitcast(I32), in_=by_row[r])

        a_planes = a.rearrange("(p t) n -> p t n", t=PACK)
        c_planes = c.rearrange("(p t) n -> p t n", t=PACK)
        a_pairs = [tile([P, 2, T], F32, f"a_pair{u}") for u in range(2)]
        a_views = [pair[:] for pair in a_pairs]
        halves = [slice(h * HALF, (h + 1) * HALF) for h in range(2)]
        c_low = tile([P, 2, T], F32, "c_low")
        c_high_zone = tile([P, 4 * T], BF16, "c_high_zone")
        c_high = c_high_zone[:].bitcast(F32).rearrange("p (j n) -> p j n", j=2)
        c_pairs = [c_low[:], c_high]
        w2_raw = tile([P, 2 * H], U8, "w2_raw")
        dy_codes = tile([P, T], U32, "dy_codes")
        wa_codes = tile([P, E, 2 * K], U8, "wa_codes")
        wb_rows = [wbt[e].rearrange("(p j) k -> p j k", j=PACK) for e in range(E)]
        wb_raw = {(e, h): tile([P, PACK, HALF], F32, f"wb_raw{e}{h}") for e in range(E) for h in range(2)}

        def load_wb(e, h):
            nc.sync.dma_start(out=wb_raw[e, h][:], in_=wb_rows[e][:, :, h * HALF : (h + 1) * HALF])

        def load_pair(pairs, planes, u):
            nc.sync.dma_start(out=pairs[u], in_=planes[:, 2 * u : 2 * u + 2, :])

        nc.sync.dma_start(list_c[:], offs2)
        nc.sync.dma_start(out=w2_raw[:].bitcast(I32), in_=w2t_words[0].bitcast(I32))
        load_scale_rows(w2_plane_raw, w2t_scales[0])
        nc.sync.dma_start(out=dy_codes[:].bitcast(I32), in_=dy_words[0].rearrange("p t d -> p (t d)").bitcast(I32))
        load_pair(a_views, a_planes, 1)
        load_scale_rows(dy_plane, dy_scales[0])
        for cols in halves:
            nc.sync.dma_start(out=a_pairs[0][:, :, cols], in_=a_planes[:, 0:2, cols])
        load_wb(0, 0)
        load_wb(1, 0)
        load_pair(c_pairs, c_planes, 0)
        load_pair(c_pairs, c_planes, 1)
        load_wb(0, 1)
        load_wb(1, 1)
        nc.sync.dma_start(list_a[:], offs)
        nc.sync.dma_start(out=wa_codes[:].bitcast(I32), in_=wat_words.rearrange("e s p b -> p (e s) b").bitcast(I32))
        wa_rows = wat_scales.bitcast(I32).rearrange("e s (q r) n -> r q (e s) n", r=4)
        for r in range(4):
            nc.sync.dma_start(out=wa_plane[r:P:32, :, :].bitcast(I32), in_=wa_rows[r])

        w2_codes = tile([P, 2 * H], U8, "w2_codes")
        w2_plane = tile([P, H], U8, "w2_plane")
        nc.vector.tensor_copy(
            out=w2_codes[:].bitcast(U16).rearrange("p (t m) -> p t m", t=PACK),
            in_=w2_raw[:].bitcast(U16).rearrange("p (m t) -> p t m", t=PACK),
        )
        nc.vector.tensor_copy(
            out=w2_plane[:].rearrange("p (t m) -> p t m", t=PACK),
            in_=w2_plane_raw[:].rearrange("p (m t) -> p t m", t=PACK),
        )

        relu_low = tile([P, 2, T], F32, "relu_low")
        for h in range(2):
            cols = slice(h * HALF, (h + 1) * HALF)
            nc.gpsimd.tensor_scalar(relu_low[:, :, cols], a_pairs[0][:, :, cols], math.inf, 0.0, ALU.min, ALU.max)

        def dh_product(target, t, cols):
            nc.tensor.matmul_mx(
                out=target,
                lhsT=w2_codes[:, 2 * P * t : 2 * P * (t + 1)].bitcast(FP4X4),
                lhsT_scale=w2_plane[:, P * t : P * (t + 1)],
                rhs=dy_codes[:, cols].bitcast(FP8X4),
                rhs_scale=dy_plane[:, cols],
                start=True,
                stop=True,
            )

        dh = {
            (u, h): ps.tile([P, 2, HALF], F32, name=f"dh{u}{h}", tag=f"low{2 * u + h}")
            for u in range(2) for h in range(2)
        }

        def quantise(values, name, codes_tag=None):
            width = values.shape[1] // PACK
            codes = tile([P, width], U32, name + "_codes", codes_tag)
            plane = tile([P, width], U8, name + "_plane")
            nc.vector.quantize_mx(codes[:].bitcast(FP8X4), plane[:], values)
            return codes, plane

        def flat(words):
            return words.rearrange("p w j -> p (w j)")

        def round_wb(engine_copy, words, raw):
            engine_copy(
                words.rearrange("p (g i j) -> p g j i", i=4, j=PACK), raw.rearrange("p j (g i) -> p g j i", i=4)
            )

        def round_on_gpsimd(words, raw):
            nc.gpsimd.tensor_scalar(
                words.rearrange("p (k j) -> p k j", j=PACK), raw.rearrange("p j k -> p k j"),
                1.0, 0.0, ALU.mult, ALU.add,
            )

        def columns(quantised, first, count):
            codes, plane = quantised
            return codes[:, first : first + count].bitcast(FP8X4), plane[:, first : first + count]

        def product(target, weights, act):
            nc.tensor.matmul_mx(
                out=target, lhsT=weights[0], lhsT_scale=weights[1],
                rhs=act[0], rhs_scale=act[1], start=True, stop=True,
            )

        def wa_block(e, kb):
            return wa_codes[:, e, 2 * P * kb : 2 * P * (kb + 1)].bitcast(FP4X4), wa_plane[:, e, P * kb : P * (kb + 1)]

        def entries(offsets, first, count):
            return offsets[:, first // PER_COL : (first + count) // PER_COL]

        def word_half(words, u):
            return flat(words).bitcast(U32).rearrange("p (w u) -> p w u", u=2)[:, :, u]

        def as_words(values):
            return values.rearrange("p (w j) -> p w j", j=PACK)

        def pair_product(words, u, factor):
            for h in range(2):
                nc.vector.tensor_tensor(
                    words[:, halves[h]].bitcast(BF16).rearrange("p (g i j) -> p g j i", i=2, j=2),
                    dh[u, h][:].rearrange("p j (g i) -> p g j i", i=2),
                    factor[:, :, halves[h]].rearrange("p j (g i) -> p g j i", i=2),
                    ALU.mult,
                )

        dc_high = tile([P, 2 * T + (HALF + C) * PACK], BF16, "dc_high")
        lower0_words = dc_high[:, 2 * T :]
        early = [ps.tile([P, HALF], F32, name=f"early{h}", tag=f"high{2 + h}") for h in range(2)]
        sources = [[bank[:] for bank in early], [dh[1, h][:, 1, :] for h in range(2)]]
        for j in range(2):
            for h in range(2):
                dh_product(sources[j][h], 2 + j, halves[h])
        for h in range(2):
            for j in range(2):
                dh_product(dh[0, h][:, j, :], j, halves[h])
        for j in range(2):
            for h in range(2):
                first = j * T + h * HALF
                nc.vector.scalar_tensor_tensor(
                    dc_high[:, first : first + HALF], a_pairs[1][:, j, halves[h]], 0.0,
                    sources[j][h], ALU.max, ALU.mult,
                )
        for h in range(2):
            dh_product(dh[1, h][:, 0, :], 2, halves[h])
        pairs = tile([P, 3 * T], U32, "pairs")
        dc_pair = pairs[:, 2 * T :]
        pair_product(dc_pair, 0, relu_low[:])

        def gather_dc(words, e, windows):
            cut = entries(list_c, e * C, C)
            for j in range(2):
                nc.scalar.activation(words[:, :, 2 + j], windows[j].indirect(cut), ACT.Copy)
            nc.vector.tensor_copy(word_half(words, 0), dc_pair.indirect(cut))

        q_tok = [tile([P, T], F32, f"q_tok{kb}") for kb in range(KB - 1)]

        def q_bank(name, tag, operands, engine_copy=nc.scalar.copy):
            width = sum(act[1].shape[1] for block, act in operands)
            bank = ps.tile([P, width], F32, name=name, tag=tag)
            first = 0
            for block, act in operands:
                count = act[1].shape[1]
                product(bank[:, first : first + count], block, act)
                first += count
            slots = tile([P, width], F32, name + "_slots")
            engine_copy(slots[:], bank[:])
            return slots

        def scatter_on_scalar(window, offsets, first, values):
            nc.scalar.activation(window[:].indirect(entries(offsets, first, values.shape[1])), values, ACT.Copy)

        def scatter_on_vector(window, offsets, first, values):
            nc.vector.tensor_copy(window[:].indirect(entries(offsets, first, values.shape[1])), values)

        gather_dc(as_words(lower0_words[:, HALF * PACK :]), 0, [dc_high[:, j * T : (j + 1) * T] for j in range(2)])
        round_on_gpsimd(lower0_words[:, 0 : HALF * PACK], wb_raw[0, 0][:])
        lower1_words = tile([P, (C + HALF) * PACK], BF16, "lower1_words")
        gather_dc(as_words(lower1_words[:, 0 : C * PACK]), 1, [dc_high[:, j * T : (j + 1) * T] for j in range(2)])
        round_on_gpsimd(lower1_words[:, C * PACK : (C + P) * PACK], wb_raw[1, 0][:, :, 0:P])
        round_wb(nc.scalar.copy, lower1_words[:, (C + P) * PACK :], wb_raw[1, 0][:, :, P:HALF])
        lower0 = quantise(lower0_words, "lower0")
        dc_q = [columns(lower0, HALF, C)]
        slots0 = [q_bank(f"q0{kb}", f"high{3 * kb}", [(columns(lower0, kb * P, P), dc_q[0])]) for kb in range(2)]
        for kb in range(2):
            scatter_on_scalar(q_tok[kb], list_c, 0, slots0[kb][:])

        gated = [tile([P, 2, T], F32, f"gated{u}") for u in range(2)]
        nc.vector.scalar_tensor_tensor(gated[0][:], a_pairs[0][:], 0.0, c_pairs[0], ALU.is_gt, ALU.mult)
        lower1 = quantise(lower1_words[:], "lower1", "c_low")
        dc_q.append(columns(lower1, 0, C))
        slots10 = q_bank(
            "q10", "high1", [(columns(lower1, C + u * P, P), dc_q[1]) for u in range(2)], nc.vector.tensor_copy
        )
        for kb in range(2):
            scatter_on_scalar(q_tok[kb], list_c, C, slots10[:, kb * C : (kb + 1) * C])

        upper_words = c_high_zone[:, 0 : 3 * P * PACK]
        nc.vector.scalar_tensor_tensor(gated[1][:], a_pairs[1][:], 0.0, c_pairs[1], ALU.is_gt, ALU.mult)
        round_on_gpsimd(upper_words[:, 0 : HALF * PACK], wb_raw[0, 1][:])
        round_on_gpsimd(upper_words[:, HALF * PACK :], wb_raw[1, 1][:, :, 0:P])
        pair_product(pairs[:, T : 2 * T], 0, gated[0][:])
        pair_product(pairs[:, 0:T], 1, gated[1][:])
        upper = quantise(upper_words, "upper")
        slots2 = [q_bank(f"q{e}2", f"high{2 + e}", [(columns(upper, e * C, P), dc_q[e])]) for e in range(E)]
        for e in range(E):
            scatter_on_scalar(q_tok[2], list_c, e * C, slots2[e][:])

        picked = tile([P, 2 * T], U32, "picked")

        def gather_da(u):
            first = (1 - u) * T
            nc.vector.tensor_copy(picked[:, u * T : (u + 1) * T], pairs[:, first : first + WIDE].indirect(list_a[:]))

        gather_da(0)
        slots03 = q_bank("q03", "high0", [(columns(upper, P, P), columns(lower0, HALF, P))], nc.vector.tensor_copy)
        gather_da(1)
        last_words = pairs[:, T + HALF : 2 * T].bitcast(BF16)
        round_wb(nc.vector.tensor_copy, last_words, wb_raw[1, 1][:, :, P:HALF])
        da_words = tile([P, 2 * T], U32, "da_words")
        nc.vector.tensor_copy(
            da_words[:].bitcast(I32).rearrange("p (g i u) -> p g u i", i=4, u=2),
            picked[:].bitcast(I32).rearrange("p (u g i) -> p g u i", i=4, u=2),
        )
        wb13 = quantise(last_words, "wb13")
        da_q = quantise(da_words[:].bitcast(BF16), "da_q")
        q_tok.append(tile([P, T], F32, "q_tok3", "picked"))
        scatter_on_vector(q_tok[3], list_c, 0, slots03[:])

        r_tok = [tile([P, WIDE if kb in (0, 3) else T], F32, f"r_tok{kb}") for kb in range(KB)]

        def r_operands(e, kb):
            return wa_block(e, kb), columns(da_q, e * C, C)

        def r_bank(name, tag, operands):
            return q_bank(name, tag, operands, nc.vector.tensor_copy)

        middle = [r_bank("r_middle0", "low1", [r_operands(0, kb) for kb in (1, 2)])]
        r_slots0 = r_bank("r0", "low0", [r_operands(e, 0) for e in range(E)])
        middle.append(r_bank("r_middle1", "low2", [r_operands(1, kb) for kb in (1, 2)]))
        scatter_on_vector(r_tok[0], list_a, 0, r_slots0[:])
        rest3 = [(columns(upper, P, P), columns(lower0, HALF + P, P)), (columns(wb13, 0, P), dc_q[1])]
        slots3 = r_bank("q3", "low1", rest3)
        r_slots3 = r_bank("r3", "low3", [r_operands(e, 3) for e in range(E)])
        scatter_on_vector(q_tok[3], list_c, P, slots3[:, 0:SHARE])
        scatter_on_vector(r_tok[3], list_a, 0, r_slots3[:])
        for e in range(E):
            for u in range(2):
                scatter_on_scalar(r_tok[1 + u], list_a, e * C, middle[e][:, u * C : (u + 1) * C])
        scatter_on_scalar(q_tok[3], list_c, P + SHARE, slots3[:, SHARE:])

        before = None
        for kb in range(KB - 1):
            total = tile([P, T], F32, f"total{kb}", before)
            nc.gpsimd.tensor_tensor(total[:], r_tok[kb][:, 0:T], q_tok[kb][:], ALU.add)
            nc.sync.dma_start(out=out[kb * P : (kb + 1) * P, :], in_=total[:])
            before = f"r_tok{kb}"

        for h in range(2):
            cols = slice(h * HALF, (h + 1) * HALF)
            last = tile([P, HALF], F32, f"last{h}")
            nc.vector.tensor_tensor(last[:], r_tok[3][:, cols], q_tok[3][:, cols], ALU.add)
            nc.scalar.dma_start(out=out[3 * P : 4 * P, cols], in_=last[:])
